import numpy as np
import ml_dtypes


def mxq(x, axis, fmt="e4m3"):
    dtype, down = {"e4m3": (ml_dtypes.float8_e4m3fn, 7), "e5m2": (ml_dtypes.float8_e5m2, 14)}[fmt]
    v = np.moveaxis(np.asarray(x, np.float32).astype(ml_dtypes.bfloat16).astype(np.float64), axis, -1)
    blocks = v.reshape(v.shape[:-1] + (-1, 32))
    amax = np.abs(blocks).max(-1, keepdims=True)
    byte = np.maximum(np.where(amax > 0, np.frexp(amax)[1] - 1 + 127, 0) - down, 1)
    scale = np.exp2(byte - 127.0)
    codes = (blocks / scale).astype(np.float32).astype(dtype).astype(np.float64)
    return np.moveaxis((codes * scale).reshape(v.shape), -1, axis)


WIDE = False


def mx_kscale(k):
    if not WIDE:
        return np.ones(k)
    levels = np.array([10, -10, 5, -5, 0])
    if k % 512:
        return np.exp2(np.random.permutation(np.resize(levels, k // 32))).repeat(32)
    a = np.empty((k // 512, 16))
    for p in range(k // 512):
        a[p, :8] = np.random.permutation(np.resize(levels, 8))
        for g in range(8):
            far = levels[np.abs(levels - a[p, g]) >= 10]
            a[p, g + 8] = far[np.random.randint(len(far))]
    return np.exp2(a.ravel()).repeat(32)


def f64(x):
    return np.asarray(x).astype(np.float64)


def striped8(idx):
    return np.asarray(idx).reshape(8, -1, 16).transpose(0, 2, 1).reshape(128, -1).astype(np.uint16)


def unstriped8(offs):
    return offs.reshape(8, 16, -1).transpose(0, 2, 1).reshape(8, -1).astype(np.int64)


def pick8(x, idx, run):
    r = np.arange(len(x))
    return x[r[:, None], idx[r % (8 * run) // run]]


E2M1 = np.array([0.0, 0.5, 1.0, 1.5, 2.0, 3.0, 4.0, 6.0, -0.0, -0.5, -1.0, -1.5, -2.0, -3.0, -4.0, -6.0])


def pack_weight(w, fmt):
    k, n = w.shape
    w = f64(np.asarray(w, np.float32).astype(ml_dtypes.bfloat16)).reshape(k // 32, 32, n)
    amax = np.abs(w).max(1)
    if fmt == "e4m3":
        byte = np.frexp(amax)[1] - 1 + 127 - 7
    else:
        mant, ex = np.frexp(amax / 6.0)
        byte = np.where(mant > 0.5, ex, ex - 1) + 127
    byte = np.clip(np.where(amax > 0, byte, 1), 1, 254)
    scaled = (w * np.exp2(127.0 - byte)[:, None, :]).reshape(k, n).astype(np.float32)
    by_word = np.ascontiguousarray(scaled.reshape(k // 512, 128, 4, n).transpose(0, 1, 3, 2))
    if fmt == "e4m3":
        words = by_word.astype(ml_dtypes.float8_e4m3fn).view(np.uint8)
    else:
        c = by_word.astype(ml_dtypes.float4_e2m1fn).view(np.uint8) & 0xF
        words = (c[..., 0::2] | (c[..., 1::2] << 4)).reshape(k // 512, 128, 2 * n)
    return np.ascontiguousarray(words), np.ascontiguousarray(byte.astype(np.uint8).reshape(k // 512, 16, n))


def unpack_weight(words, scales, fmt):
    g, _, n = scales.shape
    words = np.ascontiguousarray(words).reshape(g, 128, n, -1)
    if fmt == "e4m3":
        vals = words.view(ml_dtypes.float8_e4m3fn).astype(np.float64)
    else:
        nib = np.empty((g, 128, n, 4), np.uint8)
        nib[..., 0::2] = words & 0xF
        nib[..., 1::2] = words >> 4
        vals = E2M1[nib]
    vals = vals * np.repeat(np.exp2(scales.astype(np.float64) - 127.0), 8, axis=1)[..., None]
    return vals.transpose(0, 1, 3, 2).reshape(g * 512, n)


D, T, Q, I, E = 512, 1024, 128, 512, 512


def setup_inputs():
    n = np.random.standard_normal
    idx = np.stack([np.random.permutation(T)[:I] for _ in range(8)])
    fd = mx_kscale(D)
    ft = mx_kscale(T)
    keysp = pack_weight(n((D, T)) / fd[:, None], "e4m3")
    return {
        "query": (n((D, Q)) * 0.25 / np.sqrt(D) * fd[:, None]).astype(np.float32),
        "keys_words": keysp[0],
        "keys_scales": keysp[1],
        "pos": np.tile(np.random.uniform(0.0, 1.0, T), (128, 1)).astype(np.float32),
        "qpos": (np.random.uniform(0.2, 1.2, (Q, 1))).astype(np.float32),
        "slope": (np.random.uniform(0.2, 0.8, (Q, 1))).astype(np.float32),
        "fac": (np.random.uniform(4.0, 16.0, (1, T)) * ft).astype(np.float32),
        "vals": (n((T, E)) / ft[:, None]).astype(np.float32),
        "offs": striped8(idx),
    }


def reference(query, keys_words, keys_scales, pos, qpos, slope, fac, vals, offs):
    idx = unstriped8(offs)
    keysu = unpack_weight(keys_words, keys_scales, "e4m3")
    queryq = mxq(f64(query), 0, "e4m3")
    a = queryq.T @ keysu
    s = pick8(a, idx, 16) - f64(slope) * np.square(f64(qpos) - pick8(f64(pos), idx, 16))
    p = np.exp(s - np.max(s, axis=1, keepdims=True))
    w = p / np.sum(p, axis=1, keepdims=True)
    wf = np.zeros((Q, T))
    wf[np.arange(Q)[:, None], idx[np.arange(Q) % 128 // 16]] = w
    wg = wf * f64(fac)
    wt = wg.T
    wtq = mxq(wt, 0, "e4m3")
    valsq = mxq(f64(vals), 0, "e4m3")
    o = wtq.T @ valsq
    return o

@@ -1,0 +1,221 @@
+from contextlib import ExitStack
+
+import concourse.mybir as mybir
+from concourse.masks import make_identity
+
+D, T, Q, I, E = 512, 1024, 128, 512, 512
+FLOPS = 2 * Q * D * T + 2 * Q * T * E
+
+F32 = mybir.dt.float32
+BF16 = mybir.dt.bfloat16
+I32 = mybir.dt.int32
+U32 = mybir.dt.uint32
+U16 = mybir.dt.uint16
+U8 = mybir.dt.uint8
+FP8X4 = mybir.dt.float8_e4m3fn_x4
+ALU = mybir.AluOpType
+ACT = mybir.ActivationFunctionType
+
+P = 128
+PACK = 4
+K_PASS = P * PACK
+PASSES = T // K_PASS
+HALF = E // 2
+KEY_RUN = T // 4
+SPLIT = HALF // 2
+SLOT_PIECES = (128, 384)
+
+
+def tile_attend_ownlists_positions_kernel(tc, query, keys_words, keys_scales, pos, qpos, slope, fac, vals, offs, out):
+    nc = tc.nc
+    with ExitStack() as ctx:
+        sb = ctx.enter_context(tc.tile_pool(name="sb", bufs=1))
+        ps = ctx.enter_context(tc.psum_pool(name="ps", bufs=1))
+
+        offsets = sb.tile([P, I // 16], U16, name="offsets")
+        pos_all = sb.tile([P, T], F32, name="pos_all")
+        q_raw = sb.tile([P, PACK, Q], F32, name="q_raw")
+        k_codes = sb.tile([P, T], U32, name="k_codes", tag="early", align_bytes=64)
+        k_scales = sb.tile([P, KEY_RUN], U8, name="k_scales", align_bytes=64)
+        qpos_col = sb.tile([P, 1], F32, name="qpos_col")
+        slope_col = sb.tile([P, 1], F32, name="slope_col")
+        fac_rows = sb.tile([P, PASSES, PACK], F32, name="fac_rows")
+        placed = sb.tile([P, T], F32, name="placed")
+        ident = sb.tile([P, P], F32, name="ident")
+        warm_in = sb.tile([P, 1], F32, name="warm_in")
+        warm_out = sb.tile([P, 1], F32, name="warm_out")
+
+        nc.vector.memset(k_scales[:].bitcast(I32), 0)
+        nc.vector.memset(warm_in[:], 0.0)
+        nc.scalar.activation(warm_out[:], warm_in[:], ACT.Exp)
+        nc.vector.memset(placed[:], 0.0)
+
+        pos_rows = sb.tile([P, T // P], F32, name="pos_rows")
+        nc.sync.dma_start(pos_rows[:], pos[0].rearrange("(n c) -> n c", c=T // P))
+        nc.sync.dma_start(offsets[:], offs)
+        nc.sync.dma_start(qpos_col[:], qpos)
+        nc.sync.dma_start(slope_col[:], slope)
+        nc.sync.dma_start(q_raw[:], query.rearrange("(p j) q -> p j q", j=PACK))
+        nc.sync.dma_start(k_codes[:].bitcast(I32), keys_words[0].rearrange("p n t -> p (n t)").bitcast(I32))
+        for quad in range(4):
+            nc.sync.dma_start(
+                k_scales[32 * quad : 32 * quad + 16, :].bitcast(I32),
+                keys_scales[0, 4 * quad : 4 * quad + 4, :].bitcast(I32).rearrange("r (k n) -> k r n", k=4),
+            )
+        make_identity(nc, ident[:])
+
+        v_raw = {}
+
+        def load_values(g, h, tag):
+            rows = vals[g * K_PASS : (g + 1) * K_PASS, :].rearrange("(p j) e -> p j e", j=PACK)
+            v_raw[g, h] = sb.tile([P, PACK, HALF], F32, name="v_raw%d%d" % (g, h), tag=tag)
+            nc.sync.dma_start(v_raw[g, h][:], rows[:, :, h * HALF : (h + 1) * HALF])
+
+        load_values(0, 0, "v00")
+        load_values(0, 1, "v01")
+        load_values(1, 0, "v10")
+        load_values(1, 1, "v11")
+        nc.sync.dma_start(fac_rows[:], fac[0].rearrange("(g p j) -> p g j", g=PASSES, j=PACK))
+
+        pos_by_row = pos_all[:].rearrange("p (n c) -> p n c", c=T // P)
+        for h in range(2):
+            spread = ps.tile([P, 4, P], F32, name="pos_bank%d" % h, tag="bank%d" % h)
+            for c in range(4):
+                nc.tensor.transpose(spread[:, c, :], pos_rows[:, 4 * h + c : 4 * h + c + 1].to_broadcast([P, P]), ident[:])
+            nc.scalar.copy(pos_by_row[:, :, 4 * h : 4 * h + 4], spread[:].rearrange("p c n -> p n c"))
+
+        q_bf = sb.tile([P, Q, PACK], BF16, name="q_bf", align_bytes=64)
+        nc.vector.tensor_copy(
+            q_bf[:].rearrange("p (c i) j -> p c j i", i=4), q_raw[:].rearrange("p j (c i) -> p c j i", i=4)
+        )
+        q_codes = sb.tile([P, Q], U32, name="q_codes", tag="codes0", align_bytes=64)
+        q_scales = sb.tile([P, Q], U8, name="q_scales", align_bytes=64)
+        nc.vector.quantize_mx(q_codes[:].bitcast(FP8X4), q_scales[:], q_bf[:].rearrange("p q j -> p (q j)"))
+
+        pos_listed = sb.tile([P, I], F32, name="pos_listed")
+        nc.vector.tensor_copy(pos_listed[:], pos_all[:].indirect(offsets[:]))
+
+        scores = sb.tile([P, T], F32, name="scores")
+        for h in range(2):
+            bank = ps.tile([P, 2, KEY_RUN], F32, name="score_bank%d" % h, tag="bank%d" % h)
+            for r in range(2):
+                run = 2 * h + r
+                nc.tensor.matmul_mx(
+                    bank[:, r, :], lhsT=q_codes[:].bitcast(FP8X4), lhsT_scale=q_scales[:],
+                    rhs=k_codes[:, run * KEY_RUN : (run + 1) * KEY_RUN].bitcast(FP8X4),
+                    rhs_scale=k_scales[4 * run : P, :], start=True, stop=True,
+                )
+            nc.scalar.copy(scores[:, h * K_PASS : (h + 1) * K_PASS], bank[:].rearrange("p r n -> p (r n)"))
+
+        dist2 = sb.tile([P, I], F32, name="dist2", tag="codes0", align_bytes=64)
+        nc.scalar.activation(dist2[:], pos_listed[:], ACT.Square, bias=qpos_col[:], scale=-1.0)
+
+        fac_bank = []
+        for g in range(PASSES):
+            spread = ps.tile([P, PACK, P], F32, name="fac_bank%d" % g, tag="bank%d" % g)
+            for j in range(PACK):
+                nc.tensor.transpose(spread[:, j, :], fac_rows[:, g, j : j + 1].to_broadcast([P, P]), ident[:])
+            fac_bank.append(spread)
+
+        logits = sb.tile([P, I], F32, name="logits", tag="late", align_bytes=64)
+        scores_listed = sb.tile([P, I], F32, name="scores_listed")
+        nc.vector.tensor_copy(scores_listed[:], scores[:].indirect(offsets[:]))
+        nc.vector.scalar_tensor_tensor(logits[:], dist2[:], slope_col[:], scores_listed[:], ALU.mult, ALU.subtract)
+        neg_max = sb.tile([P, 1], F32, name="neg_max")
+        nc.vector.tensor_reduce(neg_max[:], logits[:], mybir.AxisListType.X, ALU.min)
+
+        clk = sb.tile([P, 2], F32, name="clk")
+        nc.gpsimd.tensor_copy(clk[:, 1:2], neg_max[:, 0:1])
+        v_codes, v_scales = {}, {}
+
+        def cast_values(staged, g, h, first, width):
+            nc.scalar.copy(
+                staged.rearrange("p (c i) j -> p c j i", i=4),
+                v_raw[g, h][:, :, first : first + width].rearrange("p j (c i) -> p c j i", i=4),
+            )
+
+        def new_codes(g, h, tag):
+            v_codes[g, h] = sb.tile([P, HALF], U32, name="v_codes%d%d" % (g, h), tag=tag, align_bytes=64)
+            v_scales[g, h] = sb.tile([P, HALF], U8, name="v_scales%d%d" % (g, h), align_bytes=64)
+
+        def quantise_values(staged, g, h, first, width):
+            nc.vector.quantize_mx(
+                v_codes[g, h][:, first : first + width].bitcast(FP8X4),
+                v_scales[g, h][:, first : first + width],
+                staged.rearrange("p e j -> p (e j)"),
+            )
+
+        v_early = sb.tile([P, HALF + SPLIT, PACK], BF16, name="v_early", tag="early", align_bytes=64)
+        cast_values(v_early[:, 0:HALF], 0, 0, 0, HALF)
+        cast_values(v_early[:, HALF : HALF + SPLIT], 0, 1, 0, SPLIT)
+        new_codes(0, 0, "codes0")
+        quantise_values(v_early[:, 0:HALF], 0, 0, 0, HALF)
+
+        sums = sb.tile([P, len(SLOT_PIECES)], F32, name="sums")
+        first = 0
+        for n, width in enumerate(SLOT_PIECES):
+            slots = slice(first, first + width)
+            probs = sb.tile([P, width], F32, name="probs%d" % n, tag="probs%d" % n, align_bytes=64)
+            nc.scalar.activation(probs[:], logits[:, slots], ACT.Exp, bias=neg_max[:], scale=-1.0, accum_out=sums[:, n : n + 1])
+            nc.vector.tensor_copy(placed[:].indirect(offsets[:, first // 16 : (first + width) // 16]), probs[:])
+            first = first + width
+
+        total = sb.tile([P, 1], F32, name="total")
+        nc.scalar.activation(total[:], sums[:, 0:1], ACT.Identity, bias=sums[:, 1:2])
+
+        v_late = sb.tile([P, SPLIT + E, PACK], BF16, name="v_late", tag="late", align_bytes=64)
+        cast_values(v_late[:, 0:SPLIT], 0, 1, SPLIT, SPLIT)
+        cast_values(v_late[:, SPLIT : SPLIT + HALF], 1, 0, 0, HALF)
+        cast_values(v_late[:, SPLIT + HALF : SPLIT + E], 1, 1, 0, HALF)
+        nc.gpsimd.tensor_copy(clk[:, 0:1], placed[:, 0:1])
+
+        inv_total = sb.tile([P, 1], F32, name="inv_total")
+        nc.vector.reciprocal(inv_total[:], total[:])
+
+        w_codes, w_scales = [], []
+        w_grouped = []
+        for g in range(PASSES):
+            w_bf = sb.tile([P, K_PASS], BF16, name="w_bf%d" % g, align_bytes=64)
+            nc.vector.scalar_tensor_tensor(
+                w_bf[:].rearrange("q (p j) -> q p j", j=PACK),
+                placed[:, g * K_PASS : (g + 1) * K_PASS].rearrange("q (p j) -> q p j", j=PACK),
+                inv_total[:],
+                fac_bank[g][:].rearrange("q j p -> q p j"),
+                ALU.mult, ALU.mult,
+            )
+            words = w_bf[:].bitcast(F32)
+            turned = ps.tile([P, 2, Q], F32, name="turned%d" % g)
+            for u in range(2):
+                nc.tensor.transpose(turned[:, u, :], words[:, u : K_PASS // 2 : 2], ident[:])
+            grouped = sb.tile([P, Q * PACK], BF16, name="w_grouped%d" % g, align_bytes=64)
+            nc.scalar.copy(grouped[:].bitcast(F32).rearrange("p (q u) -> p q u", u=2), turned[:].rearrange("p u q -> p q u"))
+            w_grouped.append(grouped)
+
+        new_codes(0, 1, "probs0")
+        quantise_values(v_early[:, HALF : HALF + SPLIT], 0, 1, 0, SPLIT)
+        quantise_values(v_late[:, 0:SPLIT], 0, 1, SPLIT, SPLIT)
+        new_codes(1, 0, "probs1")
+        quantise_values(v_late[:, SPLIT : SPLIT + HALF], 1, 0, 0, HALF)
+        new_codes(1, 1, "codes11")
+        quantise_values(v_late[:, SPLIT + HALF : SPLIT + E], 1, 1, 0, HALF)
+
+        acc = [ps.tile([Q, HALF], F32, name="acc%d" % h) for h in range(2)]
+        for g in range(PASSES):
+            codes = sb.tile([P, Q], U32, name="w_codes%d" % g, align_bytes=64)
+            scales = sb.tile([P, Q], U8, name="w_scales%d" % g, align_bytes=64)
+            nc.vector.quantize_mx(codes[:].bitcast(FP8X4), scales[:], w_grouped[g][:])
+            for h in range(2):
+                nc.tensor.matmul_mx(
+                    acc[h][:], lhsT=codes[:].bitcast(FP8X4), lhsT_scale=scales[:],
+                    rhs=v_codes[g, h][:].bitcast(FP8X4), rhs_scale=v_scales[g, h][:],
+                    start=(g == 0), stop=(g == PASSES - 1),
+                )
+
+        for h in range(2):
+            result = sb.tile([Q, HALF], F32, name="result%d" % h)
+            if h == 0:
+                nc.scalar.copy(result[:], acc[h][:])
+                nc.scalar.dma_start(out[:, h * HALF : (h + 1) * HALF], result[:])
+            else:
+                nc.vector.tensor_copy(result[:], acc[h][:])
+                nc.sync.dma_start(out[:, h * HALF : (h + 1) * HALF], result[:])

@@ -52,9 +52,8 @@ def tile_attend_ownlists_positions_kernel(tc, query, keys_words, keys_scales, po
 
         pos_rows = sb.tile([P, T // P], F32, name="pos_rows")
         nc.sync.dma_start(pos_rows[:], pos[0].rearrange("(n c) -> n c", c=T // P))
-        nc.sync.dma_start(offsets[:], offs)
         nc.sync.dma_start(qpos_col[:], qpos)
-        nc.sync.dma_start(slope_col[:], slope)
+        nc.sync.dma_start(offsets[:], offs)
         nc.sync.dma_start(q_raw[:], query.rearrange("(p j) q -> p j q", j=PACK))
         nc.sync.dma_start(k_codes[:].bitcast(I32), keys_words[0].rearrange("p n t -> p (n t)").bitcast(I32))
         for quad in range(4):
@@ -62,7 +61,10 @@ def tile_attend_ownlists_positions_kernel(tc, query, keys_words, keys_scales, po
                 k_scales[32 * quad : 32 * quad + 16, :].bitcast(I32),
                 keys_scales[0, 4 * quad : 4 * quad + 4, :].bitcast(I32).rearrange("r (k n) -> k r n", k=4),
             )
+        nc.sync.dma_start(slope_col[:], slope)
         make_identity(nc, ident[:])
+        minus_one = sb.tile([P, 1], F32, name="minus_one")
+        nc.gpsimd.memset(minus_one[:], -1.0)
 
         v_raw = {}
 
@@ -77,23 +79,30 @@ def tile_attend_ownlists_positions_kernel(tc, query, keys_words, keys_scales, po
         load_values(1, 1, "v11")
         nc.sync.dma_start(fac_rows[:], fac[0].rearrange("(g p j) -> p g j", g=PASSES, j=PACK))
 
+        qpos_wide = sb.tile([P, I], F32, name="qpos_wide")
+        nc.scalar.copy(qpos_wide[:], qpos_col[:].to_broadcast([P, I]))
         pos_by_row = pos_all[:].rearrange("p (n c) -> p n c", c=T // P)
         for h in range(2):
-            spread = ps.tile([P, 4, P], F32, name="pos_bank%d" % h, tag="bank%d" % h)
+            spread = ps.tile([P, 4, P], F32, name="pos_bank%d" % h, tag="bank%d" % (2 * h))
             for c in range(4):
                 nc.tensor.transpose(spread[:, c, :], pos_rows[:, 4 * h + c : 4 * h + c + 1].to_broadcast([P, P]), ident[:])
-            nc.scalar.copy(pos_by_row[:, :, 4 * h : 4 * h + 4], spread[:].rearrange("p c n -> p n c"))
+            if h == 0:
+                nc.scalar.copy(pos_by_row[:, :, 0:4], spread[:].rearrange("p c n -> p n c"))
+            else:
+                nc.vector.tensor_copy(pos_by_row[:, :, 4:8], spread[:].rearrange("p c n -> p n c"))
 
         q_bf = sb.tile([P, Q, PACK], BF16, name="q_bf", align_bytes=64)
         nc.vector.tensor_copy(
             q_bf[:].rearrange("p (c i) j -> p c j i", i=4), q_raw[:].rearrange("p j (c i) -> p c j i", i=4)
         )
-        q_codes = sb.tile([P, Q], U32, name="q_codes", tag="codes0", align_bytes=64)
+        q_codes = sb.tile([P, Q], U32, name="q_codes", align_bytes=64)
         q_scales = sb.tile([P, Q], U8, name="q_scales", align_bytes=64)
         nc.vector.quantize_mx(q_codes[:].bitcast(FP8X4), q_scales[:], q_bf[:].rearrange("p q j -> p (q j)"))
 
-        pos_listed = sb.tile([P, I], F32, name="pos_listed")
-        nc.vector.tensor_copy(pos_listed[:], pos_all[:].indirect(offsets[:]))
+        dist = sb.tile([P, I], F32, name="dist")
+        nc.vector.tensor_tensor(dist[:], pos_all[:].indirect(offsets[:]), qpos_wide[:], ALU.subtract)
+        penalty = sb.tile([P, I], F32, name="penalty", tag="codes00", align_bytes=64)
+        nc.vector.scalar_tensor_tensor(penalty[:], dist[:], slope_col[:], dist[:], ALU.mult, ALU.mult)
 
         scores = sb.tile([P, T], F32, name="scores")
         for h in range(2):
@@ -107,9 +116,6 @@ def tile_attend_ownlists_positions_kernel(tc, query, keys_words, keys_scales, po
                 )
             nc.scalar.copy(scores[:, h * K_PASS : (h + 1) * K_PASS], bank[:].rearrange("p r n -> p (r n)"))
 
-        dist2 = sb.tile([P, I], F32, name="dist2", tag="codes0", align_bytes=64)
-        nc.scalar.activation(dist2[:], pos_listed[:], ACT.Square, bias=qpos_col[:], scale=-1.0)
-
         fac_bank = []
         for g in range(PASSES):
             spread = ps.tile([P, PACK, P], F32, name="fac_bank%d" % g, tag="bank%d" % g)
@@ -118,14 +124,10 @@ def tile_attend_ownlists_positions_kernel(tc, query, keys_words, keys_scales, po
             fac_bank.append(spread)
 
         logits = sb.tile([P, I], F32, name="logits", tag="late", align_bytes=64)
-        scores_listed = sb.tile([P, I], F32, name="scores_listed")
-        nc.vector.tensor_copy(scores_listed[:], scores[:].indirect(offsets[:]))
-        nc.vector.scalar_tensor_tensor(logits[:], dist2[:], slope_col[:], scores_listed[:], ALU.mult, ALU.subtract)
+        nc.vector.tensor_tensor(logits[:], scores[:].indirect(offsets[:]), penalty[:], ALU.subtract)
         neg_max = sb.tile([P, 1], F32, name="neg_max")
-        nc.vector.tensor_reduce(neg_max[:], logits[:], mybir.AxisListType.X, ALU.min)
+        nc.vector.tensor_reduce(neg_max[:], logits[:], mybir.AxisListType.X, ALU.max, negate=True)
 
-        clk = sb.tile([P, 2], F32, name="clk")
-        nc.gpsimd.tensor_copy(clk[:, 1:2], neg_max[:, 0:1])
         v_codes, v_scales = {}, {}
 
         def cast_values(staged, g, h, first, width):
@@ -148,7 +150,7 @@ def tile_attend_ownlists_positions_kernel(tc, query, keys_words, keys_scales, po
         v_early = sb.tile([P, HALF + SPLIT, PACK], BF16, name="v_early", tag="early", align_bytes=64)
         cast_values(v_early[:, 0:HALF], 0, 0, 0, HALF)
         cast_values(v_early[:, HALF : HALF + SPLIT], 0, 1, 0, SPLIT)
-        new_codes(0, 0, "codes0")
+        new_codes(0, 0, "codes00")
         quantise_values(v_early[:, 0:HALF], 0, 0, 0, HALF)
 
         sums = sb.tile([P, len(SLOT_PIECES)], F32, name="sums")
@@ -156,7 +158,7 @@ def tile_attend_ownlists_positions_kernel(tc, query, keys_words, keys_scales, po
         for n, width in enumerate(SLOT_PIECES):
             slots = slice(first, first + width)
             probs = sb.tile([P, width], F32, name="probs%d" % n, tag="probs%d" % n, align_bytes=64)
-            nc.scalar.activation(probs[:], logits[:, slots], ACT.Exp, bias=neg_max[:], scale=-1.0, accum_out=sums[:, n : n + 1])
+            nc.scalar.activation(probs[:], logits[:, slots], ACT.Exp, bias=neg_max[:], accum_out=sums[:, n : n + 1])
             nc.vector.tensor_copy(placed[:].indirect(offsets[:, first // 16 : (first + width) // 16]), probs[:])
             first = first + width
 
@@ -167,10 +169,9 @@ def tile_attend_ownlists_positions_kernel(tc, query, keys_words, keys_scales, po
         cast_values(v_late[:, 0:SPLIT], 0, 1, SPLIT, SPLIT)
         cast_values(v_late[:, SPLIT : SPLIT + HALF], 1, 0, 0, HALF)
         cast_values(v_late[:, SPLIT + HALF : SPLIT + E], 1, 1, 0, HALF)
-        nc.gpsimd.tensor_copy(clk[:, 0:1], placed[:, 0:1])
 
         inv_total = sb.tile([P, 1], F32, name="inv_total")
-        nc.vector.reciprocal(inv_total[:], total[:])
+        nc.gpsimd.tensor_tensor(inv_total[:], total[:], minus_one[:], ALU.pow)
 
         w_codes, w_scales = [], []
         w_grouped = []

@@ -23,6 +23,7 @@ PASSES = T // K_PASS
 HALF = E // 2
 KEY_RUN = T // 4
 SPLIT = HALF // 2
+SLOT_HALF = I // 2
 SLOT_PIECES = (128, 384)
 
 
@@ -79,11 +80,12 @@ def tile_attend_ownlists_positions_kernel(tc, query, keys_words, keys_scales, po
         load_values(1, 1, "v11")
         nc.sync.dma_start(fac_rows[:], fac[0].rearrange("(g p j) -> p g j", g=PASSES, j=PACK))
 
-        qpos_wide = sb.tile([P, I], F32, name="qpos_wide")
-        nc.scalar.copy(qpos_wide[:], qpos_col[:].to_broadcast([P, I]))
+        half_offsets = [offsets[:, n * SLOT_HALF // 16 : (n + 1) * SLOT_HALF // 16] for n in range(2)]
+        qpos_wide = sb.tile([P, SLOT_HALF], F32, name="qpos_wide")
+        nc.scalar.copy(qpos_wide[:], qpos_col[:].to_broadcast([P, SLOT_HALF]))
         pos_by_row = pos_all[:].rearrange("p (n c) -> p n c", c=T // P)
         for h in range(2):
-            spread = ps.tile([P, 4, P], F32, name="pos_bank%d" % h, tag="bank%d" % (2 * h))
+            spread = ps.tile([P, 4, P], F32, name="pos_bank%d" % h, tag="bank%d" % h)
             for c in range(4):
                 nc.tensor.transpose(spread[:, c, :], pos_rows[:, 4 * h + c : 4 * h + c + 1].to_broadcast([P, P]), ident[:])
             if h == 0:
@@ -99,10 +101,13 @@ def tile_attend_ownlists_positions_kernel(tc, query, keys_words, keys_scales, po
         q_scales = sb.tile([P, Q], U8, name="q_scales", align_bytes=64)
         nc.vector.quantize_mx(q_codes[:].bitcast(FP8X4), q_scales[:], q_bf[:].rearrange("p q j -> p (q j)"))
 
-        dist = sb.tile([P, I], F32, name="dist")
-        nc.vector.tensor_tensor(dist[:], pos_all[:].indirect(offsets[:]), qpos_wide[:], ALU.subtract)
-        penalty = sb.tile([P, I], F32, name="penalty", tag="codes00", align_bytes=64)
-        nc.vector.scalar_tensor_tensor(penalty[:], dist[:], slope_col[:], dist[:], ALU.mult, ALU.mult)
+        dist, penalty = [], []
+        for n in range(2):
+            dist.append(sb.tile([P, SLOT_HALF], F32, name="dist%d" % n))
+            nc.vector.tensor_tensor(dist[n][:], pos_all[:].indirect(half_offsets[n]), qpos_wide[:], ALU.subtract)
+        for n in range(2):
+            penalty.append(sb.tile([P, SLOT_HALF], F32, name="penalty%d" % n, tag="penalty%d" % n, align_bytes=64))
+            nc.vector.scalar_tensor_tensor(penalty[n][:], dist[n][:], slope_col[:], dist[n][:], ALU.mult, ALU.mult)
 
         scores = sb.tile([P, T], F32, name="scores")
         for h in range(2):
@@ -123,10 +128,19 @@ def tile_attend_ownlists_positions_kernel(tc, query, keys_words, keys_scales, po
                 nc.tensor.transpose(spread[:, j, :], fac_rows[:, g, j : j + 1].to_broadcast([P, P]), ident[:])
             fac_bank.append(spread)
 
-        logits = sb.tile([P, I], F32, name="logits", tag="late", align_bytes=64)
-        nc.vector.tensor_tensor(logits[:], scores[:].indirect(offsets[:]), penalty[:], ALU.subtract)
+        logits = []
+        for n in range(2):
+            logits.append(sb.tile([P, SLOT_HALF], F32, name="logits%d" % n))
+            nc.vector.tensor_tensor(logits[n][:], scores[:].indirect(half_offsets[n]), penalty[n][:], ALU.subtract)
+        neg_logits = sb.tile([P, I], F32, name="neg_logits", tag="late", align_bytes=64)
+        neg_max_half = sb.tile([P, 1], F32, name="neg_max_half")
         neg_max = sb.tile([P, 1], F32, name="neg_max")
-        nc.vector.tensor_reduce(neg_max[:], logits[:], mybir.AxisListType.X, ALU.max, negate=True)
+        nc.vector.tensor_scalar(
+            neg_logits[:, 0:SLOT_HALF], logits[0][:], -1.0, None, ALU.mult, ALU.min, accum_out=neg_max_half[:]
+        )
+        nc.vector.tensor_scalar(
+            neg_logits[:, SLOT_HALF:I], logits[1][:], -1.0, neg_max_half[:], ALU.mult, ALU.min, accum_out=neg_max[:]
+        )
 
         v_codes, v_scales = {}, {}
 
@@ -150,7 +164,7 @@ def tile_attend_ownlists_positions_kernel(tc, query, keys_words, keys_scales, po
         v_early = sb.tile([P, HALF + SPLIT, PACK], BF16, name="v_early", tag="early", align_bytes=64)
         cast_values(v_early[:, 0:HALF], 0, 0, 0, HALF)
         cast_values(v_early[:, HALF : HALF + SPLIT], 0, 1, 0, SPLIT)
-        new_codes(0, 0, "codes00")
+        new_codes(0, 0, "penalty1")
         quantise_values(v_early[:, 0:HALF], 0, 0, 0, HALF)
 
         sums = sb.tile([P, len(SLOT_PIECES)], F32, name="sums")
@@ -158,7 +172,7 @@ def tile_attend_ownlists_positions_kernel(tc, query, keys_words, keys_scales, po
         for n, width in enumerate(SLOT_PIECES):
             slots = slice(first, first + width)
             probs = sb.tile([P, width], F32, name="probs%d" % n, tag="probs%d" % n, align_bytes=64)
-            nc.scalar.activation(probs[:], logits[:, slots], ACT.Exp, bias=neg_max[:], accum_out=sums[:, n : n + 1])
+            nc.scalar.activation(probs[:], neg_logits[:, slots], ACT.Exp, bias=neg_max[:], scale=-1.0, accum_out=sums[:, n : n + 1])
             nc.vector.tensor_copy(placed[:].indirect(offsets[:, first // 16 : (first + width) // 16]), probs[:])
             first = first + width
 
@@ -176,26 +190,23 @@ def tile_attend_ownlists_positions_kernel(tc, query, keys_words, keys_scales, po
         w_codes, w_scales = [], []
         w_grouped = []
         for g in range(PASSES):
-            w_bf = sb.tile([P, K_PASS], BF16, name="w_bf%d" % g, align_bytes=64)
-            nc.vector.scalar_tensor_tensor(
-                w_bf[:].rearrange("q (p j) -> q p j", j=PACK),
-                placed[:, g * K_PASS : (g + 1) * K_PASS].rearrange("q (p j) -> q p j", j=PACK),
-                inv_total[:],
-                fac_bank[g][:].rearrange("q j p -> q p j"),
-                ALU.mult, ALU.mult,
-            )
-            words = w_bf[:].bitcast(F32)
             turned = ps.tile([P, 2, Q], F32, name="turned%d" % g)
+            placed_pairs = placed[:, g * K_PASS : (g + 1) * K_PASS].rearrange("q (p u e) -> q u p e", u=2, e=2)
+            fac_pairs = fac_bank[g][:].rearrange("q (u e) p -> q u p e", e=2)
             for u in range(2):
-                nc.tensor.transpose(turned[:, u, :], words[:, u : K_PASS // 2 : 2], ident[:])
+                w_bf = sb.tile([P, P, 2], BF16, name="w_bf%d%d" % (g, u))
+                nc.vector.scalar_tensor_tensor(
+                    w_bf[:], placed_pairs[:, u], inv_total[:], fac_pairs[:, u], ALU.mult, ALU.mult
+                )
+                nc.tensor.transpose(turned[:, u, :], w_bf[:].rearrange("q p e -> q (p e)").bitcast(F32), ident[:])
             grouped = sb.tile([P, Q * PACK], BF16, name="w_grouped%d" % g, align_bytes=64)
             nc.scalar.copy(grouped[:].bitcast(F32).rearrange("p (q u) -> p q u", u=2), turned[:].rearrange("p u q -> p q u"))
             w_grouped.append(grouped)
 
-        new_codes(0, 1, "probs0")
+        new_codes(0, 1, "probs1")
         quantise_values(v_early[:, HALF : HALF + SPLIT], 0, 1, 0, SPLIT)
         quantise_values(v_late[:, 0:SPLIT], 0, 1, SPLIT, SPLIT)
-        new_codes(1, 0, "probs1")
+        new_codes(1, 0, "codes10")
         quantise_values(v_late[:, SPLIT : SPLIT + HALF], 1, 0, 0, HALF)
         new_codes(1, 1, "codes11")
         quantise_values(v_late[:, SPLIT + HALF : SPLIT + E], 1, 1, 0, HALF)

@@ -24,7 +24,7 @@ HALF = E // 2
 KEY_RUN = T // 4
 SPLIT = HALF // 2
 SLOT_HALF = I // 2
-SLOT_PIECES = (128, 384)
+QUARTER = I // 4
 
 
 def tile_attend_ownlists_positions_kernel(tc, query, keys_words, keys_scales, pos, qpos, slope, fac, vals, offs, out):
@@ -43,15 +43,15 @@ def tile_attend_ownlists_positions_kernel(tc, query, keys_words, keys_scales, po
         fac_rows = sb.tile([P, PASSES, PACK], F32, name="fac_rows")
         placed = sb.tile([P, T], F32, name="placed")
         ident = sb.tile([P, P], F32, name="ident")
-        warm_in = sb.tile([P, 1], F32, name="warm_in")
-        warm_out = sb.tile([P, 1], F32, name="warm_out")
+        zero = sb.tile([P, 1], F32, name="zero")
+        minus_one = sb.tile([P, 1], F32, name="minus_one")
 
         nc.vector.memset(k_scales[:].bitcast(I32), 0)
-        nc.vector.memset(warm_in[:], 0.0)
-        nc.scalar.activation(warm_out[:], warm_in[:], ACT.Exp)
+        nc.vector.memset(zero[:], 0.0)
+        nc.scalar.activation(minus_one[:], zero[:], ACT.Identity, bias=-1.0)
         nc.vector.memset(placed[:], 0.0)
 
-        pos_rows = sb.tile([P, T // P], F32, name="pos_rows")
+        pos_rows = sb.tile([P, T // P], F32, name="pos_rows", tag="pos_rows")
         nc.sync.dma_start(pos_rows[:], pos[0].rearrange("(n c) -> n c", c=T // P))
         nc.sync.dma_start(qpos_col[:], qpos)
         nc.sync.dma_start(offsets[:], offs)
@@ -64,8 +64,6 @@ def tile_attend_ownlists_positions_kernel(tc, query, keys_words, keys_scales, po
             )
         nc.sync.dma_start(slope_col[:], slope)
         make_identity(nc, ident[:])
-        minus_one = sb.tile([P, 1], F32, name="minus_one")
-        nc.gpsimd.memset(minus_one[:], -1.0)
 
         v_raw = {}
 
@@ -81,8 +79,6 @@ def tile_attend_ownlists_positions_kernel(tc, query, keys_words, keys_scales, po
         nc.sync.dma_start(fac_rows[:], fac[0].rearrange("(g p j) -> p g j", g=PASSES, j=PACK))
 
         half_offsets = [offsets[:, n * SLOT_HALF // 16 : (n + 1) * SLOT_HALF // 16] for n in range(2)]
-        qpos_wide = sb.tile([P, SLOT_HALF], F32, name="qpos_wide")
-        nc.scalar.copy(qpos_wide[:], qpos_col[:].to_broadcast([P, SLOT_HALF]))
         pos_by_row = pos_all[:].rearrange("p (n c) -> p n c", c=T // P)
         for h in range(2):
             spread = ps.tile([P, 4, P], F32, name="pos_bank%d" % h, tag="bank%d" % h)
@@ -92,6 +88,9 @@ def tile_attend_ownlists_positions_kernel(tc, query, keys_words, keys_scales, po
                 nc.scalar.copy(pos_by_row[:, :, 0:4], spread[:].rearrange("p c n -> p n c"))
             else:
                 nc.vector.tensor_copy(pos_by_row[:, :, 4:8], spread[:].rearrange("p c n -> p n c"))
+
+        qpos_wide = sb.tile([P, SLOT_HALF], F32, name="qpos_wide", tag="pos_rows")
+        nc.scalar.copy(qpos_wide[:], qpos_col[:].to_broadcast([P, SLOT_HALF]))
 
         q_bf = sb.tile([P, Q, PACK], BF16, name="q_bf", align_bytes=64)
         nc.vector.tensor_copy(
@@ -133,7 +132,7 @@ def tile_attend_ownlists_positions_kernel(tc, query, keys_words, keys_scales, po
             logits.append(sb.tile([P, SLOT_HALF], F32, name="logits%d" % n))
             nc.vector.tensor_tensor(logits[n][:], scores[:].indirect(half_offsets[n]), penalty[n][:], ALU.subtract)
         neg_logits = sb.tile([P, I], F32, name="neg_logits", tag="late", align_bytes=64)
-        neg_max_half = sb.tile([P, 1], F32, name="neg_max_half")
+        neg_max_half = sb.tile([P, 1], F32, name="neg_max_half", tag="neg_max_half", align_bytes=64)
         neg_max = sb.tile([P, 1], F32, name="neg_max")
         nc.vector.tensor_scalar(
             neg_logits[:, 0:SLOT_HALF], logits[0][:], -1.0, None, ALU.mult, ALU.min, accum_out=neg_max_half[:]
@@ -167,27 +166,31 @@ def tile_attend_ownlists_positions_kernel(tc, query, keys_words, keys_scales, po
         new_codes(0, 0, "penalty1")
         quantise_values(v_early[:, 0:HALF], 0, 0, 0, HALF)
 
-        sums = sb.tile([P, len(SLOT_PIECES)], F32, name="sums")
-        first = 0
-        for n, width in enumerate(SLOT_PIECES):
-            slots = slice(first, first + width)
-            probs = sb.tile([P, width], F32, name="probs%d" % n, tag="probs%d" % n, align_bytes=64)
-            nc.scalar.activation(probs[:], neg_logits[:, slots], ACT.Exp, bias=neg_max[:], scale=-1.0, accum_out=sums[:, n : n + 1])
-            nc.vector.tensor_copy(placed[:].indirect(offsets[:, first // 16 : (first + width) // 16]), probs[:])
-            first = first + width
+        v_mid = sb.tile([P, SPLIT, PACK], BF16, name="v_mid", tag="neg_max_half", align_bytes=64)
+        nc.vector.tensor_copy(
+            v_mid[:].rearrange("p (c i) j -> p c j i", i=4),
+            v_raw[0, 1][:, :, SPLIT:HALF].rearrange("p j (c i) -> p c j i", i=4),
+        )
+
+        sums = sb.tile([P, 2], F32, name="sums", tag="sums", align_bytes=64)
+        probs = sb.tile([P, I], F32, name="probs")
+        for n, slots in enumerate((slice(0, QUARTER), slice(QUARTER, I))):
+            nc.scalar.activation(
+                probs[:, slots], neg_logits[:, slots], ACT.Exp, bias=neg_max[:], scale=-1.0, accum_out=sums[:, n : n + 1]
+            )
+        for first, last in ((0, QUARTER), (QUARTER, 2 * QUARTER), (2 * QUARTER, I)):
+            nc.vector.tensor_copy(placed[:].indirect(offsets[:, first // 16 : last // 16]), probs[:, first:last])
 
         total = sb.tile([P, 1], F32, name="total")
         nc.scalar.activation(total[:], sums[:, 0:1], ACT.Identity, bias=sums[:, 1:2])
 
-        v_late = sb.tile([P, SPLIT + E, PACK], BF16, name="v_late", tag="late", align_bytes=64)
-        cast_values(v_late[:, 0:SPLIT], 0, 1, SPLIT, SPLIT)
-        cast_values(v_late[:, SPLIT : SPLIT + HALF], 1, 0, 0, HALF)
-        cast_values(v_late[:, SPLIT + HALF : SPLIT + E], 1, 1, 0, HALF)
+        v_late = sb.tile([P, E, PACK], BF16, name="v_late", tag="late", align_bytes=64)
+        cast_values(v_late[:, 0:HALF], 1, 0, 0, HALF)
+        cast_values(v_late[:, HALF:E], 1, 1, 0, HALF)
 
         inv_total = sb.tile([P, 1], F32, name="inv_total")
         nc.gpsimd.tensor_tensor(inv_total[:], total[:], minus_one[:], ALU.pow)
 
-        w_codes, w_scales = [], []
         w_grouped = []
         for g in range(PASSES):
             turned = ps.tile([P, 2, Q], F32, name="turned%d" % g)
@@ -203,13 +206,13 @@ def tile_attend_ownlists_positions_kernel(tc, query, keys_words, keys_scales, po
             nc.scalar.copy(grouped[:].bitcast(F32).rearrange("p (q u) -> p q u", u=2), turned[:].rearrange("p u q -> p q u"))
             w_grouped.append(grouped)
 
-        new_codes(0, 1, "probs1")
+        new_codes(0, 1, "sums")
         quantise_values(v_early[:, HALF : HALF + SPLIT], 0, 1, 0, SPLIT)
-        quantise_values(v_late[:, 0:SPLIT], 0, 1, SPLIT, SPLIT)
+        quantise_values(v_mid[:], 0, 1, SPLIT, SPLIT)
         new_codes(1, 0, "codes10")
-        quantise_values(v_late[:, SPLIT : SPLIT + HALF], 1, 0, 0, HALF)
+        quantise_values(v_late[:, 0:HALF], 1, 0, 0, HALF)
         new_codes(1, 1, "codes11")
-        quantise_values(v_late[:, SPLIT + HALF : SPLIT + E], 1, 1, 0, HALF)
+        quantise_values(v_late[:, HALF:E], 1, 1, 0, HALF)
 
         acc = [ps.tile([Q, HALF], F32, name="acc%d" % h) for h in range(2)]
         for g in range(PASSES):

@@ -15,6 +15,7 @@ U8 = mybir.dt.uint8
 FP8X4 = mybir.dt.float8_e4m3fn_x4
 ALU = mybir.AluOpType
 ACT = mybir.ActivationFunctionType
+AXIS = mybir.AxisListType
 
 P = 128
 PACK = 4
@@ -22,7 +23,7 @@ K_PASS = P * PACK
 PASSES = T // K_PASS
 HALF = E // 2
 KEY_RUN = T // 4
-SPLIT = HALF // 2
+STRIP = HALF // 2
 SLOT_HALF = I // 2
 QUARTER = I // 4
 
@@ -45,192 +46,163 @@ def tile_attend_ownlists_positions_kernel(tc, query, keys_words, keys_scales, po
         ident = sb.tile([P, P], F32, name="ident")
         zero = sb.tile([P, 1], F32, name="zero")
         minus_one = sb.tile([P, 1], F32, name="minus_one")
+        pos_rows = sb.tile([P, T // P], F32, name="pos_rows", tag="pos_rows", align_bytes=64)
 
-        nc.vector.memset(k_scales[:].bitcast(I32), 0)
+        nc.gpsimd.memset(k_scales[:].bitcast(I32), 0)
+        make_identity(nc, ident[:])
         nc.vector.memset(zero[:], 0.0)
         nc.scalar.activation(minus_one[:], zero[:], ACT.Identity, bias=-1.0)
         nc.vector.memset(placed[:], 0.0)
 
-        pos_rows = sb.tile([P, T // P], F32, name="pos_rows", tag="pos_rows")
         nc.sync.dma_start(pos_rows[:], pos[0].rearrange("(n c) -> n c", c=T // P))
         nc.sync.dma_start(qpos_col[:], qpos)
-        nc.sync.dma_start(offsets[:], offs)
         nc.sync.dma_start(q_raw[:], query.rearrange("(p j) q -> p j q", j=PACK))
-        nc.sync.dma_start(k_codes[:].bitcast(I32), keys_words[0].rearrange("p n t -> p (n t)").bitcast(I32))
         for quad in range(4):
             nc.sync.dma_start(
                 k_scales[32 * quad : 32 * quad + 16, :].bitcast(I32),
                 keys_scales[0, 4 * quad : 4 * quad + 4, :].bitcast(I32).rearrange("r (k n) -> k r n", k=4),
             )
+        nc.sync.dma_start(k_codes[:].bitcast(I32), keys_words[0].rearrange("p n t -> p (n t)").bitcast(I32))
+        nc.sync.dma_start(offsets[:], offs)
         nc.sync.dma_start(slope_col[:], slope)
-        make_identity(nc, ident[:])
 
         v_raw = {}
-
-        def load_values(g, h, tag):
+        for g in range(PASSES):
             rows = vals[g * K_PASS : (g + 1) * K_PASS, :].rearrange("(p j) e -> p j e", j=PACK)
-            v_raw[g, h] = sb.tile([P, PACK, HALF], F32, name="v_raw%d%d" % (g, h), tag=tag)
-            nc.sync.dma_start(v_raw[g, h][:], rows[:, :, h * HALF : (h + 1) * HALF])
-
-        load_values(0, 0, "v00")
-        load_values(0, 1, "v01")
-        load_values(1, 0, "v10")
-        load_values(1, 1, "v11")
+            for h in range(2):
+                v_raw[g, h] = sb.tile([P, PACK, HALF], F32, name="v_raw%d%d" % (g, h), tag="v_raw%d%d" % (g, h))
+                nc.sync.dma_start(v_raw[g, h][:], rows[:, :, h * HALF : (h + 1) * HALF])
         nc.sync.dma_start(fac_rows[:], fac[0].rearrange("(g p j) -> p g j", g=PASSES, j=PACK))
 
-        half_offsets = [offsets[:, n * SLOT_HALF // 16 : (n + 1) * SLOT_HALF // 16] for n in range(2)]
         pos_by_row = pos_all[:].rearrange("p (n c) -> p n c", c=T // P)
         for h in range(2):
-            spread = ps.tile([P, 4, P], F32, name="pos_bank%d" % h, tag="bank%d" % h)
+            spread = ps.tile([P, 4, P], F32, name="pos_bank%d" % h, tag="side%d" % h)
             for c in range(4):
                 nc.tensor.transpose(spread[:, c, :], pos_rows[:, 4 * h + c : 4 * h + c + 1].to_broadcast([P, P]), ident[:])
-            if h == 0:
-                nc.scalar.copy(pos_by_row[:, :, 0:4], spread[:].rearrange("p c n -> p n c"))
-            else:
-                nc.vector.tensor_copy(pos_by_row[:, :, 4:8], spread[:].rearrange("p c n -> p n c"))
-
-        qpos_wide = sb.tile([P, SLOT_HALF], F32, name="qpos_wide", tag="pos_rows")
-        nc.scalar.copy(qpos_wide[:], qpos_col[:].to_broadcast([P, SLOT_HALF]))
+            nc.scalar.copy(pos_by_row[:, :, 4 * h : 4 * h + 4], spread[:].rearrange("p c n -> p n c"))
 
         q_bf = sb.tile([P, Q, PACK], BF16, name="q_bf", align_bytes=64)
         nc.vector.tensor_copy(
             q_bf[:].rearrange("p (c i) j -> p c j i", i=4), q_raw[:].rearrange("p j (c i) -> p c j i", i=4)
         )
+        qpos_wide = sb.tile([P, SLOT_HALF], F32, name="qpos_wide")
+        nc.vector.tensor_copy(qpos_wide[:], qpos_col[:].to_broadcast([P, SLOT_HALF]))
         q_codes = sb.tile([P, Q], U32, name="q_codes", align_bytes=64)
-        q_scales = sb.tile([P, Q], U8, name="q_scales", align_bytes=64)
+        q_scales = sb.tile([P, Q], U8, name="q_scales", tag="pos_rows", align_bytes=64)
         nc.vector.quantize_mx(q_codes[:].bitcast(FP8X4), q_scales[:], q_bf[:].rearrange("p q j -> p (q j)"))
 
-        dist, penalty = [], []
+        dist = sb.tile([P, I], F32, name="dist", tag="codes0", align_bytes=64)
+        penalty = sb.tile([P, I], F32, name="penalty")
+        slot_halves = [slice(n * SLOT_HALF, (n + 1) * SLOT_HALF) for n in range(2)]
         for n in range(2):
-            dist.append(sb.tile([P, SLOT_HALF], F32, name="dist%d" % n))
-            nc.vector.tensor_tensor(dist[n][:], pos_all[:].indirect(half_offsets[n]), qpos_wide[:], ALU.subtract)
-        for n in range(2):
-            penalty.append(sb.tile([P, SLOT_HALF], F32, name="penalty%d" % n, tag="penalty%d" % n, align_bytes=64))
-            nc.vector.scalar_tensor_tensor(penalty[n][:], dist[n][:], slope_col[:], dist[n][:], ALU.mult, ALU.mult)
+            half_offsets = offsets[:, n * SLOT_HALF // 16 : (n + 1) * SLOT_HALF // 16]
+            nc.vector.tensor_tensor(dist[:, slot_halves[n]], pos_all[:].indirect(half_offsets), qpos_wide[:], ALU.subtract)
+        for slots in slot_halves:
+            nc.vector.scalar_tensor_tensor(penalty[:, slots], dist[:, slots], slope_col[:], dist[:, slots], ALU.mult, ALU.mult)
 
         scores = sb.tile([P, T], F32, name="scores")
-        for h in range(2):
-            bank = ps.tile([P, 2, KEY_RUN], F32, name="score_bank%d" % h, tag="bank%d" % h)
-            for r in range(2):
-                run = 2 * h + r
-                nc.tensor.matmul_mx(
-                    bank[:, r, :], lhsT=q_codes[:].bitcast(FP8X4), lhsT_scale=q_scales[:],
-                    rhs=k_codes[:, run * KEY_RUN : (run + 1) * KEY_RUN].bitcast(FP8X4),
-                    rhs_scale=k_scales[4 * run : P, :], start=True, stop=True,
-                )
-            nc.scalar.copy(scores[:, h * K_PASS : (h + 1) * K_PASS], bank[:].rearrange("p r n -> p (r n)"))
+        for run in range(4):
+            bank = ps.tile([P, KEY_RUN], F32, name="score_bank%d" % run, tag="main%d" % run)
+            nc.tensor.matmul_mx(
+                bank[:], lhsT=q_codes[:].bitcast(FP8X4), lhsT_scale=q_scales[:],
+                rhs=k_codes[:, run * KEY_RUN : (run + 1) * KEY_RUN].bitcast(FP8X4),
+                rhs_scale=k_scales[4 * run : P, :], start=True, stop=True,
+            )
+            nc.scalar.copy(scores[:, run * KEY_RUN : (run + 1) * KEY_RUN], bank[:])
 
         fac_bank = []
         for g in range(PASSES):
-            spread = ps.tile([P, PACK, P], F32, name="fac_bank%d" % g, tag="bank%d" % g)
+            spread = ps.tile([P, PACK, P], F32, name="fac_bank%d" % g, tag="main%d" % (2 + g))
             for j in range(PACK):
                 nc.tensor.transpose(spread[:, j, :], fac_rows[:, g, j : j + 1].to_broadcast([P, P]), ident[:])
             fac_bank.append(spread)
 
-        logits = []
-        for n in range(2):
-            logits.append(sb.tile([P, SLOT_HALF], F32, name="logits%d" % n))
-            nc.vector.tensor_tensor(logits[n][:], scores[:].indirect(half_offsets[n]), penalty[n][:], ALU.subtract)
-        neg_logits = sb.tile([P, I], F32, name="neg_logits", tag="late", align_bytes=64)
-        neg_max_half = sb.tile([P, 1], F32, name="neg_max_half", tag="neg_max_half", align_bytes=64)
-        neg_max = sb.tile([P, 1], F32, name="neg_max")
-        nc.vector.tensor_scalar(
-            neg_logits[:, 0:SLOT_HALF], logits[0][:], -1.0, None, ALU.mult, ALU.min, accum_out=neg_max_half[:]
-        )
-        nc.vector.tensor_scalar(
-            neg_logits[:, SLOT_HALF:I], logits[1][:], -1.0, neg_max_half[:], ALU.mult, ALU.min, accum_out=neg_max[:]
-        )
+        logits = sb.tile([P, I], F32, name="logits", tag="late", align_bytes=64)
+        nc.vector.tensor_tensor(logits[:], scores[:].indirect(offsets[:]), penalty[:], ALU.subtract)
 
-        v_codes, v_scales = {}, {}
+        v_codes = [sb.tile([P, E], U32, name="v_codes%d" % g, tag="codes%d" % g, align_bytes=64) for g in range(PASSES)]
+        v_scales = [sb.tile([P, E], U8, name="v_scales%d" % g, align_bytes=64) for g in range(PASSES)]
 
-        def cast_values(staged, g, h, first, width):
+        def cast_values(staged, g, first, width):
+            h, start = divmod(first, HALF)
             nc.scalar.copy(
                 staged.rearrange("p (c i) j -> p c j i", i=4),
-                v_raw[g, h][:, :, first : first + width].rearrange("p j (c i) -> p c j i", i=4),
+                v_raw[g, h][:, :, start : start + width].rearrange("p j (c i) -> p c j i", i=4),
             )
 
-        def new_codes(g, h, tag):
-            v_codes[g, h] = sb.tile([P, HALF], U32, name="v_codes%d%d" % (g, h), tag=tag, align_bytes=64)
-            v_scales[g, h] = sb.tile([P, HALF], U8, name="v_scales%d%d" % (g, h), align_bytes=64)
-
-        def quantise_values(staged, g, h, first, width):
+        def quantise_values(staged, g, first, width):
             nc.vector.quantize_mx(
-                v_codes[g, h][:, first : first + width].bitcast(FP8X4),
-                v_scales[g, h][:, first : first + width],
+                v_codes[g][:, first : first + width].bitcast(FP8X4),
+                v_scales[g][:, first : first + width],
                 staged.rearrange("p e j -> p (e j)"),
             )
 
-        v_early = sb.tile([P, HALF + SPLIT, PACK], BF16, name="v_early", tag="early", align_bytes=64)
-        cast_values(v_early[:, 0:HALF], 0, 0, 0, HALF)
-        cast_values(v_early[:, HALF : HALF + SPLIT], 0, 1, 0, SPLIT)
-        new_codes(0, 0, "penalty1")
-        quantise_values(v_early[:, 0:HALF], 0, 0, 0, HALF)
+        v_early = sb.tile([P, 3 * STRIP, PACK], BF16, name="v_early", tag="early", align_bytes=64)
+        for s in range(3):
+            cast_values(v_early[:, s * STRIP : (s + 1) * STRIP], 0, s * STRIP, STRIP)
+        quantise_values(v_early[:, 0:STRIP], 0, 0, STRIP)
 
-        v_mid = sb.tile([P, SPLIT, PACK], BF16, name="v_mid", tag="neg_max_half", align_bytes=64)
-        nc.vector.tensor_copy(
-            v_mid[:].rearrange("p (c i) j -> p c j i", i=4),
-            v_raw[0, 1][:, :, SPLIT:HALF].rearrange("p j (c i) -> p c j i", i=4),
-        )
+        neg_max = v_raw[0, 0][:, 0, 0:1]
+        nc.vector.tensor_reduce(neg_max, logits[:], AXIS.X, ALU.max, negate=True)
+        quantise_values(v_early[:, STRIP : 2 * STRIP], 0, STRIP, STRIP)
 
-        sums = sb.tile([P, 2], F32, name="sums", tag="sums", align_bytes=64)
+        sums = sb.tile([P, 2], F32, name="sums")
         probs = sb.tile([P, I], F32, name="probs")
-        for n, slots in enumerate((slice(0, QUARTER), slice(QUARTER, I))):
+        pieces = ((0, QUARTER), (QUARTER, I))
+        for n, (first, last) in enumerate(pieces):
             nc.scalar.activation(
-                probs[:, slots], neg_logits[:, slots], ACT.Exp, bias=neg_max[:], scale=-1.0, accum_out=sums[:, n : n + 1]
+                probs[:, first:last], logits[:, first:last], ACT.Exp, bias=neg_max, scale=1.0, accum_out=sums[:, n : n + 1]
             )
-        for first, last in ((0, QUARTER), (QUARTER, 2 * QUARTER), (2 * QUARTER, I)):
+        for n, (first, last) in enumerate(pieces):
             nc.vector.tensor_copy(placed[:].indirect(offsets[:, first // 16 : last // 16]), probs[:, first:last])
+            if n == 0:
+                quantise_values(v_early[:, 2 * STRIP : 3 * STRIP], 0, 2 * STRIP, STRIP)
 
         total = sb.tile([P, 1], F32, name="total")
-        nc.scalar.activation(total[:], sums[:, 0:1], ACT.Identity, bias=sums[:, 1:2])
-
-        v_late = sb.tile([P, E, PACK], BF16, name="v_late", tag="late", align_bytes=64)
-        cast_values(v_late[:, 0:HALF], 1, 0, 0, HALF)
-        cast_values(v_late[:, HALF:E], 1, 1, 0, HALF)
-
+        nc.gpsimd.tensor_tensor(total[:], sums[:, 0:1], sums[:, 1:2], ALU.add)
         inv_total = sb.tile([P, 1], F32, name="inv_total")
         nc.gpsimd.tensor_tensor(inv_total[:], total[:], minus_one[:], ALU.pow)
 
+        v_late = sb.tile([P, STRIP + E, PACK], BF16, name="v_late", tag="late", align_bytes=64)
+        cast_values(v_late[:, 0:STRIP], 0, 3 * STRIP, STRIP)
+        cast_values(v_late[:, STRIP : STRIP + HALF], 1, 0, HALF)
+        cast_values(v_late[:, STRIP + HALF : STRIP + E], 1, HALF, HALF)
+        quantise_values(v_late[:, 0:STRIP], 0, 3 * STRIP, STRIP)
+
+        w_bf = sb.tile([P, PASSES, 2, P, 2], BF16, name="w_bf", tag="v_raw01")
         w_grouped = []
         for g in range(PASSES):
-            turned = ps.tile([P, 2, Q], F32, name="turned%d" % g)
+            turned = ps.tile([P, 2, Q], F32, name="turned%d" % g, tag="side%d" % g)
             placed_pairs = placed[:, g * K_PASS : (g + 1) * K_PASS].rearrange("q (p u e) -> q u p e", u=2, e=2)
             fac_pairs = fac_bank[g][:].rearrange("q (u e) p -> q u p e", e=2)
             for u in range(2):
-                w_bf = sb.tile([P, P, 2], BF16, name="w_bf%d%d" % (g, u))
                 nc.vector.scalar_tensor_tensor(
-                    w_bf[:], placed_pairs[:, u], inv_total[:], fac_pairs[:, u], ALU.mult, ALU.mult
+                    w_bf[:, g, u], placed_pairs[:, u], inv_total[:], fac_pairs[:, u], ALU.mult, ALU.mult
                 )
-                nc.tensor.transpose(turned[:, u, :], w_bf[:].rearrange("q p e -> q (p e)").bitcast(F32), ident[:])
+                nc.tensor.transpose(turned[:, u, :], w_bf[:, g, u].rearrange("q p e -> q (p e)").bitcast(F32), ident[:])
             grouped = sb.tile([P, Q * PACK], BF16, name="w_grouped%d" % g, align_bytes=64)
             nc.scalar.copy(grouped[:].bitcast(F32).rearrange("p (q u) -> p q u", u=2), turned[:].rearrange("p u q -> p q u"))
             w_grouped.append(grouped)
 
-        new_codes(0, 1, "sums")
-        quantise_values(v_early[:, HALF : HALF + SPLIT], 0, 1, 0, SPLIT)
-        quantise_values(v_mid[:], 0, 1, SPLIT, SPLIT)
-        new_codes(1, 0, "codes10")
-        quantise_values(v_late[:, 0:HALF], 1, 0, 0, HALF)
-        new_codes(1, 1, "codes11")
-        quantise_values(v_late[:, HALF:E], 1, 1, 0, HALF)
-
-        acc = [ps.tile([Q, HALF], F32, name="acc%d" % h) for h in range(2)]
+        acc = [ps.tile([Q, HALF], F32, name="acc%d" % h, tag="main%d" % h) for h in range(2)]
         for g in range(PASSES):
+            quantise_values(v_late[:, STRIP + g * HALF : STRIP + (g + 1) * HALF], 1, g * HALF, HALF)
             codes = sb.tile([P, Q], U32, name="w_codes%d" % g, align_bytes=64)
             scales = sb.tile([P, Q], U8, name="w_scales%d" % g, align_bytes=64)
             nc.vector.quantize_mx(codes[:].bitcast(FP8X4), scales[:], w_grouped[g][:])
             for h in range(2):
+                cols = slice(h * HALF, (h + 1) * HALF)
                 nc.tensor.matmul_mx(
                     acc[h][:], lhsT=codes[:].bitcast(FP8X4), lhsT_scale=scales[:],
-                    rhs=v_codes[g, h][:].bitcast(FP8X4), rhs_scale=v_scales[g, h][:],
+                    rhs=v_codes[g][:, cols].bitcast(FP8X4), rhs_scale=v_scales[g][:, cols],
                     start=(g == 0), stop=(g == PASSES - 1),
                 )
 
         for h in range(2):
             result = sb.tile([Q, HALF], F32, name="result%d" % h)
             if h == 0:
-                nc.scalar.copy(result[:], acc[h][:])
-                nc.scalar.dma_start(out[:, h * HALF : (h + 1) * HALF], result[:])
-            else:
                 nc.vector.tensor_copy(result[:], acc[h][:])
                 nc.sync.dma_start(out[:, h * HALF : (h + 1) * HALF], result[:])
+            else:
+                nc.scalar.copy(result[:], acc[h][:])
+                nc.scalar.dma_start(out[:, h * HALF : (h + 1) * HALF], result[:])

@@ -118,7 +118,9 @@ def tile_attend_ownlists_positions_kernel(tc, query, keys_words, keys_scales, po
             fac_bank.append(spread)
 
         logits = sb.tile([P, I], F32, name="logits", tag="late", align_bytes=64)
-        nc.vector.tensor_tensor(logits[:], scores[:].indirect(offsets[:]), penalty[:], ALU.subtract)
+        for n, slots in enumerate(slot_halves):
+            half_offsets = offsets[:, n * SLOT_HALF // 16 : (n + 1) * SLOT_HALF // 16]
+            nc.vector.tensor_tensor(logits[:, slots], scores[:].indirect(half_offsets), penalty[:, slots], ALU.subtract)
 
         v_codes = [sb.tile([P, E], U32, name="v_codes%d" % g, tag="codes%d" % g, align_bytes=64) for g in range(PASSES)]
         v_scales = [sb.tile([P, E], U8, name="v_scales%d" % g, align_bytes=64) for g in range(PASSES)]
@@ -146,20 +148,15 @@ def tile_attend_ownlists_positions_kernel(tc, query, keys_words, keys_scales, po
         nc.vector.tensor_reduce(neg_max, logits[:], AXIS.X, ALU.max, negate=True)
         quantise_values(v_early[:, STRIP : 2 * STRIP], 0, STRIP, STRIP)
 
-        sums = sb.tile([P, 2], F32, name="sums")
-        probs = sb.tile([P, I], F32, name="probs")
-        pieces = ((0, QUARTER), (QUARTER, I))
-        for n, (first, last) in enumerate(pieces):
-            nc.scalar.activation(
-                probs[:, first:last], logits[:, first:last], ACT.Exp, bias=neg_max, scale=1.0, accum_out=sums[:, n : n + 1]
-            )
-        for n, (first, last) in enumerate(pieces):
-            nc.vector.tensor_copy(placed[:].indirect(offsets[:, first // 16 : last // 16]), probs[:, first:last])
-            if n == 0:
-                quantise_values(v_early[:, 2 * STRIP : 3 * STRIP], 0, 2 * STRIP, STRIP)
-
         total = sb.tile([P, 1], F32, name="total")
-        nc.gpsimd.tensor_tensor(total[:], sums[:, 0:1], sums[:, 1:2], ALU.add)
+        probs_first = sb.tile([P, QUARTER], F32, name="probs_first")
+        probs = sb.tile([P, I], F32, name="probs")
+        nc.scalar.activation(probs_first[:], logits[:, 0:QUARTER], ACT.Exp, bias=neg_max, scale=1.0)
+        nc.scalar.activation(probs[:], logits[:], ACT.Exp, bias=neg_max, scale=1.0, accum_out=total[:])
+        nc.vector.tensor_copy(placed[:].indirect(offsets[:, 0 : QUARTER // 16]), probs_first[:])
+        quantise_values(v_early[:, 2 * STRIP : 3 * STRIP], 0, 2 * STRIP, STRIP)
+        nc.vector.tensor_copy(placed[:].indirect(offsets[:, QUARTER // 16 : I // 16]), probs[:, QUARTER:I])
+
         inv_total = sb.tile([P, 1], F32, name="inv_total")
         nc.gpsimd.tensor_tensor(inv_total[:], total[:], minus_one[:], ALU.pow)
 
@@ -184,25 +181,25 @@ def tile_attend_ownlists_positions_kernel(tc, query, keys_words, keys_scales, po
             nc.scalar.copy(grouped[:].bitcast(F32).rearrange("p (q u) -> p q u", u=2), turned[:].rearrange("p u q -> p q u"))
             w_grouped.append(grouped)
 
-        acc = [ps.tile([Q, HALF], F32, name="acc%d" % h, tag="main%d" % h) for h in range(2)]
+        acc = [ps.tile([Q, STRIP], F32, name="acc%d" % s, tag=("main0", "main1", "acc2", "acc3")[s]) for s in range(4)]
         for g in range(PASSES):
             quantise_values(v_late[:, STRIP + g * HALF : STRIP + (g + 1) * HALF], 1, g * HALF, HALF)
             codes = sb.tile([P, Q], U32, name="w_codes%d" % g, align_bytes=64)
             scales = sb.tile([P, Q], U8, name="w_scales%d" % g, align_bytes=64)
             nc.vector.quantize_mx(codes[:].bitcast(FP8X4), scales[:], w_grouped[g][:])
-            for h in range(2):
-                cols = slice(h * HALF, (h + 1) * HALF)
+            for s in range(4):
+                cols = slice(s * STRIP, (s + 1) * STRIP)
                 nc.tensor.matmul_mx(
-                    acc[h][:], lhsT=codes[:].bitcast(FP8X4), lhsT_scale=scales[:],
+                    acc[s][:], lhsT=codes[:].bitcast(FP8X4), lhsT_scale=scales[:],
                     rhs=v_codes[g][:, cols].bitcast(FP8X4), rhs_scale=v_scales[g][:, cols],
                     start=(g == 0), stop=(g == PASSES - 1),
                 )
 
-        for h in range(2):
-            result = sb.tile([Q, HALF], F32, name="result%d" % h)
-            if h == 0:
-                nc.vector.tensor_copy(result[:], acc[h][:])
-                nc.sync.dma_start(out[:, h * HALF : (h + 1) * HALF], result[:])
+        for s in range(4):
+            result = sb.tile([Q, STRIP], F32, name="result%d" % s)
+            if s % 2 == 0:
+                nc.vector.tensor_copy(result[:], acc[s][:])
+                nc.sync.dma_start(out[:, s * STRIP : (s + 1) * STRIP], result[:])
             else:
-                nc.scalar.copy(result[:], acc[h][:])
-                nc.scalar.dma_start(out[:, h * HALF : (h + 1) * HALF], result[:])
+                nc.scalar.copy(result[:], acc[s][:])
+                nc.scalar.dma_start(out[:, s * STRIP : (s + 1) * STRIP], result[:])

@@ -70,7 +70,7 @@ def tile_attend_ownlists_positions_kernel(tc, query, keys_words, keys_scales, po
         for g in range(PASSES):
             rows = vals[g * K_PASS : (g + 1) * K_PASS, :].rearrange("(p j) e -> p j e", j=PACK)
             for h in range(2):
-                v_raw[g, h] = sb.tile([P, PACK, HALF], F32, name="v_raw%d%d" % (g, h), tag="v_raw%d%d" % (g, h))
+                v_raw[g, h] = sb.tile([P, PACK, HALF], F32, name="v_raw%d%d" % (g, h), tag="v_raw%d%d" % (g, h), align_bytes=64)
                 nc.sync.dma_start(v_raw[g, h][:], rows[:, :, h * HALF : (h + 1) * HALF])
         nc.sync.dma_start(fac_rows[:], fac[0].rearrange("(g p j) -> p g j", g=PASSES, j=PACK))
 
@@ -122,8 +122,11 @@ def tile_attend_ownlists_positions_kernel(tc, query, keys_words, keys_scales, po
             half_offsets = offsets[:, n * SLOT_HALF // 16 : (n + 1) * SLOT_HALF // 16]
             nc.vector.tensor_tensor(logits[:, slots], scores[:].indirect(half_offsets), penalty[:, slots], ALU.subtract)
 
-        v_codes = [sb.tile([P, E], U32, name="v_codes%d" % g, tag="codes%d" % g, align_bytes=64) for g in range(PASSES)]
-        v_scales = [sb.tile([P, E], U8, name="v_scales%d" % g, align_bytes=64) for g in range(PASSES)]
+        v_codes, v_scales = {}, {}
+
+        def new_codes(g, h, tag):
+            v_codes[g, h] = sb.tile([P, HALF], U32, name="v_codes%d%d" % (g, h), tag=tag, align_bytes=64)
+            v_scales[g, h] = sb.tile([P, HALF], U8, name="v_scales%d%d" % (g, h), align_bytes=64)
 
         def cast_values(staged, g, first, width):
             h, start = divmod(first, HALF)
@@ -133,20 +136,24 @@ def tile_attend_ownlists_positions_kernel(tc, query, keys_words, keys_scales, po
             )
 
         def quantise_values(staged, g, first, width):
+            h, start = divmod(first, HALF)
             nc.vector.quantize_mx(
-                v_codes[g][:, first : first + width].bitcast(FP8X4),
-                v_scales[g][:, first : first + width],
+                v_codes[g, h][:, start : start + width].bitcast(FP8X4),
+                v_scales[g, h][:, start : start + width],
                 staged.rearrange("p e j -> p (e j)"),
             )
 
-        v_early = sb.tile([P, 3 * STRIP, PACK], BF16, name="v_early", tag="early", align_bytes=64)
-        for s in range(3):
+        v_early = sb.tile([P, E, PACK], BF16, name="v_early", tag="early", align_bytes=64)
+        for s in range(4):
             cast_values(v_early[:, s * STRIP : (s + 1) * STRIP], 0, s * STRIP, STRIP)
+        new_codes(0, 0, "codes0")
+        new_codes(0, 1, "codes01")
         quantise_values(v_early[:, 0:STRIP], 0, 0, STRIP)
 
         neg_max = v_raw[0, 0][:, 0, 0:1]
         nc.vector.tensor_reduce(neg_max, logits[:], AXIS.X, ALU.max, negate=True)
         quantise_values(v_early[:, STRIP : 2 * STRIP], 0, STRIP, STRIP)
+        quantise_values(v_early[:, 2 * STRIP : 3 * STRIP], 0, 2 * STRIP, STRIP)
 
         total = sb.tile([P, 1], F32, name="total")
         probs_first = sb.tile([P, QUARTER], F32, name="probs_first")
@@ -154,19 +161,20 @@ def tile_attend_ownlists_positions_kernel(tc, query, keys_words, keys_scales, po
         nc.scalar.activation(probs_first[:], logits[:, 0:QUARTER], ACT.Exp, bias=neg_max, scale=1.0)
         nc.scalar.activation(probs[:], logits[:], ACT.Exp, bias=neg_max, scale=1.0, accum_out=total[:])
         nc.vector.tensor_copy(placed[:].indirect(offsets[:, 0 : QUARTER // 16]), probs_first[:])
-        quantise_values(v_early[:, 2 * STRIP : 3 * STRIP], 0, 2 * STRIP, STRIP)
+        quantise_values(v_early[:, 3 * STRIP : E], 0, 3 * STRIP, STRIP)
         nc.vector.tensor_copy(placed[:].indirect(offsets[:, QUARTER // 16 : I // 16]), probs[:, QUARTER:I])
 
         inv_total = sb.tile([P, 1], F32, name="inv_total")
         nc.gpsimd.tensor_tensor(inv_total[:], total[:], minus_one[:], ALU.pow)
 
-        v_late = sb.tile([P, STRIP + E, PACK], BF16, name="v_late", tag="late", align_bytes=64)
-        cast_values(v_late[:, 0:STRIP], 0, 3 * STRIP, STRIP)
-        cast_values(v_late[:, STRIP : STRIP + HALF], 1, 0, HALF)
-        cast_values(v_late[:, STRIP + HALF : STRIP + E], 1, HALF, HALF)
-        quantise_values(v_late[:, 0:STRIP], 0, 3 * STRIP, STRIP)
+        v_late = sb.tile([P, E, PACK], BF16, name="v_late", tag="late", align_bytes=64)
+        cast_values(v_late[:, 0:STRIP], 1, 0, STRIP)
+        cast_values(v_late[:, STRIP:HALF], 1, STRIP, STRIP)
+        cast_values(v_late[:, HALF:E], 1, HALF, HALF)
+        new_codes(1, 0, "codes10")
+        quantise_values(v_late[:, 0:STRIP], 1, 0, STRIP)
 
-        w_bf = sb.tile([P, PASSES, 2, P, 2], BF16, name="w_bf", tag="v_raw01")
+        w_bf = sb.tile([P, PASSES, 2, P, 2], BF16, name="w_bf", tag="v_raw10", align_bytes=64)
         w_grouped = []
         for g in range(PASSES):
             turned = ps.tile([P, 2, Q], F32, name="turned%d" % g, tag="side%d" % g)
@@ -183,15 +191,19 @@ def tile_attend_ownlists_positions_kernel(tc, query, keys_words, keys_scales, po
 
         acc = [ps.tile([Q, STRIP], F32, name="acc%d" % s, tag=("main0", "main1", "acc2", "acc3")[s]) for s in range(4)]
         for g in range(PASSES):
-            quantise_values(v_late[:, STRIP + g * HALF : STRIP + (g + 1) * HALF], 1, g * HALF, HALF)
+            if g == 0:
+                quantise_values(v_late[:, STRIP:HALF], 1, STRIP, STRIP)
+            else:
+                new_codes(1, 1, "v_raw10")
+                quantise_values(v_late[:, HALF:E], 1, HALF, HALF)
             codes = sb.tile([P, Q], U32, name="w_codes%d" % g, align_bytes=64)
             scales = sb.tile([P, Q], U8, name="w_scales%d" % g, align_bytes=64)
             nc.vector.quantize_mx(codes[:].bitcast(FP8X4), scales[:], w_grouped[g][:])
             for s in range(4):
-                cols = slice(s * STRIP, (s + 1) * STRIP)
+                h, cols = s // 2, slice(s % 2 * STRIP, (s % 2 + 1) * STRIP)
                 nc.tensor.matmul_mx(
                     acc[s][:], lhsT=codes[:].bitcast(FP8X4), lhsT_scale=scales[:],
-                    rhs=v_codes[g][:, cols].bitcast(FP8X4), rhs_scale=v_scales[g][:, cols],
+                    rhs=v_codes[g, h][:, cols].bitcast(FP8X4), rhs_scale=v_scales[g, h][:, cols],
                     start=(g == 0), stop=(g == PASSES - 1),
                 )
 

@@ -25,7 +25,8 @@ HALF = E // 2
 KEY_RUN = T // 4
 STRIP = HALF // 2
 SLOT_HALF = I // 2
-QUARTER = I // 4
+LAST_CAST = 64
+UNLISTED = -(2.0**127)
 
 
 def tile_attend_ownlists_positions_kernel(tc, query, keys_words, keys_scales, pos, qpos, slope, fac, vals, offs, out):
@@ -42,7 +43,7 @@ def tile_attend_ownlists_positions_kernel(tc, query, keys_words, keys_scales, po
         qpos_col = sb.tile([P, 1], F32, name="qpos_col")
         slope_col = sb.tile([P, 1], F32, name="slope_col")
         fac_rows = sb.tile([P, PASSES, PACK], F32, name="fac_rows")
-        placed = sb.tile([P, T], F32, name="placed")
+        placed = sb.tile([P, T], F32, name="placed", tag="placed", align_bytes=64)
         ident = sb.tile([P, P], F32, name="ident")
         zero = sb.tile([P, 1], F32, name="zero")
         minus_one = sb.tile([P, 1], F32, name="minus_one")
@@ -52,7 +53,7 @@ def tile_attend_ownlists_positions_kernel(tc, query, keys_words, keys_scales, po
         make_identity(nc, ident[:])
         nc.vector.memset(zero[:], 0.0)
         nc.scalar.activation(minus_one[:], zero[:], ACT.Identity, bias=-1.0)
-        nc.vector.memset(placed[:], 0.0)
+        nc.vector.memset(placed[:], UNLISTED)
 
         nc.sync.dma_start(pos_rows[:], pos[0].rearrange("(n c) -> n c", c=T // P))
         nc.sync.dma_start(qpos_col[:], qpos)
@@ -87,11 +88,11 @@ def tile_attend_ownlists_positions_kernel(tc, query, keys_words, keys_scales, po
         )
         qpos_wide = sb.tile([P, SLOT_HALF], F32, name="qpos_wide")
         nc.vector.tensor_copy(qpos_wide[:], qpos_col[:].to_broadcast([P, SLOT_HALF]))
-        q_codes = sb.tile([P, Q], U32, name="q_codes", align_bytes=64)
+        q_codes = sb.tile([P, Q], U32, name="q_codes", tag="keys_free", align_bytes=64)
         q_scales = sb.tile([P, Q], U8, name="q_scales", tag="pos_rows", align_bytes=64)
         nc.vector.quantize_mx(q_codes[:].bitcast(FP8X4), q_scales[:], q_bf[:].rearrange("p q j -> p (q j)"))
 
-        dist = sb.tile([P, I], F32, name="dist", tag="codes0", align_bytes=64)
+        dist = sb.tile([P, I], F32, name="dist")
         penalty = sb.tile([P, I], F32, name="penalty")
         slot_halves = [slice(n * SLOT_HALF, (n + 1) * SLOT_HALF) for n in range(2)]
         for n in range(2):
@@ -124,9 +125,13 @@ def tile_attend_ownlists_positions_kernel(tc, query, keys_words, keys_scales, po
 
         v_codes, v_scales = {}, {}
 
-        def new_codes(g, h, tag):
-            v_codes[g, h] = sb.tile([P, HALF], U32, name="v_codes%d%d" % (g, h), tag=tag, align_bytes=64)
-            v_scales[g, h] = sb.tile([P, HALF], U8, name="v_scales%d%d" % (g, h), align_bytes=64)
+        def quantise_values(staged, g, first, width, tag):
+            codes = sb.tile([P, width], U32, name="v_codes%d_%d" % (g, first), tag=tag, align_bytes=64)
+            scales = sb.tile([P, width], U8, name="v_scales%d_%d" % (g, first), align_bytes=64)
+            nc.vector.quantize_mx(codes[:].bitcast(FP8X4), scales[:], staged.rearrange("p e j -> p (e j)"))
+            for start in range(0, width, STRIP):
+                v_codes[g, (first + start) // STRIP] = codes[:, start : start + STRIP]
+                v_scales[g, (first + start) // STRIP] = scales[:, start : start + STRIP]
 
         def cast_values(staged, g, first, width):
             h, start = divmod(first, HALF)
@@ -135,54 +140,43 @@ def tile_attend_ownlists_positions_kernel(tc, query, keys_words, keys_scales, po
                 v_raw[g, h][:, :, start : start + width].rearrange("p j (c i) -> p c j i", i=4),
             )
 
-        def quantise_values(staged, g, first, width):
-            h, start = divmod(first, HALF)
-            nc.vector.quantize_mx(
-                v_codes[g, h][:, start : start + width].bitcast(FP8X4),
-                v_scales[g, h][:, start : start + width],
-                staged.rearrange("p e j -> p (e j)"),
-            )
+        neg_max = sb.tile([P, 1], F32, name="neg_max")
+        for n, slots in enumerate(slot_halves):
+            half_offsets = offsets[:, n * SLOT_HALF // 16 : (n + 1) * SLOT_HALF // 16]
+            nc.vector.tensor_copy(placed[:].indirect(half_offsets), logits[:, slots])
+            if n == 0:
+                nc.vector.tensor_reduce(neg_max[:], logits[:], AXIS.X, ALU.max, negate=True)
 
         v_early = sb.tile([P, E, PACK], BF16, name="v_early", tag="early", align_bytes=64)
-        for s in range(4):
-            cast_values(v_early[:, s * STRIP : (s + 1) * STRIP], 0, s * STRIP, STRIP)
-        new_codes(0, 0, "codes0")
-        new_codes(0, 1, "codes01")
-        quantise_values(v_early[:, 0:STRIP], 0, 0, STRIP)
-
-        neg_max = v_raw[0, 0][:, 0, 0:1]
-        nc.vector.tensor_reduce(neg_max, logits[:], AXIS.X, ALU.max, negate=True)
-        quantise_values(v_early[:, STRIP : 2 * STRIP], 0, STRIP, STRIP)
-        quantise_values(v_early[:, 2 * STRIP : 3 * STRIP], 0, 2 * STRIP, STRIP)
+        cast_values(v_early[:, 0:HALF], 0, 0, HALF)
+        cast_values(v_early[:, HALF:E], 0, HALF, HALF)
+        v_late = sb.tile([P, E, PACK], BF16, name="v_late", tag="keys_free", align_bytes=64)
+        cast_values(v_late[:, 0:HALF], 1, 0, HALF)
+        cast_values(v_late[:, HALF : 3 * STRIP], 1, HALF, STRIP)
 
         total = sb.tile([P, 1], F32, name="total")
-        probs_first = sb.tile([P, QUARTER], F32, name="probs_first")
-        probs = sb.tile([P, I], F32, name="probs")
-        nc.scalar.activation(probs_first[:], logits[:, 0:QUARTER], ACT.Exp, bias=neg_max, scale=1.0)
-        nc.scalar.activation(probs[:], logits[:], ACT.Exp, bias=neg_max, scale=1.0, accum_out=total[:])
-        nc.vector.tensor_copy(placed[:].indirect(offsets[:, 0 : QUARTER // 16]), probs_first[:])
-        quantise_values(v_early[:, 3 * STRIP : E], 0, 3 * STRIP, STRIP)
-        nc.vector.tensor_copy(placed[:].indirect(offsets[:, QUARTER // 16 : I // 16]), probs[:, QUARTER:I])
-
+        probs_listed = sb.tile([P, I], F32, name="probs_listed", tag="v_raw01", align_bytes=64)
+        nc.scalar.activation(probs_listed[:], logits[:], ACT.Exp, bias=neg_max[:], scale=1.0, accum_out=total[:])
         inv_total = sb.tile([P, 1], F32, name="inv_total")
         nc.gpsimd.tensor_tensor(inv_total[:], total[:], minus_one[:], ALU.pow)
+        cast_values(v_late[:, 3 * STRIP : E - LAST_CAST], 1, 3 * STRIP, STRIP - LAST_CAST)
 
-        v_late = sb.tile([P, E, PACK], BF16, name="v_late", tag="late", align_bytes=64)
-        cast_values(v_late[:, 0:STRIP], 1, 0, STRIP)
-        cast_values(v_late[:, STRIP:HALF], 1, STRIP, STRIP)
-        cast_values(v_late[:, HALF:E], 1, HALF, HALF)
-        new_codes(1, 0, "codes10")
-        quantise_values(v_late[:, 0:STRIP], 1, 0, STRIP)
+        quantise_values(v_early[:], 0, 0, E, "v_raw01")
 
-        w_bf = sb.tile([P, PASSES, 2, P, 2], BF16, name="w_bf", tag="v_raw10", align_bytes=64)
+        probs = sb.tile([P, PASSES, 2, P, 2], F32, name="probs", tag="v_raw10", align_bytes=64)
+        w_bf = sb.tile([P, PASSES, 2, P, 2], BF16, name="w_bf", tag="w_bf", align_bytes=64)
+        for g in range(PASSES):
+            placed_pairs = placed[:, g * K_PASS : (g + 1) * K_PASS].rearrange("q (p u e) -> q u p e", u=2, e=2)
+            for u in range(2):
+                nc.scalar.activation(probs[:, g, u], placed_pairs[:, u], ACT.Exp, bias=neg_max[:], scale=1.0)
+        cast_values(v_late[:, E - LAST_CAST : E], 1, E - LAST_CAST, LAST_CAST)
         w_grouped = []
         for g in range(PASSES):
             turned = ps.tile([P, 2, Q], F32, name="turned%d" % g, tag="side%d" % g)
-            placed_pairs = placed[:, g * K_PASS : (g + 1) * K_PASS].rearrange("q (p u e) -> q u p e", u=2, e=2)
             fac_pairs = fac_bank[g][:].rearrange("q (u e) p -> q u p e", e=2)
             for u in range(2):
                 nc.vector.scalar_tensor_tensor(
-                    w_bf[:, g, u], placed_pairs[:, u], inv_total[:], fac_pairs[:, u], ALU.mult, ALU.mult
+                    w_bf[:, g, u], probs[:, g, u], inv_total[:], fac_pairs[:, u], ALU.mult, ALU.mult
                 )
                 nc.tensor.transpose(turned[:, u, :], w_bf[:, g, u].rearrange("q p e -> q (p e)").bitcast(F32), ident[:])
             grouped = sb.tile([P, Q * PACK], BF16, name="w_grouped%d" % g, align_bytes=64)
@@ -191,19 +185,14 @@ def tile_attend_ownlists_positions_kernel(tc, query, keys_words, keys_scales, po
 
         acc = [ps.tile([Q, STRIP], F32, name="acc%d" % s, tag=("main0", "main1", "acc2", "acc3")[s]) for s in range(4)]
         for g in range(PASSES):
-            if g == 0:
-                quantise_values(v_late[:, STRIP:HALF], 1, STRIP, STRIP)
-            else:
-                new_codes(1, 1, "v_raw10")
-                quantise_values(v_late[:, HALF:E], 1, HALF, HALF)
+            quantise_values(v_late[:, g * HALF : (g + 1) * HALF], 1, g * HALF, HALF, ("placed", "w_bf")[g])
             codes = sb.tile([P, Q], U32, name="w_codes%d" % g, align_bytes=64)
             scales = sb.tile([P, Q], U8, name="w_scales%d" % g, align_bytes=64)
             nc.vector.quantize_mx(codes[:].bitcast(FP8X4), scales[:], w_grouped[g][:])
             for s in range(4):
-                h, cols = s // 2, slice(s % 2 * STRIP, (s % 2 + 1) * STRIP)
                 nc.tensor.matmul_mx(
                     acc[s][:], lhsT=codes[:].bitcast(FP8X4), lhsT_scale=scales[:],
-                    rhs=v_codes[g, h][:, cols].bitcast(FP8X4), rhs_scale=v_scales[g, h][:, cols],
+                    rhs=v_codes[g, s].bitcast(FP8X4), rhs_scale=v_scales[g, s],
                     start=(g == 0), stop=(g == PASSES - 1),
                 )
 

@@ -25,6 +25,7 @@ HALF = E // 2
 KEY_RUN = T // 4
 STRIP = HALF // 2
 SLOT_HALF = I // 2
+VALUE_LOADS = ((0, 0, 256), (0, 256, 512), (1, 0, 384), (1, 384, 512))
 LAST_CAST = 64
 UNLISTED = -(2.0**127)
 
@@ -45,14 +46,10 @@ def tile_attend_ownlists_positions_kernel(tc, query, keys_words, keys_scales, po
         fac_rows = sb.tile([P, PASSES, PACK], F32, name="fac_rows")
         placed = sb.tile([P, T], F32, name="placed", tag="placed", align_bytes=64)
         ident = sb.tile([P, P], F32, name="ident")
-        zero = sb.tile([P, 1], F32, name="zero")
-        minus_one = sb.tile([P, 1], F32, name="minus_one")
         pos_rows = sb.tile([P, T // P], F32, name="pos_rows", tag="pos_rows", align_bytes=64)
 
         nc.gpsimd.memset(k_scales[:].bitcast(I32), 0)
         make_identity(nc, ident[:])
-        nc.vector.memset(zero[:], 0.0)
-        nc.scalar.activation(minus_one[:], zero[:], ACT.Identity, bias=-1.0)
         nc.vector.memset(placed[:], UNLISTED)
 
         nc.sync.dma_start(pos_rows[:], pos[0].rearrange("(n c) -> n c", c=T // P))
@@ -68,11 +65,11 @@ def tile_attend_ownlists_positions_kernel(tc, query, keys_words, keys_scales, po
         nc.sync.dma_start(slope_col[:], slope)
 
         v_raw = {}
-        for g in range(PASSES):
+        for g, first, last in VALUE_LOADS:
             rows = vals[g * K_PASS : (g + 1) * K_PASS, :].rearrange("(p j) e -> p j e", j=PACK)
-            for h in range(2):
-                v_raw[g, h] = sb.tile([P, PACK, HALF], F32, name="v_raw%d%d" % (g, h), tag="v_raw%d%d" % (g, h), align_bytes=64)
-                nc.sync.dma_start(v_raw[g, h][:], rows[:, :, h * HALF : (h + 1) * HALF])
+            name = "v_raw%d_%d" % (g, first)
+            v_raw[g, first] = sb.tile([P, PACK, last - first], F32, name=name, tag=name, align_bytes=64)
+            nc.sync.dma_start(v_raw[g, first][:], rows[:, :, first:last])
         nc.sync.dma_start(fac_rows[:], fac[0].rearrange("(g p j) -> p g j", g=PASSES, j=PACK))
 
         pos_by_row = pos_all[:].rearrange("p (n c) -> p n c", c=T // P)
@@ -80,7 +77,7 @@ def tile_attend_ownlists_positions_kernel(tc, query, keys_words, keys_scales, po
             spread = ps.tile([P, 4, P], F32, name="pos_bank%d" % h, tag="side%d" % h)
             for c in range(4):
                 nc.tensor.transpose(spread[:, c, :], pos_rows[:, 4 * h + c : 4 * h + c + 1].to_broadcast([P, P]), ident[:])
-            nc.scalar.copy(pos_by_row[:, :, 4 * h : 4 * h + 4], spread[:].rearrange("p c n -> p n c"))
+            nc.scalar.activation(pos_by_row[:, :, 4 * h : 4 * h + 4], spread[:].rearrange("p c n -> p n c"), ACT.Copy)
 
         q_bf = sb.tile([P, Q, PACK], BF16, name="q_bf", align_bytes=64)
         nc.vector.tensor_copy(
@@ -133,12 +130,8 @@ def tile_attend_ownlists_positions_kernel(tc, query, keys_words, keys_scales, po
                 v_codes[g, (first + start) // STRIP] = codes[:, start : start + STRIP]
                 v_scales[g, (first + start) // STRIP] = scales[:, start : start + STRIP]
 
-        def cast_values(staged, g, first, width):
-            h, start = divmod(first, HALF)
-            nc.scalar.copy(
-                staged.rearrange("p (c i) j -> p c j i", i=4),
-                v_raw[g, h][:, :, start : start + width].rearrange("p j (c i) -> p c j i", i=4),
-            )
+        def cast_values(copy, staged, raw):
+            copy(staged.rearrange("p (c i) j -> p c j i", i=4), raw.rearrange("p j (c i) -> p c j i", i=4))
 
         neg_max = sb.tile([P, 1], F32, name="neg_max")
         for n, slots in enumerate(slot_halves):
@@ -148,28 +141,27 @@ def tile_attend_ownlists_positions_kernel(tc, query, keys_words, keys_scales, po
                 nc.vector.tensor_reduce(neg_max[:], logits[:], AXIS.X, ALU.max, negate=True)
 
         v_early = sb.tile([P, E, PACK], BF16, name="v_early", tag="early", align_bytes=64)
-        cast_values(v_early[:, 0:HALF], 0, 0, HALF)
-        cast_values(v_early[:, HALF:E], 0, HALF, HALF)
+        cast_values(nc.scalar.copy, v_early[:, 0:HALF], v_raw[0, 0][:])
+        cast_values(nc.scalar.copy, v_early[:, HALF:E], v_raw[0, HALF][:])
         v_late = sb.tile([P, E, PACK], BF16, name="v_late", tag="keys_free", align_bytes=64)
-        cast_values(v_late[:, 0:HALF], 1, 0, HALF)
-        cast_values(v_late[:, HALF : 3 * STRIP], 1, HALF, STRIP)
+        cast_values(nc.scalar.copy, v_late[:, 0 : 3 * STRIP], v_raw[1, 0][:])
 
         total = sb.tile([P, 1], F32, name="total")
-        probs_listed = sb.tile([P, I], F32, name="probs_listed", tag="v_raw01", align_bytes=64)
+        probs_listed = sb.tile([P, I], F32, name="probs_listed", tag="v_raw0_256", align_bytes=64)
         nc.scalar.activation(probs_listed[:], logits[:], ACT.Exp, bias=neg_max[:], scale=1.0, accum_out=total[:])
         inv_total = sb.tile([P, 1], F32, name="inv_total")
-        nc.gpsimd.tensor_tensor(inv_total[:], total[:], minus_one[:], ALU.pow)
-        cast_values(v_late[:, 3 * STRIP : E - LAST_CAST], 1, 3 * STRIP, STRIP - LAST_CAST)
+        cast_values(nc.scalar.copy, v_late[:, 3 * STRIP : E - LAST_CAST], v_raw[1, 3 * STRIP][:, :, 0 : STRIP - LAST_CAST])
 
-        quantise_values(v_early[:], 0, 0, E, "v_raw01")
+        nc.vector.reciprocal(inv_total[:], total[:])
+        quantise_values(v_early[:], 0, 0, E, "v_raw0_256")
 
-        probs = sb.tile([P, PASSES, 2, P, 2], F32, name="probs", tag="v_raw10", align_bytes=64)
+        probs = sb.tile([P, PASSES, 2, P, 2], F32, name="probs", tag="v_raw1_0", align_bytes=64)
         w_bf = sb.tile([P, PASSES, 2, P, 2], BF16, name="w_bf", tag="w_bf", align_bytes=64)
         for g in range(PASSES):
             placed_pairs = placed[:, g * K_PASS : (g + 1) * K_PASS].rearrange("q (p u e) -> q u p e", u=2, e=2)
             for u in range(2):
                 nc.scalar.activation(probs[:, g, u], placed_pairs[:, u], ACT.Exp, bias=neg_max[:], scale=1.0)
-        cast_values(v_late[:, E - LAST_CAST : E], 1, E - LAST_CAST, LAST_CAST)
+        cast_values(nc.scalar.copy, v_late[:, E - LAST_CAST : E], v_raw[1, 3 * STRIP][:, :, STRIP - LAST_CAST : STRIP])
         w_grouped = []
         for g in range(PASSES):
             turned = ps.tile([P, 2, Q], F32, name="turned%d" % g, tag="side%d" % g)

@@ -25,8 +25,7 @@ HALF = E // 2
 KEY_RUN = T // 4
 STRIP = HALF // 2
 SLOT_HALF = I // 2
-VALUE_LOADS = ((0, 0, 256), (0, 256, 512), (1, 0, 384), (1, 384, 512))
-LAST_CAST = 64
+VALUE_LOADS = ((0, 0, 256), (0, 256, 512), (1, 0, 256), (1, 256, 512))
 UNLISTED = -(2.0**127)
 
 
@@ -143,17 +142,18 @@ def tile_attend_ownlists_positions_kernel(tc, query, keys_words, keys_scales, po
         v_early = sb.tile([P, E, PACK], BF16, name="v_early", tag="early", align_bytes=64)
         cast_values(nc.scalar.copy, v_early[:, 0:HALF], v_raw[0, 0][:])
         cast_values(nc.scalar.copy, v_early[:, HALF:E], v_raw[0, HALF][:])
-        v_late = sb.tile([P, E, PACK], BF16, name="v_late", tag="keys_free", align_bytes=64)
-        cast_values(nc.scalar.copy, v_late[:, 0 : 3 * STRIP], v_raw[1, 0][:])
+        v_late = sb.tile([P, HALF, PACK], BF16, name="v_late", tag="keys_free", align_bytes=64)
+        cast_values(nc.scalar.copy, v_late[:], v_raw[1, 0][:])
 
         total = sb.tile([P, 1], F32, name="total")
         probs_listed = sb.tile([P, I], F32, name="probs_listed", tag="v_raw0_256", align_bytes=64)
         nc.scalar.activation(probs_listed[:], logits[:], ACT.Exp, bias=neg_max[:], scale=1.0, accum_out=total[:])
         inv_total = sb.tile([P, 1], F32, name="inv_total")
-        cast_values(nc.scalar.copy, v_late[:, 3 * STRIP : E - LAST_CAST], v_raw[1, 3 * STRIP][:, :, 0 : STRIP - LAST_CAST])
 
         nc.vector.reciprocal(inv_total[:], total[:])
         quantise_values(v_early[:], 0, 0, E, "v_raw0_256")
+        v_last = sb.tile([P, HALF, PACK], BF16, name="v_last", tag="early", align_bytes=64)
+        nc.gpsimd.tensor_scalar(v_last[:], v_raw[1, HALF][:].rearrange("p j e -> p e j"), 1.0, 0.0, ALU.mult, ALU.add)
 
         probs = sb.tile([P, PASSES, 2, P, 2], F32, name="probs", tag="v_raw1_0", align_bytes=64)
         w_bf = sb.tile([P, PASSES, 2, P, 2], BF16, name="w_bf", tag="w_bf", align_bytes=64)
@@ -161,7 +161,6 @@ def tile_attend_ownlists_positions_kernel(tc, query, keys_words, keys_scales, po
             placed_pairs = placed[:, g * K_PASS : (g + 1) * K_PASS].rearrange("q (p u e) -> q u p e", u=2, e=2)
             for u in range(2):
                 nc.scalar.activation(probs[:, g, u], placed_pairs[:, u], ACT.Exp, bias=neg_max[:], scale=1.0)
-        cast_values(nc.scalar.copy, v_late[:, E - LAST_CAST : E], v_raw[1, 3 * STRIP][:, :, STRIP - LAST_CAST : STRIP])
         w_grouped = []
         for g in range(PASSES):
             turned = ps.tile([P, 2, Q], F32, name="turned%d" % g, tag="side%d" % g)
@@ -177,7 +176,7 @@ def tile_attend_ownlists_positions_kernel(tc, query, keys_words, keys_scales, po
 
         acc = [ps.tile([Q, STRIP], F32, name="acc%d" % s, tag=("main0", "main1", "acc2", "acc3")[s]) for s in range(4)]
         for g in range(PASSES):
-            quantise_values(v_late[:, g * HALF : (g + 1) * HALF], 1, g * HALF, HALF, ("placed", "w_bf")[g])
+            quantise_values((v_late, v_last)[g][:], 1, g * HALF, HALF, ("placed", "w_bf")[g])
             codes = sb.tile([P, Q], U32, name="w_codes%d" % g, align_bytes=64)
             scales = sb.tile([P, Q], U8, name="w_scales%d" % g, align_bytes=64)
             nc.vector.quantize_mx(codes[:].bitcast(FP8X4), scales[:], w_grouped[g][:])

@@ -1,7 +1,6 @@
 from contextlib import ExitStack
 
 import concourse.mybir as mybir
-from concourse.masks import make_identity
 
 D, T, Q, I, E = 512, 1024, 128, 512, 512
 FLOPS = 2 * Q * D * T + 2 * Q * T * E
@@ -26,6 +25,7 @@ KEY_RUN = T // 4
 STRIP = HALF // 2
 SLOT_HALF = I // 2
 VALUE_LOADS = ((0, 0, 256), (0, 256, 512), (1, 0, 256), (1, 256, 512))
+SCORE_RUNS = ((0, 256), (256, 512), (512, 768), (768, 896), (896, 1024))
 UNLISTED = -(2.0**127)
 
 
@@ -48,7 +48,11 @@ def tile_attend_ownlists_positions_kernel(tc, query, keys_words, keys_scales, po
         pos_rows = sb.tile([P, T // P], F32, name="pos_rows", tag="pos_rows", align_bytes=64)
 
         nc.gpsimd.memset(k_scales[:].bitcast(I32), 0)
-        make_identity(nc, ident[:])
+        zeros = sb.tile([P, P], F32, name="zeros", tag="zeros", align_bytes=64)
+        nc.gpsimd.memset(zeros[:], 0.0)
+        nc.gpsimd.affine_select(
+            out=ident[:], in_=zeros[:], compare_op=ALU.not_equal, fill=1.0, base=0, pattern=[[-1, P]], channel_multiplier=1
+        )
         nc.vector.memset(placed[:], UNLISTED)
 
         nc.sync.dma_start(pos_rows[:], pos[0].rearrange("(n c) -> n c", c=T // P))
@@ -69,7 +73,8 @@ def tile_attend_ownlists_positions_kernel(tc, query, keys_words, keys_scales, po
             name = "v_raw%d_%d" % (g, first)
             v_raw[g, first] = sb.tile([P, PACK, last - first], F32, name=name, tag=name, align_bytes=64)
             nc.sync.dma_start(v_raw[g, first][:], rows[:, :, first:last])
-        nc.sync.dma_start(fac_rows[:], fac[0].rearrange("(g p j) -> p g j", g=PASSES, j=PACK))
+            if last == E and g == 0:
+                nc.sync.dma_start(fac_rows[:], fac[0].rearrange("(g p j) -> p g j", g=PASSES, j=PACK))
 
         pos_by_row = pos_all[:].rearrange("p (n c) -> p n c", c=T // P)
         for h in range(2):
@@ -85,7 +90,7 @@ def tile_attend_ownlists_positions_kernel(tc, query, keys_words, keys_scales, po
         qpos_wide = sb.tile([P, SLOT_HALF], F32, name="qpos_wide")
         nc.vector.tensor_copy(qpos_wide[:], qpos_col[:].to_broadcast([P, SLOT_HALF]))
         q_codes = sb.tile([P, Q], U32, name="q_codes", tag="keys_free", align_bytes=64)
-        q_scales = sb.tile([P, Q], U8, name="q_scales", tag="pos_rows", align_bytes=64)
+        q_scales = sb.tile([P, Q], U8, name="q_scales", tag="zeros", align_bytes=64)
         nc.vector.quantize_mx(q_codes[:].bitcast(FP8X4), q_scales[:], q_bf[:].rearrange("p q j -> p (q j)"))
 
         dist = sb.tile([P, I], F32, name="dist")
@@ -98,14 +103,15 @@ def tile_attend_ownlists_positions_kernel(tc, query, keys_words, keys_scales, po
             nc.vector.scalar_tensor_tensor(penalty[:, slots], dist[:, slots], slope_col[:], dist[:, slots], ALU.mult, ALU.mult)
 
         scores = sb.tile([P, T], F32, name="scores")
-        for run in range(4):
-            bank = ps.tile([P, KEY_RUN], F32, name="score_bank%d" % run, tag="main%d" % run)
+        for n, (first, last) in enumerate(SCORE_RUNS):
+            bank = ps.tile([P, last - first], F32, name="score_bank%d" % n, tag=("main0", "main1", "main2", "main3", "acc2")[n])
+            plane = first // KEY_RUN
             nc.tensor.matmul_mx(
                 bank[:], lhsT=q_codes[:].bitcast(FP8X4), lhsT_scale=q_scales[:],
-                rhs=k_codes[:, run * KEY_RUN : (run + 1) * KEY_RUN].bitcast(FP8X4),
-                rhs_scale=k_scales[4 * run : P, :], start=True, stop=True,
+                rhs=k_codes[:, first:last].bitcast(FP8X4),
+                rhs_scale=k_scales[4 * plane : P, first - plane * KEY_RUN : last - plane * KEY_RUN], start=True, stop=True,
             )
-            nc.scalar.copy(scores[:, run * KEY_RUN : (run + 1) * KEY_RUN], bank[:])
+            nc.scalar.copy(scores[:, first:last], bank[:])
 
         fac_bank = []
         for g in range(PASSES):
@@ -121,13 +127,14 @@ def tile_attend_ownlists_positions_kernel(tc, query, keys_words, keys_scales, po
 
         v_codes, v_scales = {}, {}
 
-        def quantise_values(staged, g, first, width, tag):
-            codes = sb.tile([P, width], U32, name="v_codes%d_%d" % (g, first), tag=tag, align_bytes=64)
-            scales = sb.tile([P, width], U8, name="v_scales%d_%d" % (g, first), align_bytes=64)
+        def quantise_values(staged, strips, tag):
+            width = len(strips) * STRIP
+            codes = sb.tile([P, width], U32, name="v_codes%d_%d" % strips[0], tag=tag, align_bytes=64)
+            scales = sb.tile([P, width], U8, name="v_scales%d_%d" % strips[0], align_bytes=64)
             nc.vector.quantize_mx(codes[:].bitcast(FP8X4), scales[:], staged.rearrange("p e j -> p (e j)"))
-            for start in range(0, width, STRIP):
-                v_codes[g, (first + start) // STRIP] = codes[:, start : start + STRIP]
-                v_scales[g, (first + start) // STRIP] = scales[:, start : start + STRIP]
+            for n, key in enumerate(strips):
+                v_codes[key] = codes[:, n * STRIP : (n + 1) * STRIP]
+                v_scales[key] = scales[:, n * STRIP : (n + 1) * STRIP]
 
         def cast_values(copy, staged, raw):
             copy(staged.rearrange("p (c i) j -> p c j i", i=4), raw.rearrange("p j (c i) -> p c j i", i=4))
@@ -139,21 +146,25 @@ def tile_attend_ownlists_positions_kernel(tc, query, keys_words, keys_scales, po
             if n == 0:
                 nc.vector.tensor_reduce(neg_max[:], logits[:], AXIS.X, ALU.max, negate=True)
 
-        v_early = sb.tile([P, E, PACK], BF16, name="v_early", tag="early", align_bytes=64)
+        v_early = sb.tile([P, 4 * STRIP, PACK], BF16, name="v_early", tag="early", align_bytes=64)
         cast_values(nc.scalar.copy, v_early[:, 0:HALF], v_raw[0, 0][:])
-        cast_values(nc.scalar.copy, v_early[:, HALF:E], v_raw[0, HALF][:])
-        v_late = sb.tile([P, HALF, PACK], BF16, name="v_late", tag="keys_free", align_bytes=64)
-        cast_values(nc.scalar.copy, v_late[:], v_raw[1, 0][:])
+        cast_values(nc.scalar.copy, v_early[:, HALF : 3 * STRIP], v_raw[0, HALF][:, :, 0:STRIP])
+        cast_values(nc.scalar.copy, v_early[:, 3 * STRIP : 4 * STRIP], v_raw[1, 0][:, :, 0:STRIP])
+        v_late = sb.tile([P, 2 * STRIP, PACK], BF16, name="v_late", tag="keys_free", align_bytes=64)
+        cast_values(nc.scalar.copy, v_late[:, 0:STRIP], v_raw[1, 0][:, :, STRIP:HALF])
+        cast_values(nc.scalar.copy, v_late[:, STRIP:HALF], v_raw[1, HALF][:, :, 0:STRIP])
 
         total = sb.tile([P, 1], F32, name="total")
-        probs_listed = sb.tile([P, I], F32, name="probs_listed", tag="v_raw0_256", align_bytes=64)
+        probs_listed = sb.tile([P, I], F32, name="probs_listed", tag="v_raw0_0", align_bytes=64)
         nc.scalar.activation(probs_listed[:], logits[:], ACT.Exp, bias=neg_max[:], scale=1.0, accum_out=total[:])
         inv_total = sb.tile([P, 1], F32, name="inv_total")
 
         nc.vector.reciprocal(inv_total[:], total[:])
-        quantise_values(v_early[:], 0, 0, E, "v_raw0_256")
-        v_last = sb.tile([P, HALF, PACK], BF16, name="v_last", tag="early", align_bytes=64)
-        nc.gpsimd.tensor_scalar(v_last[:], v_raw[1, HALF][:].rearrange("p j e -> p e j"), 1.0, 0.0, ALU.mult, ALU.add)
+        quantise_values(v_early[:], ((0, 0), (0, 1), (0, 2), (1, 0)), "v_raw0_0")
+        v_last = sb.tile([P, PASSES, STRIP, PACK], BF16, name="v_last", tag="early", align_bytes=64)
+        for g in range(PASSES):
+            raw = v_raw[g, HALF][:, :, STRIP:HALF].rearrange("p j e -> p e j")
+            nc.gpsimd.tensor_scalar(v_last[:, g], raw, 1.0, 0.0, ALU.mult, ALU.add)
 
         probs = sb.tile([P, PASSES, 2, P, 2], F32, name="probs", tag="v_raw1_0", align_bytes=64)
         w_bf = sb.tile([P, PASSES, 2, P, 2], BF16, name="w_bf", tag="w_bf", align_bytes=64)
@@ -175,21 +186,29 @@ def tile_attend_ownlists_positions_kernel(tc, query, keys_words, keys_scales, po
             w_grouped.append(grouped)
 
         acc = [ps.tile([Q, STRIP], F32, name="acc%d" % s, tag=("main0", "main1", "acc2", "acc3")[s]) for s in range(4)]
+        w_codes, w_scales = [], []
+
+        def multiply(g, s):
+            nc.tensor.matmul_mx(
+                acc[s][:], lhsT=w_codes[g][:].bitcast(FP8X4), lhsT_scale=w_scales[g][:],
+                rhs=v_codes[g, s].bitcast(FP8X4), rhs_scale=v_scales[g, s],
+                start=(g == 0), stop=(g == PASSES - 1),
+            )
+
+        quantise_values(v_late[:], ((1, 1), (1, 2)), "placed")
         for g in range(PASSES):
-            quantise_values((v_late, v_last)[g][:], 1, g * HALF, HALF, ("placed", "w_bf")[g])
-            codes = sb.tile([P, Q], U32, name="w_codes%d" % g, align_bytes=64)
-            scales = sb.tile([P, Q], U8, name="w_scales%d" % g, align_bytes=64)
-            nc.vector.quantize_mx(codes[:].bitcast(FP8X4), scales[:], w_grouped[g][:])
-            for s in range(4):
-                nc.tensor.matmul_mx(
-                    acc[s][:], lhsT=codes[:].bitcast(FP8X4), lhsT_scale=scales[:],
-                    rhs=v_codes[g, s].bitcast(FP8X4), rhs_scale=v_scales[g, s],
-                    start=(g == 0), stop=(g == PASSES - 1),
-                )
+            w_codes.append(sb.tile([P, Q], U32, name="w_codes%d" % g, align_bytes=64))
+            w_scales.append(sb.tile([P, Q], U8, name="w_scales%d" % g, align_bytes=64))
+            nc.vector.quantize_mx(w_codes[g][:].bitcast(FP8X4), w_scales[g][:], w_grouped[g][:])
+            for s in range(3):
+                multiply(g, s)
+        quantise_values(v_last[:].rearrange("p g e j -> p (g e) j"), ((0, 3), (1, 3)), "w_grouped1")
+        for g in range(PASSES):
+            multiply(g, 3)
 
         for s in range(4):
             result = sb.tile([Q, STRIP], F32, name="result%d" % s)
-            if s % 2 == 0:
+            if s % 2 == 1:
                 nc.vector.tensor_copy(result[:], acc[s][:])
                 nc.sync.dma_start(out[:, s * STRIP : (s + 1) * STRIP], result[:])
             else:

@@ -26,6 +26,7 @@ STRIP = HALF // 2
 SLOT_HALF = I // 2
 VALUE_LOADS = ((0, 0, 256), (0, 256, 512), (1, 0, 256), (1, 256, 512))
 SCORE_RUNS = ((0, 256), (256, 512), (512, 768), (768, 896), (896, 1024))
+PLANE_PIECES = ((0, slice(0, 128)), (1, slice(0, 88)), (1, slice(88, 128)))
 UNLISTED = -(2.0**127)
 
 
@@ -33,6 +34,7 @@ def tile_attend_ownlists_positions_kernel(tc, query, keys_words, keys_scales, po
     nc = tc.nc
     with ExitStack() as ctx:
         sb = ctx.enter_context(tc.tile_pool(name="sb", bufs=1))
+        hand = ctx.enter_context(tc.tile_pool(name="hand", bufs=1))
         ps = ctx.enter_context(tc.psum_pool(name="ps", bufs=1))
 
         offsets = sb.tile([P, I // 16], U16, name="offsets")
@@ -43,12 +45,12 @@ def tile_attend_ownlists_positions_kernel(tc, query, keys_words, keys_scales, po
         qpos_col = sb.tile([P, 1], F32, name="qpos_col")
         slope_col = sb.tile([P, 1], F32, name="slope_col")
         fac_rows = sb.tile([P, PASSES, PACK], F32, name="fac_rows")
-        placed = sb.tile([P, T], F32, name="placed", tag="placed", align_bytes=64)
+        placed = hand.tile([P, T], F32, name="placed", offset=Q, align_bytes=64)
         ident = sb.tile([P, P], F32, name="ident")
         pos_rows = sb.tile([P, T // P], F32, name="pos_rows", tag="pos_rows", align_bytes=64)
 
-        nc.gpsimd.memset(k_scales[:].bitcast(I32), 0)
-        zeros = sb.tile([P, P], F32, name="zeros", tag="zeros", align_bytes=64)
+        nc.vector.memset(k_scales[:].bitcast(I32), 0)
+        zeros = hand.tile([P, P], F32, name="zeros", offset=0, align_bytes=64)
         nc.gpsimd.memset(zeros[:], 0.0)
         nc.gpsimd.affine_select(
             out=ident[:], in_=zeros[:], compare_op=ALU.not_equal, fill=1.0, base=0, pattern=[[-1, P]], channel_multiplier=1
@@ -56,7 +58,7 @@ def tile_attend_ownlists_positions_kernel(tc, query, keys_words, keys_scales, po
         nc.vector.memset(placed[:], UNLISTED)
 
         nc.sync.dma_start(pos_rows[:], pos[0].rearrange("(n c) -> n c", c=T // P))
-        nc.sync.dma_start(qpos_col[:], qpos)
+        nc.scalar.dma_start(qpos_col[:], qpos)
         nc.sync.dma_start(q_raw[:], query.rearrange("(p j) q -> p j q", j=PACK))
         for quad in range(4):
             nc.sync.dma_start(
@@ -90,7 +92,7 @@ def tile_attend_ownlists_positions_kernel(tc, query, keys_words, keys_scales, po
         qpos_wide = sb.tile([P, SLOT_HALF], F32, name="qpos_wide")
         nc.vector.tensor_copy(qpos_wide[:], qpos_col[:].to_broadcast([P, SLOT_HALF]))
         q_codes = sb.tile([P, Q], U32, name="q_codes", tag="keys_free", align_bytes=64)
-        q_scales = sb.tile([P, Q], U8, name="q_scales", tag="zeros", align_bytes=64)
+        q_scales = hand.tile([P, Q], U8, name="q_scales", offset=0, align_bytes=64)
         nc.vector.quantize_mx(q_codes[:].bitcast(FP8X4), q_scales[:], q_bf[:].rearrange("p q j -> p (q j)"))
 
         dist = sb.tile([P, I], F32, name="dist")
@@ -129,7 +131,10 @@ def tile_attend_ownlists_positions_kernel(tc, query, keys_words, keys_scales, po
 
         def quantise_values(staged, strips, tag):
             width = len(strips) * STRIP
-            codes = sb.tile([P, width], U32, name="v_codes%d_%d" % strips[0], tag=tag, align_bytes=64)
+            if tag is None:
+                codes = hand.tile([P, width], U32, name="v_codes%d_%d" % strips[0], offset=Q, align_bytes=64)
+            else:
+                codes = sb.tile([P, width], U32, name="v_codes%d_%d" % strips[0], tag=tag, align_bytes=64)
             scales = sb.tile([P, width], U8, name="v_scales%d_%d" % strips[0], align_bytes=64)
             nc.vector.quantize_mx(codes[:].bitcast(FP8X4), scales[:], staged.rearrange("p e j -> p (e j)"))
             for n, key in enumerate(strips):
@@ -170,16 +175,17 @@ def tile_attend_ownlists_positions_kernel(tc, query, keys_words, keys_scales, po
         w_bf = sb.tile([P, PASSES, 2, P, 2], BF16, name="w_bf", tag="w_bf", align_bytes=64)
         for g in range(PASSES):
             placed_pairs = placed[:, g * K_PASS : (g + 1) * K_PASS].rearrange("q (p u e) -> q u p e", u=2, e=2)
-            for u in range(2):
-                nc.scalar.activation(probs[:, g, u], placed_pairs[:, u], ACT.Exp, bias=neg_max[:], scale=1.0)
+            for u, rows in PLANE_PIECES:
+                nc.scalar.activation(probs[:, g, u, rows], placed_pairs[:, u, rows], ACT.Exp, bias=neg_max[:], scale=1.0)
         w_grouped = []
         for g in range(PASSES):
             turned = ps.tile([P, 2, Q], F32, name="turned%d" % g, tag="side%d" % g)
             fac_pairs = fac_bank[g][:].rearrange("q (u e) p -> q u p e", e=2)
-            for u in range(2):
+            for u, rows in PLANE_PIECES:
                 nc.vector.scalar_tensor_tensor(
-                    w_bf[:, g, u], probs[:, g, u], inv_total[:], fac_pairs[:, u], ALU.mult, ALU.mult
+                    w_bf[:, g, u, rows], probs[:, g, u, rows], inv_total[:], fac_pairs[:, u, rows], ALU.mult, ALU.mult
                 )
+            for u in range(2):
                 nc.tensor.transpose(turned[:, u, :], w_bf[:, g, u].rearrange("q p e -> q (p e)").bitcast(F32), ident[:])
             grouped = sb.tile([P, Q * PACK], BF16, name="w_grouped%d" % g, align_bytes=64)
             nc.scalar.copy(grouped[:].bitcast(F32).rearrange("p (q u) -> p q u", u=2), turned[:].rearrange("p u q -> p q u"))
@@ -195,7 +201,7 @@ def tile_attend_ownlists_positions_kernel(tc, query, keys_words, keys_scales, po
                 start=(g == 0), stop=(g == PASSES - 1),
             )
 
-        quantise_values(v_late[:], ((1, 1), (1, 2)), "placed")
+        quantise_values(v_late[:], ((1, 1), (1, 2)), None)
         for g in range(PASSES):
             w_codes.append(sb.tile([P, Q], U32, name="w_codes%d" % g, align_bytes=64))
             w_scales.append(sb.tile([P, Q], U8, name="w_scales%d" % g, align_bytes=64))

@@ -58,14 +58,14 @@ def tile_attend_ownlists_positions_kernel(tc, query, keys_words, keys_scales, po
         nc.vector.memset(placed[:], UNLISTED)
 
         nc.sync.dma_start(pos_rows[:], pos[0].rearrange("(n c) -> n c", c=T // P))
-        nc.scalar.dma_start(qpos_col[:], qpos)
         nc.sync.dma_start(q_raw[:], query.rearrange("(p j) q -> p j q", j=PACK))
+        nc.sync.dma_start(qpos_col[:], qpos)
+        nc.sync.dma_start(k_codes[:].bitcast(I32), keys_words[0].rearrange("p n t -> p (n t)").bitcast(I32))
         for quad in range(4):
             nc.sync.dma_start(
                 k_scales[32 * quad : 32 * quad + 16, :].bitcast(I32),
                 keys_scales[0, 4 * quad : 4 * quad + 4, :].bitcast(I32).rearrange("r (k n) -> k r n", k=4),
             )
-        nc.sync.dma_start(k_codes[:].bitcast(I32), keys_words[0].rearrange("p n t -> p (n t)").bitcast(I32))
         nc.sync.dma_start(offsets[:], offs)
         nc.sync.dma_start(slope_col[:], slope)
 
@@ -89,12 +89,12 @@ def tile_attend_ownlists_positions_kernel(tc, query, keys_words, keys_scales, po
         nc.vector.tensor_copy(
             q_bf[:].rearrange("p (c i) j -> p c j i", i=4), q_raw[:].rearrange("p j (c i) -> p c j i", i=4)
         )
-        qpos_wide = sb.tile([P, SLOT_HALF], F32, name="qpos_wide")
-        nc.vector.tensor_copy(qpos_wide[:], qpos_col[:].to_broadcast([P, SLOT_HALF]))
         q_codes = sb.tile([P, Q], U32, name="q_codes", tag="keys_free", align_bytes=64)
         q_scales = hand.tile([P, Q], U8, name="q_scales", offset=0, align_bytes=64)
         nc.vector.quantize_mx(q_codes[:].bitcast(FP8X4), q_scales[:], q_bf[:].rearrange("p q j -> p (q j)"))
 
+        qpos_wide = sb.tile([P, SLOT_HALF], F32, name="qpos_wide")
+        nc.vector.tensor_copy(qpos_wide[:], qpos_col[:].to_broadcast([P, SLOT_HALF]))
         dist = sb.tile([P, I], F32, name="dist")
         penalty = sb.tile([P, I], F32, name="penalty")
         slot_halves = [slice(n * SLOT_HALF, (n + 1) * SLOT_HALF) for n in range(2)]
@@ -167,7 +167,7 @@ def tile_attend_ownlists_positions_kernel(tc, query, keys_words, keys_scales, po
         nc.vector.reciprocal(inv_total[:], total[:])
         quantise_values(v_early[:], ((0, 0), (0, 1), (0, 2), (1, 0)), "v_raw0_0")
         v_last = sb.tile([P, PASSES, STRIP, PACK], BF16, name="v_last", tag="early", align_bytes=64)
-        for g in range(PASSES):
+        for g in reversed(range(PASSES)):
             raw = v_raw[g, HALF][:, :, STRIP:HALF].rearrange("p j e -> p e j")
             nc.gpsimd.tensor_scalar(v_last[:, g], raw, 1.0, 0.0, ALU.mult, ALU.add)
 
@@ -194,11 +194,11 @@ def tile_attend_ownlists_positions_kernel(tc, query, keys_words, keys_scales, po
         acc = [ps.tile([Q, STRIP], F32, name="acc%d" % s, tag=("main0", "main1", "acc2", "acc3")[s]) for s in range(4)]
         w_codes, w_scales = [], []
 
-        def multiply(g, s):
+        def multiply(g, s, first_pass):
             nc.tensor.matmul_mx(
                 acc[s][:], lhsT=w_codes[g][:].bitcast(FP8X4), lhsT_scale=w_scales[g][:],
                 rhs=v_codes[g, s].bitcast(FP8X4), rhs_scale=v_scales[g, s],
-                start=(g == 0), stop=(g == PASSES - 1),
+                start=(g == first_pass), stop=(g != first_pass),
             )
 
         quantise_values(v_late[:], ((1, 1), (1, 2)), None)
@@ -206,11 +206,11 @@ def tile_attend_ownlists_positions_kernel(tc, query, keys_words, keys_scales, po
             w_codes.append(sb.tile([P, Q], U32, name="w_codes%d" % g, align_bytes=64))
             w_scales.append(sb.tile([P, Q], U8, name="w_scales%d" % g, align_bytes=64))
             nc.vector.quantize_mx(w_codes[g][:].bitcast(FP8X4), w_scales[g][:], w_grouped[g][:])
+            quantise_values(v_last[:, 1 - g], ((1 - g, 3),), ("w_bf", "w_grouped1")[g])
             for s in range(3):
-                multiply(g, s)
-        quantise_values(v_last[:].rearrange("p g e j -> p (g e) j"), ((0, 3), (1, 3)), "w_grouped1")
-        for g in range(PASSES):
-            multiply(g, 3)
+                multiply(g, s, 0)
+        for g in reversed(range(PASSES)):
+            multiply(g, 3, 1)
 
         for s in range(4):
             result = sb.tile([Q, STRIP], F32, name="result%d" % s)

@@ -34,7 +34,6 @@ def tile_attend_ownlists_positions_kernel(tc, query, keys_words, keys_scales, po
     nc = tc.nc
     with ExitStack() as ctx:
         sb = ctx.enter_context(tc.tile_pool(name="sb", bufs=1))
-        hand = ctx.enter_context(tc.tile_pool(name="hand", bufs=1))
         ps = ctx.enter_context(tc.psum_pool(name="ps", bufs=1))
 
         offsets = sb.tile([P, I // 16], U16, name="offsets")
@@ -45,12 +44,12 @@ def tile_attend_ownlists_positions_kernel(tc, query, keys_words, keys_scales, po
         qpos_col = sb.tile([P, 1], F32, name="qpos_col")
         slope_col = sb.tile([P, 1], F32, name="slope_col")
         fac_rows = sb.tile([P, PASSES, PACK], F32, name="fac_rows")
-        placed = hand.tile([P, T], F32, name="placed", offset=Q, align_bytes=64)
+        placed = sb.tile([P, T], F32, name="placed", tag="placed", align_bytes=64)
         ident = sb.tile([P, P], F32, name="ident")
         pos_rows = sb.tile([P, T // P], F32, name="pos_rows", tag="pos_rows", align_bytes=64)
 
-        nc.vector.memset(k_scales[:].bitcast(I32), 0)
-        zeros = hand.tile([P, P], F32, name="zeros", offset=0, align_bytes=64)
+        nc.gpsimd.memset(k_scales[:].bitcast(I32), 0)
+        zeros = sb.tile([P, P], F32, name="zeros", tag="zeros", align_bytes=64)
         nc.gpsimd.memset(zeros[:], 0.0)
         nc.gpsimd.affine_select(
             out=ident[:], in_=zeros[:], compare_op=ALU.not_equal, fill=1.0, base=0, pattern=[[-1, P]], channel_multiplier=1
@@ -58,14 +57,14 @@ def tile_attend_ownlists_positions_kernel(tc, query, keys_words, keys_scales, po
         nc.vector.memset(placed[:], UNLISTED)
 
         nc.sync.dma_start(pos_rows[:], pos[0].rearrange("(n c) -> n c", c=T // P))
-        nc.sync.dma_start(q_raw[:], query.rearrange("(p j) q -> p j q", j=PACK))
         nc.sync.dma_start(qpos_col[:], qpos)
-        nc.sync.dma_start(k_codes[:].bitcast(I32), keys_words[0].rearrange("p n t -> p (n t)").bitcast(I32))
+        nc.sync.dma_start(q_raw[:], query.rearrange("(p j) q -> p j q", j=PACK))
         for quad in range(4):
             nc.sync.dma_start(
                 k_scales[32 * quad : 32 * quad + 16, :].bitcast(I32),
                 keys_scales[0, 4 * quad : 4 * quad + 4, :].bitcast(I32).rearrange("r (k n) -> k r n", k=4),
             )
+        nc.sync.dma_start(k_codes[:].bitcast(I32), keys_words[0].rearrange("p n t -> p (n t)").bitcast(I32))
         nc.sync.dma_start(offsets[:], offs)
         nc.sync.dma_start(slope_col[:], slope)
 
@@ -90,7 +89,7 @@ def tile_attend_ownlists_positions_kernel(tc, query, keys_words, keys_scales, po
             q_bf[:].rearrange("p (c i) j -> p c j i", i=4), q_raw[:].rearrange("p j (c i) -> p c j i", i=4)
         )
         q_codes = sb.tile([P, Q], U32, name="q_codes", tag="keys_free", align_bytes=64)
-        q_scales = hand.tile([P, Q], U8, name="q_scales", offset=0, align_bytes=64)
+        q_scales = sb.tile([P, Q], U8, name="q_scales", tag="zeros", align_bytes=64)
         nc.vector.quantize_mx(q_codes[:].bitcast(FP8X4), q_scales[:], q_bf[:].rearrange("p q j -> p (q j)"))
 
         qpos_wide = sb.tile([P, SLOT_HALF], F32, name="qpos_wide")
@@ -131,10 +130,7 @@ def tile_attend_ownlists_positions_kernel(tc, query, keys_words, keys_scales, po
 
         def quantise_values(staged, strips, tag):
             width = len(strips) * STRIP
-            if tag is None:
-                codes = hand.tile([P, width], U32, name="v_codes%d_%d" % strips[0], offset=Q, align_bytes=64)
-            else:
-                codes = sb.tile([P, width], U32, name="v_codes%d_%d" % strips[0], tag=tag, align_bytes=64)
+            codes = sb.tile([P, width], U32, name="v_codes%d_%d" % strips[0], tag=tag, align_bytes=64)
             scales = sb.tile([P, width], U8, name="v_scales%d_%d" % strips[0], align_bytes=64)
             nc.vector.quantize_mx(codes[:].bitcast(FP8X4), scales[:], staged.rearrange("p e j -> p (e j)"))
             for n, key in enumerate(strips):
@@ -201,7 +197,7 @@ def tile_attend_ownlists_positions_kernel(tc, query, keys_words, keys_scales, po
                 start=(g == first_pass), stop=(g != first_pass),
             )
 
-        quantise_values(v_late[:], ((1, 1), (1, 2)), None)
+        quantise_values(v_late[:], ((1, 1), (1, 2)), "placed")
         for g in range(PASSES):
             w_codes.append(sb.tile([P, Q], U32, name="w_codes%d" % g, align_bytes=64))
             w_scales.append(sb.tile([P, Q], U8, name="w_scales%d" % g, align_bytes=64))
@@ -219,4 +215,4 @@ def tile_attend_ownlists_positions_kernel(tc, query, keys_words, keys_scales, po
                 nc.sync.dma_start(out[:, s * STRIP : (s + 1) * STRIP], result[:])
             else:
                 nc.scalar.copy(result[:], acc[s][:])
-                nc.scalar.dma_start(out[:, s * STRIP : (s + 1) * STRIP], result[:])
+                nc.sync.dma_start(out[:, s * STRIP : (s + 1) * STRIP], result[:])

@@ -215,4 +215,4 @@ def tile_attend_ownlists_positions_kernel(tc, query, keys_words, keys_scales, po
                 nc.sync.dma_start(out[:, s * STRIP : (s + 1) * STRIP], result[:])
             else:
                 nc.scalar.copy(result[:], acc[s][:])
-                nc.sync.dma_start(out[:, s * STRIP : (s + 1) * STRIP], result[:])
+                nc.scalar.dma_start(out[:, s * STRIP : (s + 1) * STRIP], result[:])

@@ -147,25 +147,21 @@ def tile_attend_ownlists_positions_kernel(tc, query, keys_words, keys_scales, po
             if n == 0:
                 nc.vector.tensor_reduce(neg_max[:], logits[:], AXIS.X, ALU.max, negate=True)
 
-        v_early = sb.tile([P, 4 * STRIP, PACK], BF16, name="v_early", tag="early", align_bytes=64)
+        v_early = sb.tile([P, E, PACK], BF16, name="v_early", tag="early", align_bytes=64)
         cast_values(nc.scalar.copy, v_early[:, 0:HALF], v_raw[0, 0][:])
-        cast_values(nc.scalar.copy, v_early[:, HALF : 3 * STRIP], v_raw[0, HALF][:, :, 0:STRIP])
-        cast_values(nc.scalar.copy, v_early[:, 3 * STRIP : 4 * STRIP], v_raw[1, 0][:, :, 0:STRIP])
-        v_late = sb.tile([P, 2 * STRIP, PACK], BF16, name="v_late", tag="keys_free", align_bytes=64)
-        cast_values(nc.scalar.copy, v_late[:, 0:STRIP], v_raw[1, 0][:, :, STRIP:HALF])
-        cast_values(nc.scalar.copy, v_late[:, STRIP:HALF], v_raw[1, HALF][:, :, 0:STRIP])
+        cast_values(nc.scalar.copy, v_early[:, HALF:E], v_raw[0, HALF][:])
+        v_late = sb.tile([P, HALF, PACK], BF16, name="v_late", tag="keys_free", align_bytes=64)
+        cast_values(nc.scalar.copy, v_late[:], v_raw[1, 0][:])
 
         total = sb.tile([P, 1], F32, name="total")
-        probs_listed = sb.tile([P, I], F32, name="probs_listed", tag="v_raw0_0", align_bytes=64)
+        probs_listed = sb.tile([P, I], F32, name="probs_listed", tag="v_raw0_256", align_bytes=64)
         nc.scalar.activation(probs_listed[:], logits[:], ACT.Exp, bias=neg_max[:], scale=1.0, accum_out=total[:])
         inv_total = sb.tile([P, 1], F32, name="inv_total")
 
         nc.vector.reciprocal(inv_total[:], total[:])
-        quantise_values(v_early[:], ((0, 0), (0, 1), (0, 2), (1, 0)), "v_raw0_0")
-        v_last = sb.tile([P, PASSES, STRIP, PACK], BF16, name="v_last", tag="early", align_bytes=64)
-        for g in reversed(range(PASSES)):
-            raw = v_raw[g, HALF][:, :, STRIP:HALF].rearrange("p j e -> p e j")
-            nc.gpsimd.tensor_scalar(v_last[:, g], raw, 1.0, 0.0, ALU.mult, ALU.add)
+        quantise_values(v_early[:], ((0, 0), (0, 1), (0, 2), (0, 3)), "v_raw0_256")
+        v_last = sb.tile([P, HALF, PACK], BF16, name="v_last", tag="early", align_bytes=64)
+        nc.gpsimd.tensor_scalar(v_last[:], v_raw[1, HALF][:].rearrange("p j e -> p e j"), 1.0, 0.0, ALU.mult, ALU.add)
 
         probs = sb.tile([P, PASSES, 2, P, 2], F32, name="probs", tag="v_raw1_0", align_bytes=64)
         w_bf = sb.tile([P, PASSES, 2, P, 2], BF16, name="w_bf", tag="w_bf", align_bytes=64)
@@ -188,31 +184,26 @@ def tile_attend_ownlists_positions_kernel(tc, query, keys_words, keys_scales, po
             w_grouped.append(grouped)
 
         acc = [ps.tile([Q, STRIP], F32, name="acc%d" % s, tag=("main0", "main1", "acc2", "acc3")[s]) for s in range(4)]
-        w_codes, w_scales = [], []
-
-        def multiply(g, s, first_pass):
-            nc.tensor.matmul_mx(
-                acc[s][:], lhsT=w_codes[g][:].bitcast(FP8X4), lhsT_scale=w_scales[g][:],
-                rhs=v_codes[g, s].bitcast(FP8X4), rhs_scale=v_scales[g, s],
-                start=(g == first_pass), stop=(g != first_pass),
-            )
-
-        quantise_values(v_late[:], ((1, 1), (1, 2)), "placed")
         for g in range(PASSES):
-            w_codes.append(sb.tile([P, Q], U32, name="w_codes%d" % g, align_bytes=64))
-            w_scales.append(sb.tile([P, Q], U8, name="w_scales%d" % g, align_bytes=64))
-            nc.vector.quantize_mx(w_codes[g][:].bitcast(FP8X4), w_scales[g][:], w_grouped[g][:])
-            quantise_values(v_last[:, 1 - g], ((1 - g, 3),), ("w_bf", "w_grouped1")[g])
-            for s in range(3):
-                multiply(g, s, 0)
-        for g in reversed(range(PASSES)):
-            multiply(g, 3, 1)
+            quantise_values((v_late, v_last)[g][:], ((1, 2 * g), (1, 2 * g + 1)), ("placed", "w_bf")[g])
+            w_codes = sb.tile([P, Q], U32, name="w_codes%d" % g, align_bytes=64)
+            w_scales = sb.tile([P, Q], U8, name="w_scales%d" % g, align_bytes=64)
+            nc.vector.quantize_mx(w_codes[:].bitcast(FP8X4), w_scales[:], w_grouped[g][:])
+            for s in range(4):
+                nc.tensor.matmul_mx(
+                    acc[s][:], lhsT=w_codes[:].bitcast(FP8X4), lhsT_scale=w_scales[:],
+                    rhs=v_codes[g, s].bitcast(FP8X4), rhs_scale=v_scales[g, s],
+                    start=(g == 0), stop=(g == PASSES - 1),
+                )
 
-        for s in range(4):
-            result = sb.tile([Q, STRIP], F32, name="result%d" % s)
-            if s % 2 == 1:
-                nc.vector.tensor_copy(result[:], acc[s][:])
-                nc.sync.dma_start(out[:, s * STRIP : (s + 1) * STRIP], result[:])
-            else:
-                nc.scalar.copy(result[:], acc[s][:])
-                nc.scalar.dma_start(out[:, s * STRIP : (s + 1) * STRIP], result[:])
+        front = sb.tile([Q, HALF], F32, name="front")
+        for s in range(2):
+            nc.scalar.copy(front[:, s * STRIP : (s + 1) * STRIP], acc[s][:])
+        nc.scalar.dma_start(out[:, 0:HALF], front[:])
+        third = sb.tile([Q, STRIP], F32, name="third")
+        nc.vector.tensor_copy(third[:], acc[2][:])
+        nc.sync.dma_start(out[:, HALF : 3 * STRIP], third[:])
+        fourth = sb.tile([Q, STRIP], F32, name="fourth")
+        nc.vector.tensor_copy(fourth[:], acc[3][:])
+        nc.sync.dma_start(out[0 : Q // 2, 3 * STRIP : E], fourth[0 : Q // 2])
+        nc.scalar.dma_start(out[Q // 2 : Q, 3 * STRIP : E], fourth[Q // 2 : Q])

@@ -150,18 +150,21 @@ def tile_attend_ownlists_positions_kernel(tc, query, keys_words, keys_scales, po
         v_early = sb.tile([P, E, PACK], BF16, name="v_early", tag="early", align_bytes=64)
         cast_values(nc.scalar.copy, v_early[:, 0:HALF], v_raw[0, 0][:])
         cast_values(nc.scalar.copy, v_early[:, HALF:E], v_raw[0, HALF][:])
-        v_late = sb.tile([P, HALF, PACK], BF16, name="v_late", tag="keys_free", align_bytes=64)
-        cast_values(nc.scalar.copy, v_late[:], v_raw[1, 0][:])
+        v_late = sb.tile([P, 3 * STRIP, PACK], BF16, name="v_late", tag="keys_free", align_bytes=64)
+        cast_values(nc.scalar.copy, v_late[:, 0:HALF], v_raw[1, 0][:])
 
         total = sb.tile([P, 1], F32, name="total")
         probs_listed = sb.tile([P, I], F32, name="probs_listed", tag="v_raw0_256", align_bytes=64)
         nc.scalar.activation(probs_listed[:], logits[:], ACT.Exp, bias=neg_max[:], scale=1.0, accum_out=total[:])
+        cast_values(nc.scalar.copy, v_late[:, HALF : 3 * STRIP], v_raw[1, HALF][:, :, 0:STRIP])
         inv_total = sb.tile([P, 1], F32, name="inv_total")
 
         nc.vector.reciprocal(inv_total[:], total[:])
         quantise_values(v_early[:], ((0, 0), (0, 1), (0, 2), (0, 3)), "v_raw0_256")
-        v_last = sb.tile([P, HALF, PACK], BF16, name="v_last", tag="early", align_bytes=64)
-        nc.gpsimd.tensor_scalar(v_last[:], v_raw[1, HALF][:].rearrange("p j e -> p e j"), 1.0, 0.0, ALU.mult, ALU.add)
+        v_last = sb.tile([P, STRIP, PACK], BF16, name="v_last", tag="early", align_bytes=64)
+        nc.gpsimd.tensor_scalar(
+            v_last[:], v_raw[1, HALF][:, :, STRIP:HALF].rearrange("p j e -> p e j"), 1.0, 0.0, ALU.mult, ALU.add
+        )
 
         probs = sb.tile([P, PASSES, 2, P, 2], F32, name="probs", tag="v_raw1_0", align_bytes=64)
         w_bf = sb.tile([P, PASSES, 2, P, 2], BF16, name="w_bf", tag="w_bf", align_bytes=64)
@@ -185,7 +188,11 @@ def tile_attend_ownlists_positions_kernel(tc, query, keys_words, keys_scales, po
 
         acc = [ps.tile([Q, STRIP], F32, name="acc%d" % s, tag=("main0", "main1", "acc2", "acc3")[s]) for s in range(4)]
         for g in range(PASSES):
-            quantise_values((v_late, v_last)[g][:], ((1, 2 * g), (1, 2 * g + 1)), ("placed", "w_bf")[g])
+            if g == 0:
+                quantise_values(v_late[:, 0:HALF], ((1, 0), (1, 1)), "placed")
+            else:
+                quantise_values(v_late[:, HALF : 3 * STRIP], ((1, 2),), "w_bf")
+                quantise_values(v_last[:], ((1, 3),), "w_grouped0")
             w_codes = sb.tile([P, Q], U32, name="w_codes%d" % g, align_bytes=64)
             w_scales = sb.tile([P, Q], U8, name="w_scales%d" % g, align_bytes=64)
             nc.vector.quantize_mx(w_codes[:].bitcast(FP8X4), w_scales[:], w_grouped[g][:])
@@ -196,14 +203,10 @@ def tile_attend_ownlists_positions_kernel(tc, query, keys_words, keys_scales, po
                     start=(g == 0), stop=(g == PASSES - 1),
                 )
 
-        front = sb.tile([Q, HALF], F32, name="front")
-        for s in range(2):
-            nc.scalar.copy(front[:, s * STRIP : (s + 1) * STRIP], acc[s][:])
-        nc.scalar.dma_start(out[:, 0:HALF], front[:])
-        third = sb.tile([Q, STRIP], F32, name="third")
-        nc.vector.tensor_copy(third[:], acc[2][:])
-        nc.sync.dma_start(out[:, HALF : 3 * STRIP], third[:])
-        fourth = sb.tile([Q, STRIP], F32, name="fourth")
-        nc.vector.tensor_copy(fourth[:], acc[3][:])
-        nc.sync.dma_start(out[0 : Q // 2, 3 * STRIP : E], fourth[0 : Q // 2])
-        nc.scalar.dma_start(out[Q // 2 : Q, 3 * STRIP : E], fourth[Q // 2 : Q])
+        results = []
+        for s in range(4):
+            result = sb.tile([Q, STRIP], F32, name="result%d" % s)
+            (nc.scalar.copy if s < 2 else nc.vector.tensor_copy)(result[:], acc[s][:])
+            results.append(result)
+        for s in range(4):
+            (nc.scalar if s in (1, 2) else nc.sync).dma_start(out[:, s * STRIP : (s + 1) * STRIP], results[s][:])

@@ -26,7 +26,8 @@ STRIP = HALF // 2
 SLOT_HALF = I // 2
 VALUE_LOADS = ((0, 0, 256), (0, 256, 512), (1, 0, 256), (1, 256, 512))
 SCORE_RUNS = ((0, 256), (256, 512), (512, 768), (768, 896), (896, 1024))
-PLANE_PIECES = ((0, slice(0, 128)), (1, slice(0, 88)), (1, slice(88, 128)))
+LAST_PLANE = ((1, slice(0, 88)), (1, slice(88, 128)))
+PLANE_PIECES = (((0, slice(0, 40)), (0, slice(40, 128))) + LAST_PLANE, ((0, slice(0, 128)),) + LAST_PLANE)
 UNLISTED = -(2.0**127)
 
 
@@ -147,20 +148,21 @@ def tile_attend_ownlists_positions_kernel(tc, query, keys_words, keys_scales, po
             if n == 0:
                 nc.vector.tensor_reduce(neg_max[:], logits[:], AXIS.X, ALU.max, negate=True)
 
-        v_early = sb.tile([P, E, PACK], BF16, name="v_early", tag="early", align_bytes=64)
-        cast_values(nc.scalar.copy, v_early[:, 0:HALF], v_raw[0, 0][:])
-        cast_values(nc.scalar.copy, v_early[:, HALF:E], v_raw[0, HALF][:])
-        v_late = sb.tile([P, 3 * STRIP, PACK], BF16, name="v_late", tag="keys_free", align_bytes=64)
-        cast_values(nc.scalar.copy, v_late[:, 0:HALF], v_raw[1, 0][:])
+        v_first = sb.tile([P, HALF, PACK], BF16, name="v_first", tag="early", align_bytes=64)
+        cast_values(nc.scalar.copy, v_first[:], v_raw[0, 0][:])
+        v_mid = sb.tile([P, E, PACK], BF16, name="v_mid", tag="keys_free", align_bytes=64)
+        cast_values(nc.scalar.copy, v_mid[:, 0:HALF], v_raw[0, HALF][:])
+        cast_values(nc.scalar.copy, v_mid[:, HALF:E], v_raw[1, 0][:])
 
         total = sb.tile([P, 1], F32, name="total")
         probs_listed = sb.tile([P, I], F32, name="probs_listed", tag="v_raw0_256", align_bytes=64)
         nc.scalar.activation(probs_listed[:], logits[:], ACT.Exp, bias=neg_max[:], scale=1.0, accum_out=total[:])
-        cast_values(nc.scalar.copy, v_late[:, HALF : 3 * STRIP], v_raw[1, HALF][:, :, 0:STRIP])
+        v_third = sb.tile([P, STRIP, PACK], BF16, name="v_third", tag="v_raw0_0", align_bytes=64)
+        cast_values(nc.scalar.copy, v_third[:], v_raw[1, HALF][:, :, 0:STRIP])
         inv_total = sb.tile([P, 1], F32, name="inv_total")
 
         nc.vector.reciprocal(inv_total[:], total[:])
-        quantise_values(v_early[:], ((0, 0), (0, 1), (0, 2), (0, 3)), "v_raw0_256")
+        quantise_values(v_first[:], ((0, 0), (0, 1)), "v_raw0_256")
         v_last = sb.tile([P, STRIP, PACK], BF16, name="v_last", tag="early", align_bytes=64)
         nc.gpsimd.tensor_scalar(
             v_last[:], v_raw[1, HALF][:, :, STRIP:HALF].rearrange("p j e -> p e j"), 1.0, 0.0, ALU.mult, ALU.add
@@ -170,13 +172,13 @@ def tile_attend_ownlists_positions_kernel(tc, query, keys_words, keys_scales, po
         w_bf = sb.tile([P, PASSES, 2, P, 2], BF16, name="w_bf", tag="w_bf", align_bytes=64)
         for g in range(PASSES):
             placed_pairs = placed[:, g * K_PASS : (g + 1) * K_PASS].rearrange("q (p u e) -> q u p e", u=2, e=2)
-            for u, rows in PLANE_PIECES:
+            for u, rows in PLANE_PIECES[g]:
                 nc.scalar.activation(probs[:, g, u, rows], placed_pairs[:, u, rows], ACT.Exp, bias=neg_max[:], scale=1.0)
         w_grouped = []
         for g in range(PASSES):
             turned = ps.tile([P, 2, Q], F32, name="turned%d" % g, tag="side%d" % g)
             fac_pairs = fac_bank[g][:].rearrange("q (u e) p -> q u p e", e=2)
-            for u, rows in PLANE_PIECES:
+            for u, rows in PLANE_PIECES[g]:
                 nc.vector.scalar_tensor_tensor(
                     w_bf[:, g, u, rows], probs[:, g, u, rows], inv_total[:], fac_pairs[:, u, rows], ALU.mult, ALU.mult
                 )
@@ -189,9 +191,9 @@ def tile_attend_ownlists_positions_kernel(tc, query, keys_words, keys_scales, po
         acc = [ps.tile([Q, STRIP], F32, name="acc%d" % s, tag=("main0", "main1", "acc2", "acc3")[s]) for s in range(4)]
         for g in range(PASSES):
             if g == 0:
-                quantise_values(v_late[:, 0:HALF], ((1, 0), (1, 1)), "placed")
+                quantise_values(v_mid[:], ((0, 2), (0, 3), (1, 0), (1, 1)), "placed")
             else:
-                quantise_values(v_late[:, HALF : 3 * STRIP], ((1, 2),), "w_bf")
+                quantise_values(v_third[:], ((1, 2),), "w_bf")
                 quantise_values(v_last[:], ((1, 3),), "w_grouped0")
             w_codes = sb.tile([P, Q], U32, name="w_codes%d" % g, align_bytes=64)
             w_scales = sb.tile([P, Q], U8, name="w_scales%d" % g, align_bytes=64)

@@ -89,7 +89,7 @@ def tile_attend_ownlists_positions_kernel(tc, query, keys_words, keys_scales, po
         nc.vector.tensor_copy(
             q_bf[:].rearrange("p (c i) j -> p c j i", i=4), q_raw[:].rearrange("p j (c i) -> p c j i", i=4)
         )
-        q_codes = sb.tile([P, Q], U32, name="q_codes", tag="keys_free", align_bytes=64)
+        q_codes = sb.tile([P, Q], U32, name="q_codes", align_bytes=64)
         q_scales = sb.tile([P, Q], U8, name="q_scales", tag="zeros", align_bytes=64)
         nc.vector.quantize_mx(q_codes[:].bitcast(FP8X4), q_scales[:], q_bf[:].rearrange("p q j -> p (q j)"))
 
@@ -104,7 +104,7 @@ def tile_attend_ownlists_positions_kernel(tc, query, keys_words, keys_scales, po
         for slots in slot_halves:
             nc.vector.scalar_tensor_tensor(penalty[:, slots], dist[:, slots], slope_col[:], dist[:, slots], ALU.mult, ALU.mult)
 
-        scores = sb.tile([P, T], F32, name="scores")
+        scores = sb.tile([P, T], F32, name="scores", tag="scores", align_bytes=64)
         for n, (first, last) in enumerate(SCORE_RUNS):
             bank = ps.tile([P, last - first], F32, name="score_bank%d" % n, tag=("main0", "main1", "main2", "main3", "acc2")[n])
             plane = first // KEY_RUN
@@ -150,8 +150,10 @@ def tile_attend_ownlists_positions_kernel(tc, query, keys_words, keys_scales, po
 
         v_first = sb.tile([P, HALF, PACK], BF16, name="v_first", tag="early", align_bytes=64)
         cast_values(nc.scalar.copy, v_first[:], v_raw[0, 0][:])
-        v_mid = sb.tile([P, E, PACK], BF16, name="v_mid", tag="keys_free", align_bytes=64)
-        cast_values(nc.scalar.copy, v_mid[:, 0:HALF], v_raw[0, HALF][:])
+        v_mid = sb.tile([P, E, PACK], BF16, name="v_mid", tag="scores", align_bytes=64)
+        nc.gpsimd.tensor_scalar(
+            v_mid[:, 0:HALF], v_raw[0, HALF][:].rearrange("p j e -> p e j"), 1.0, 0.0, ALU.mult, ALU.add
+        )
         cast_values(nc.scalar.copy, v_mid[:, HALF:E], v_raw[1, 0][:])
 
         total = sb.tile([P, 1], F32, name="total")

@@ -22,6 +22,7 @@ K_PASS = P * PACK
 PASSES = T // K_PASS
 HALF = E // 2
 KEY_RUN = T // 4
+KEY_HALF = T // 2
 STRIP = HALF // 2
 SLOT_HALF = I // 2
 VALUE_LOADS = ((0, 0, 256), (0, 256, 512), (1, 0, 256), (1, 256, 512))
@@ -40,7 +41,7 @@ def tile_attend_ownlists_positions_kernel(tc, query, keys_words, keys_scales, po
         offsets = sb.tile([P, I // 16], U16, name="offsets")
         pos_all = sb.tile([P, T], F32, name="pos_all")
         q_raw = sb.tile([P, PACK, Q], F32, name="q_raw")
-        k_codes = sb.tile([P, T], U32, name="k_codes", tag="early", align_bytes=64)
+        k_codes = [sb.tile([P, KEY_HALF], U32, name="k_codes%d" % n, align_bytes=64) for n in range(2)]
         k_scales = sb.tile([P, KEY_RUN], U8, name="k_scales", align_bytes=64)
         qpos_col = sb.tile([P, 1], F32, name="qpos_col")
         slope_col = sb.tile([P, 1], F32, name="slope_col")
@@ -57,6 +58,7 @@ def tile_attend_ownlists_positions_kernel(tc, query, keys_words, keys_scales, po
         )
         nc.vector.memset(placed[:], UNLISTED)
 
+        key_words = keys_words[0].rearrange("p n t -> p (n t)").bitcast(I32)
         nc.sync.dma_start(pos_rows[:], pos[0].rearrange("(n c) -> n c", c=T // P))
         nc.sync.dma_start(qpos_col[:], qpos)
         nc.sync.dma_start(q_raw[:], query.rearrange("(p j) q -> p j q", j=PACK))
@@ -65,8 +67,9 @@ def tile_attend_ownlists_positions_kernel(tc, query, keys_words, keys_scales, po
                 k_scales[32 * quad : 32 * quad + 16, :].bitcast(I32),
                 keys_scales[0, 4 * quad : 4 * quad + 4, :].bitcast(I32).rearrange("r (k n) -> k r n", k=4),
             )
-        nc.sync.dma_start(k_codes[:].bitcast(I32), keys_words[0].rearrange("p n t -> p (n t)").bitcast(I32))
+        nc.sync.dma_start(k_codes[0][:].bitcast(I32), key_words[:, 0:KEY_HALF])
         nc.sync.dma_start(offsets[:], offs)
+        nc.sync.dma_start(k_codes[1][:].bitcast(I32), key_words[:, KEY_HALF:T])
         nc.sync.dma_start(slope_col[:], slope)
 
         v_raw = {}
@@ -92,28 +95,37 @@ def tile_attend_ownlists_positions_kernel(tc, query, keys_words, keys_scales, po
         q_codes = sb.tile([P, Q], U32, name="q_codes", align_bytes=64)
         q_scales = sb.tile([P, Q], U8, name="q_scales", tag="zeros", align_bytes=64)
         nc.vector.quantize_mx(q_codes[:].bitcast(FP8X4), q_scales[:], q_bf[:].rearrange("p q j -> p (q j)"))
-
         qpos_wide = sb.tile([P, SLOT_HALF], F32, name="qpos_wide")
         nc.vector.tensor_copy(qpos_wide[:], qpos_col[:].to_broadcast([P, SLOT_HALF]))
-        dist = sb.tile([P, I], F32, name="dist")
-        penalty = sb.tile([P, I], F32, name="penalty")
-        slot_halves = [slice(n * SLOT_HALF, (n + 1) * SLOT_HALF) for n in range(2)]
-        for n in range(2):
-            half_offsets = offsets[:, n * SLOT_HALF // 16 : (n + 1) * SLOT_HALF // 16]
-            nc.vector.tensor_tensor(dist[:, slot_halves[n]], pos_all[:].indirect(half_offsets), qpos_wide[:], ALU.subtract)
-        for slots in slot_halves:
-            nc.vector.scalar_tensor_tensor(penalty[:, slots], dist[:, slots], slope_col[:], dist[:, slots], ALU.mult, ALU.mult)
 
-        scores = sb.tile([P, T], F32, name="scores", tag="scores", align_bytes=64)
+        first_slots, second_slots = slice(0, SLOT_HALF), slice(SLOT_HALF, I)
+        first_offsets, second_offsets = offsets[:, 0 : SLOT_HALF // 16], offsets[:, SLOT_HALF // 16 : I // 16]
+
+        scores = sb.tile([P, T], F32, name="scores")
+        banks = []
         for n, (first, last) in enumerate(SCORE_RUNS):
             bank = ps.tile([P, last - first], F32, name="score_bank%d" % n, tag=("main0", "main1", "main2", "main3", "acc2")[n])
-            plane = first // KEY_RUN
+            plane, half = first // KEY_RUN, first // KEY_HALF
             nc.tensor.matmul_mx(
                 bank[:], lhsT=q_codes[:].bitcast(FP8X4), lhsT_scale=q_scales[:],
-                rhs=k_codes[:, first:last].bitcast(FP8X4),
+                rhs=k_codes[half][:, first - half * KEY_HALF : last - half * KEY_HALF].bitcast(FP8X4),
                 rhs_scale=k_scales[4 * plane : P, first - plane * KEY_RUN : last - plane * KEY_RUN], start=True, stop=True,
             )
-            nc.scalar.copy(scores[:, first:last], bank[:])
+            banks.append(bank)
+
+        def empty_bank(copy, n):
+            copy(scores[:, SCORE_RUNS[n][0] : SCORE_RUNS[n][1]], banks[n][:])
+
+        dist = sb.tile([P, SLOT_HALF], F32, name="dist")
+        penalty = sb.tile([P, SLOT_HALF], F32, name="penalty")
+        pos_second = sb.tile([P, SLOT_HALF], F32, name="pos_second", tag="pos_second", align_bytes=64)
+        empty_bank(nc.vector.tensor_copy, 0)
+        nc.vector.tensor_tensor(dist[:], pos_all[:].indirect(first_offsets), qpos_wide[:], ALU.subtract)
+        nc.scalar.activation(pos_second[:], pos_all[:].indirect(second_offsets), ACT.Copy)
+        empty_bank(nc.vector.tensor_copy, 1)
+        nc.vector.scalar_tensor_tensor(penalty[:], dist[:], slope_col[:], dist[:], ALU.mult, ALU.mult)
+        for n in range(2, len(SCORE_RUNS)):
+            empty_bank(nc.scalar.copy, n)
 
         fac_bank = []
         for g in range(PASSES):
@@ -123,9 +135,15 @@ def tile_attend_ownlists_positions_kernel(tc, query, keys_words, keys_scales, po
             fac_bank.append(spread)
 
         logits = sb.tile([P, I], F32, name="logits", tag="late", align_bytes=64)
-        for n, slots in enumerate(slot_halves):
-            half_offsets = offsets[:, n * SLOT_HALF // 16 : (n + 1) * SLOT_HALF // 16]
-            nc.vector.tensor_tensor(logits[:, slots], scores[:].indirect(half_offsets), penalty[:, slots], ALU.subtract)
+        nc.vector.tensor_tensor(logits[:, first_slots], scores[:].indirect(first_offsets), penalty[:], ALU.subtract)
+
+        square = sb.tile([P, SLOT_HALF], F32, name="square", tag="square", align_bytes=64)
+        scores_second = sb.tile([P, SLOT_HALF], F32, name="scores_second", tag="scores_second", align_bytes=64)
+        penalty_second = sb.tile([P, SLOT_HALF], F32, name="penalty_second", tag="penalty_second", align_bytes=64)
+        nc.scalar.activation(square[:], pos_second[:], ACT.Square, bias=qpos_col[:], scale=-1.0)
+        nc.scalar.activation(scores_second[:], scores[:].indirect(second_offsets), ACT.Copy)
+        nc.scalar.activation(penalty_second[:], square[:], ACT.Copy, scale=slope_col[:])
+        nc.gpsimd.tensor_tensor(logits[:, second_slots], scores_second[:], penalty_second[:], ALU.subtract)
 
         v_codes, v_scales = {}, {}
 
@@ -138,37 +156,34 @@ def tile_attend_ownlists_positions_kernel(tc, query, keys_words, keys_scales, po
                 v_codes[key] = codes[:, n * STRIP : (n + 1) * STRIP]
                 v_scales[key] = scales[:, n * STRIP : (n + 1) * STRIP]
 
-        def cast_values(copy, staged, raw):
-            copy(staged.rearrange("p (c i) j -> p c j i", i=4), raw.rearrange("p j (c i) -> p c j i", i=4))
+        def cast_on_scalar(staged, raw):
+            nc.scalar.copy(staged.rearrange("p (c i) j -> p c j i", i=4), raw.rearrange("p j (c i) -> p c j i", i=4))
+
+        def cast_on_gpsimd(staged, raw):
+            nc.gpsimd.tensor_scalar(staged, raw.rearrange("p j e -> p e j"), 1.0, 0.0, ALU.mult, ALU.add)
 
         neg_max = sb.tile([P, 1], F32, name="neg_max")
-        for n, slots in enumerate(slot_halves):
-            half_offsets = offsets[:, n * SLOT_HALF // 16 : (n + 1) * SLOT_HALF // 16]
-            nc.vector.tensor_copy(placed[:].indirect(half_offsets), logits[:, slots])
-            if n == 0:
-                nc.vector.tensor_reduce(neg_max[:], logits[:], AXIS.X, ALU.max, negate=True)
+        nc.vector.tensor_copy(placed[:].indirect(first_offsets), logits[:, first_slots])
+        nc.vector.tensor_reduce(neg_max[:], logits[:], AXIS.X, ALU.max, negate=True)
+        nc.vector.tensor_copy(placed[:].indirect(second_offsets), logits[:, second_slots])
 
-        v_first = sb.tile([P, HALF, PACK], BF16, name="v_first", tag="early", align_bytes=64)
-        cast_values(nc.scalar.copy, v_first[:], v_raw[0, 0][:])
-        v_mid = sb.tile([P, E, PACK], BF16, name="v_mid", tag="scores", align_bytes=64)
-        nc.gpsimd.tensor_scalar(
-            v_mid[:, 0:HALF], v_raw[0, HALF][:].rearrange("p j e -> p e j"), 1.0, 0.0, ALU.mult, ALU.add
-        )
-        cast_values(nc.scalar.copy, v_mid[:, HALF:E], v_raw[1, 0][:])
+        v_first = sb.tile([P, HALF, PACK], BF16, name="v_first", tag="pos_second", align_bytes=64)
+        cast_on_scalar(v_first[:], v_raw[0, 0][:])
+        v_mid = sb.tile([P, E, PACK], BF16, name="v_mid", tag="scores_second", align_bytes=64)
+        cast_on_gpsimd(v_mid[:, HALF:E], v_raw[1, 0][:])
+        cast_on_scalar(v_mid[:, 0:HALF], v_raw[0, HALF][:])
 
         total = sb.tile([P, 1], F32, name="total")
         probs_listed = sb.tile([P, I], F32, name="probs_listed", tag="v_raw0_256", align_bytes=64)
         nc.scalar.activation(probs_listed[:], logits[:], ACT.Exp, bias=neg_max[:], scale=1.0, accum_out=total[:])
         v_third = sb.tile([P, STRIP, PACK], BF16, name="v_third", tag="v_raw0_0", align_bytes=64)
-        cast_values(nc.scalar.copy, v_third[:], v_raw[1, HALF][:, :, 0:STRIP])
+        cast_on_scalar(v_third[:], v_raw[1, HALF][:, :, 0:STRIP])
+        v_last = sb.tile([P, STRIP, PACK], BF16, name="v_last", tag="penalty_second", align_bytes=64)
+        cast_on_gpsimd(v_last[:], v_raw[1, HALF][:, :, STRIP:HALF])
         inv_total = sb.tile([P, 1], F32, name="inv_total")
 
         nc.vector.reciprocal(inv_total[:], total[:])
         quantise_values(v_first[:], ((0, 0), (0, 1)), "v_raw0_256")
-        v_last = sb.tile([P, STRIP, PACK], BF16, name="v_last", tag="early", align_bytes=64)
-        nc.gpsimd.tensor_scalar(
-            v_last[:], v_raw[1, HALF][:, :, STRIP:HALF].rearrange("p j e -> p e j"), 1.0, 0.0, ALU.mult, ALU.add
-        )
 
         probs = sb.tile([P, PASSES, 2, P, 2], F32, name="probs", tag="v_raw1_0", align_bytes=64)
         w_bf = sb.tile([P, PASSES, 2, P, 2], BF16, name="w_bf", tag="w_bf", align_bytes=64)

@@ -22,7 +22,6 @@ K_PASS = P * PACK
 PASSES = T // K_PASS
 HALF = E // 2
 KEY_RUN = T // 4
-KEY_HALF = T // 2
 STRIP = HALF // 2
 SLOT_HALF = I // 2
 VALUE_LOADS = ((0, 0, 256), (0, 256, 512), (1, 0, 256), (1, 256, 512))
@@ -41,7 +40,7 @@ def tile_attend_ownlists_positions_kernel(tc, query, keys_words, keys_scales, po
         offsets = sb.tile([P, I // 16], U16, name="offsets")
         pos_all = sb.tile([P, T], F32, name="pos_all")
         q_raw = sb.tile([P, PACK, Q], F32, name="q_raw")
-        k_codes = [sb.tile([P, KEY_HALF], U32, name="k_codes%d" % n, align_bytes=64) for n in range(2)]
+        k_codes = sb.tile([P, T], U32, name="k_codes", tag="early", align_bytes=64)
         k_scales = sb.tile([P, KEY_RUN], U8, name="k_scales", align_bytes=64)
         qpos_col = sb.tile([P, 1], F32, name="qpos_col")
         slope_col = sb.tile([P, 1], F32, name="slope_col")
@@ -67,9 +66,8 @@ def tile_attend_ownlists_positions_kernel(tc, query, keys_words, keys_scales, po
                 k_scales[32 * quad : 32 * quad + 16, :].bitcast(I32),
                 keys_scales[0, 4 * quad : 4 * quad + 4, :].bitcast(I32).rearrange("r (k n) -> k r n", k=4),
             )
-        nc.sync.dma_start(k_codes[0][:].bitcast(I32), key_words[:, 0:KEY_HALF])
+        nc.sync.dma_start(k_codes[:].bitcast(I32), key_words)
         nc.sync.dma_start(offsets[:], offs)
-        nc.sync.dma_start(k_codes[1][:].bitcast(I32), key_words[:, KEY_HALF:T])
         nc.sync.dma_start(slope_col[:], slope)
 
         v_raw = {}
@@ -105,10 +103,10 @@ def tile_attend_ownlists_positions_kernel(tc, query, keys_words, keys_scales, po
         banks = []
         for n, (first, last) in enumerate(SCORE_RUNS):
             bank = ps.tile([P, last - first], F32, name="score_bank%d" % n, tag=("main0", "main1", "main2", "main3", "acc2")[n])
-            plane, half = first // KEY_RUN, first // KEY_HALF
+            plane = first // KEY_RUN
             nc.tensor.matmul_mx(
                 bank[:], lhsT=q_codes[:].bitcast(FP8X4), lhsT_scale=q_scales[:],
-                rhs=k_codes[half][:, first - half * KEY_HALF : last - half * KEY_HALF].bitcast(FP8X4),
+                rhs=k_codes[:, first:last].bitcast(FP8X4),
                 rhs_scale=k_scales[4 * plane : P, first - plane * KEY_RUN : last - plane * KEY_RUN], start=True, stop=True,
             )
             banks.append(bank)
@@ -116,15 +114,16 @@ def tile_attend_ownlists_positions_kernel(tc, query, keys_words, keys_scales, po
         def empty_bank(copy, n):
             copy(scores[:, SCORE_RUNS[n][0] : SCORE_RUNS[n][1]], banks[n][:])
 
-        dist = sb.tile([P, SLOT_HALF], F32, name="dist")
-        penalty = sb.tile([P, SLOT_HALF], F32, name="penalty")
-        pos_second = sb.tile([P, SLOT_HALF], F32, name="pos_second", tag="pos_second", align_bytes=64)
-        empty_bank(nc.vector.tensor_copy, 0)
-        nc.vector.tensor_tensor(dist[:], pos_all[:].indirect(first_offsets), qpos_wide[:], ALU.subtract)
-        nc.scalar.activation(pos_second[:], pos_all[:].indirect(second_offsets), ACT.Copy)
-        empty_bank(nc.vector.tensor_copy, 1)
-        nc.vector.scalar_tensor_tensor(penalty[:], dist[:], slope_col[:], dist[:], ALU.mult, ALU.mult)
-        for n in range(2, len(SCORE_RUNS)):
+        dist = sb.tile([P, I], F32, name="dist")
+        penalty = sb.tile([P, SLOT_HALF], F32, name="penalty", tag="penalty", align_bytes=64)
+        penalty_second = sb.tile([P, SLOT_HALF], F32, name="penalty_second", tag="penalty_second", align_bytes=64)
+        nc.vector.tensor_tensor(dist[:, first_slots], pos_all[:].indirect(first_offsets), qpos_wide[:], ALU.subtract)
+        nc.vector.tensor_tensor(dist[:, second_slots], pos_all[:].indirect(second_offsets), qpos_wide[:], ALU.subtract)
+        nc.vector.scalar_tensor_tensor(penalty[:], dist[:, first_slots], slope_col[:], dist[:, first_slots], ALU.mult, ALU.mult)
+        nc.vector.scalar_tensor_tensor(
+            penalty_second[:], dist[:, second_slots], slope_col[:], dist[:, second_slots], ALU.mult, ALU.mult
+        )
+        for n in range(len(SCORE_RUNS)):
             empty_bank(nc.scalar.copy, n)
 
         fac_bank = []
@@ -137,12 +136,8 @@ def tile_attend_ownlists_positions_kernel(tc, query, keys_words, keys_scales, po
         logits = sb.tile([P, I], F32, name="logits", tag="late", align_bytes=64)
         nc.vector.tensor_tensor(logits[:, first_slots], scores[:].indirect(first_offsets), penalty[:], ALU.subtract)
 
-        square = sb.tile([P, SLOT_HALF], F32, name="square", tag="square", align_bytes=64)
         scores_second = sb.tile([P, SLOT_HALF], F32, name="scores_second", tag="scores_second", align_bytes=64)
-        penalty_second = sb.tile([P, SLOT_HALF], F32, name="penalty_second", tag="penalty_second", align_bytes=64)
-        nc.scalar.activation(square[:], pos_second[:], ACT.Square, bias=qpos_col[:], scale=-1.0)
         nc.scalar.activation(scores_second[:], scores[:].indirect(second_offsets), ACT.Copy)
-        nc.scalar.activation(penalty_second[:], square[:], ACT.Copy, scale=slope_col[:])
         nc.gpsimd.tensor_tensor(logits[:, second_slots], scores_second[:], penalty_second[:], ALU.subtract)
 
         v_codes, v_scales = {}, {}
@@ -167,7 +162,7 @@ def tile_attend_ownlists_positions_kernel(tc, query, keys_words, keys_scales, po
         nc.vector.tensor_reduce(neg_max[:], logits[:], AXIS.X, ALU.max, negate=True)
         nc.vector.tensor_copy(placed[:].indirect(second_offsets), logits[:, second_slots])
 
-        v_first = sb.tile([P, HALF, PACK], BF16, name="v_first", tag="pos_second", align_bytes=64)
+        v_first = sb.tile([P, HALF, PACK], BF16, name="v_first", tag="penalty", align_bytes=64)
         cast_on_scalar(v_first[:], v_raw[0, 0][:])
         v_mid = sb.tile([P, E, PACK], BF16, name="v_mid", tag="scores_second", align_bytes=64)
         cast_on_gpsimd(v_mid[:, HALF:E], v_raw[1, 0][:])

@@ -49,7 +49,7 @@ def tile_attend_ownlists_positions_kernel(tc, query, keys_words, keys_scales, po
         ident = sb.tile([P, P], F32, name="ident")
         pos_rows = sb.tile([P, T // P], F32, name="pos_rows", tag="pos_rows", align_bytes=64)
 
-        nc.gpsimd.memset(k_scales[:].bitcast(I32), 0)
+        nc.vector.memset(k_scales[:].bitcast(I32), 0)
         zeros = sb.tile([P, P], F32, name="zeros", tag="zeros", align_bytes=64)
         nc.gpsimd.memset(zeros[:], 0.0)
         nc.gpsimd.affine_select(
@@ -87,12 +87,17 @@ def tile_attend_ownlists_positions_kernel(tc, query, keys_words, keys_scales, po
             nc.scalar.activation(pos_by_row[:, :, 4 * h : 4 * h + 4], spread[:].rearrange("p c n -> p n c"), ACT.Copy)
 
         q_bf = sb.tile([P, Q, PACK], BF16, name="q_bf", align_bytes=64)
-        nc.vector.tensor_copy(
-            q_bf[:].rearrange("p (c i) j -> p c j i", i=4), q_raw[:].rearrange("p j (c i) -> p c j i", i=4)
-        )
+        query_halves = (slice(0, Q // 2), slice(Q // 2, Q))
+        for rows in query_halves:
+            nc.vector.tensor_copy(
+                q_bf[:, rows].rearrange("p (c i) j -> p c j i", i=4), q_raw[:, :, rows].rearrange("p j (c i) -> p c j i", i=4)
+            )
         q_codes = sb.tile([P, Q], U32, name="q_codes", align_bytes=64)
         q_scales = sb.tile([P, Q], U8, name="q_scales", tag="zeros", align_bytes=64)
-        nc.vector.quantize_mx(q_codes[:].bitcast(FP8X4), q_scales[:], q_bf[:].rearrange("p q j -> p (q j)"))
+        for rows in query_halves:
+            nc.vector.quantize_mx(
+                q_codes[:, rows].bitcast(FP8X4), q_scales[:, rows], q_bf[:, rows].rearrange("p q j -> p (q j)")
+            )
         qpos_wide = sb.tile([P, SLOT_HALF], F32, name="qpos_wide")
         nc.vector.tensor_copy(qpos_wide[:], qpos_col[:].to_broadcast([P, SLOT_HALF]))
 

@@ -24,7 +24,6 @@ HALF = E // 2
 KEY_RUN = T // 4
 STRIP = HALF // 2
 SLOT_HALF = I // 2
-VALUE_LOADS = ((0, 0, 256), (0, 256, 512), (1, 0, 256), (1, 256, 512))
 SCORE_RUNS = ((0, 256), (256, 512), (512, 768), (768, 896), (896, 1024))
 LAST_PLANE = ((1, slice(0, 88)), (1, slice(88, 128)))
 PLANE_PIECES = (((0, slice(0, 40)), (0, slice(40, 128))) + LAST_PLANE, ((0, slice(0, 128)),) + LAST_PLANE)
@@ -70,13 +69,12 @@ def tile_attend_ownlists_positions_kernel(tc, query, keys_words, keys_scales, po
         nc.sync.dma_start(offsets[:], offs)
         nc.sync.dma_start(slope_col[:], slope)
 
-        v_raw = {}
-        for g, first, last in VALUE_LOADS:
-            rows = vals[g * K_PASS : (g + 1) * K_PASS, :].rearrange("(p j) e -> p j e", j=PACK)
-            name = "v_raw%d_%d" % (g, first)
-            v_raw[g, first] = sb.tile([P, PACK, last - first], F32, name=name, tag=name, align_bytes=64)
-            nc.sync.dma_start(v_raw[g, first][:], rows[:, :, first:last])
-            if last == E and g == 0:
+        v_raw = []
+        for g in range(PASSES):
+            raw = sb.tile([P, PACK, E], F32, name="v_raw%d" % g, tag="v_raw%d" % g, align_bytes=64)
+            nc.sync.dma_start(raw[:], vals[g * K_PASS : (g + 1) * K_PASS, :].rearrange("(p j) e -> p j e", j=PACK))
+            v_raw.append(raw)
+            if g == 0:
                 nc.sync.dma_start(fac_rows[:], fac[0].rearrange("(g p j) -> p g j", g=PASSES, j=PACK))
 
         pos_by_row = pos_all[:].rearrange("p (n c) -> p n c", c=T // P)
@@ -168,24 +166,25 @@ def tile_attend_ownlists_positions_kernel(tc, query, keys_words, keys_scales, po
         nc.vector.tensor_copy(placed[:].indirect(second_offsets), logits[:, second_slots])
 
         v_first = sb.tile([P, HALF, PACK], BF16, name="v_first", tag="penalty", align_bytes=64)
-        cast_on_scalar(v_first[:], v_raw[0, 0][:])
+        cast_on_scalar(v_first[:], v_raw[0][:, :, 0:HALF])
         v_mid = sb.tile([P, E, PACK], BF16, name="v_mid", tag="scores_second", align_bytes=64)
-        cast_on_gpsimd(v_mid[:, HALF:E], v_raw[1, 0][:])
-        cast_on_scalar(v_mid[:, 0:HALF], v_raw[0, HALF][:])
+        cast_on_scalar(v_mid[:, 0:STRIP], v_raw[0][:, :, HALF : HALF + STRIP])
+        cast_on_gpsimd(v_mid[:, STRIP:HALF], v_raw[0][:, :, HALF + STRIP : E])
+        cast_on_gpsimd(v_mid[:, HALF:E], v_raw[1][:, :, 0:HALF])
+        v_third = sb.tile([P, STRIP, PACK], BF16, name="v_third", tag="penalty_second", align_bytes=64)
+        cast_on_scalar(v_third[:], v_raw[1][:, :, HALF : HALF + STRIP])
 
         total = sb.tile([P, 1], F32, name="total")
-        probs_listed = sb.tile([P, I], F32, name="probs_listed", tag="v_raw0_256", align_bytes=64)
+        probs_listed = sb.tile([P, I], F32, name="probs_listed", tag="v_raw0", align_bytes=64)
         nc.scalar.activation(probs_listed[:], logits[:], ACT.Exp, bias=neg_max[:], scale=1.0, accum_out=total[:])
-        v_third = sb.tile([P, STRIP, PACK], BF16, name="v_third", tag="v_raw0_0", align_bytes=64)
-        cast_on_scalar(v_third[:], v_raw[1, HALF][:, :, 0:STRIP])
-        v_last = sb.tile([P, STRIP, PACK], BF16, name="v_last", tag="penalty_second", align_bytes=64)
-        cast_on_gpsimd(v_last[:], v_raw[1, HALF][:, :, STRIP:HALF])
         inv_total = sb.tile([P, 1], F32, name="inv_total")
 
         nc.vector.reciprocal(inv_total[:], total[:])
-        quantise_values(v_first[:], ((0, 0), (0, 1)), "v_raw0_256")
+        quantise_values(v_first[:], ((0, 0), (0, 1)), "v_raw0")
+        v_last = sb.tile([P, STRIP, PACK], BF16, name="v_last", tag="penalty", align_bytes=64)
+        cast_on_gpsimd(v_last[:], v_raw[1][:, :, HALF + STRIP : E])
 
-        probs = sb.tile([P, PASSES, 2, P, 2], F32, name="probs", tag="v_raw1_0", align_bytes=64)
+        probs = sb.tile([P, PASSES, 2, P, 2], F32, name="probs", align_bytes=64)
         w_bf = sb.tile([P, PASSES, 2, P, 2], BF16, name="w_bf", tag="w_bf", align_bytes=64)
         for g in range(PASSES):
             placed_pairs = placed[:, g * K_PASS : (g + 1) * K_PASS].rearrange("q (p u e) -> q u p e", u=2, e=2)

@@ -22,6 +22,7 @@ K_PASS = P * PACK
 PASSES = T // K_PASS
 HALF = E // 2
 KEY_RUN = T // 4
+KEY_HALF = T // 2
 STRIP = HALF // 2
 SLOT_HALF = I // 2
 SCORE_RUNS = ((0, 256), (256, 512), (512, 768), (768, 896), (896, 1024))
@@ -39,11 +40,10 @@ def tile_attend_ownlists_positions_kernel(tc, query, keys_words, keys_scales, po
         offsets = sb.tile([P, I // 16], U16, name="offsets")
         pos_all = sb.tile([P, T], F32, name="pos_all")
         q_raw = sb.tile([P, PACK, Q], F32, name="q_raw")
-        k_codes = sb.tile([P, T], U32, name="k_codes", tag="early", align_bytes=64)
+        k_codes = [sb.tile([P, KEY_HALF], U32, name="k_codes%d" % n, align_bytes=64) for n in range(2)]
         k_scales = sb.tile([P, KEY_RUN], U8, name="k_scales", align_bytes=64)
         qpos_col = sb.tile([P, 1], F32, name="qpos_col")
         slope_col = sb.tile([P, 1], F32, name="slope_col")
-        fac_rows = sb.tile([P, PASSES, PACK], F32, name="fac_rows")
         placed = sb.tile([P, T], F32, name="placed", tag="placed", align_bytes=64)
         ident = sb.tile([P, P], F32, name="ident")
         pos_rows = sb.tile([P, T // P], F32, name="pos_rows", tag="pos_rows", align_bytes=64)
@@ -65,8 +65,9 @@ def tile_attend_ownlists_positions_kernel(tc, query, keys_words, keys_scales, po
                 k_scales[32 * quad : 32 * quad + 16, :].bitcast(I32),
                 keys_scales[0, 4 * quad : 4 * quad + 4, :].bitcast(I32).rearrange("r (k n) -> k r n", k=4),
             )
-        nc.sync.dma_start(k_codes[:].bitcast(I32), key_words)
+        nc.sync.dma_start(k_codes[0][:].bitcast(I32), key_words[:, 0:KEY_HALF])
         nc.sync.dma_start(offsets[:], offs)
+        nc.sync.dma_start(k_codes[1][:].bitcast(I32), key_words[:, KEY_HALF:T])
         nc.sync.dma_start(slope_col[:], slope)
 
         v_raw = []
@@ -74,8 +75,6 @@ def tile_attend_ownlists_positions_kernel(tc, query, keys_words, keys_scales, po
             raw = sb.tile([P, PACK, E], F32, name="v_raw%d" % g, tag="v_raw%d" % g, align_bytes=64)
             nc.sync.dma_start(raw[:], vals[g * K_PASS : (g + 1) * K_PASS, :].rearrange("(p j) e -> p j e", j=PACK))
             v_raw.append(raw)
-            if g == 0:
-                nc.sync.dma_start(fac_rows[:], fac[0].rearrange("(g p j) -> p g j", g=PASSES, j=PACK))
 
         pos_by_row = pos_all[:].rearrange("p (n c) -> p n c", c=T // P)
         for h in range(2):
@@ -84,7 +83,7 @@ def tile_attend_ownlists_positions_kernel(tc, query, keys_words, keys_scales, po
                 nc.tensor.transpose(spread[:, c, :], pos_rows[:, 4 * h + c : 4 * h + c + 1].to_broadcast([P, P]), ident[:])
             nc.scalar.activation(pos_by_row[:, :, 4 * h : 4 * h + 4], spread[:].rearrange("p c n -> p n c"), ACT.Copy)
 
-        q_bf = sb.tile([P, Q, PACK], BF16, name="q_bf", align_bytes=64)
+        q_bf = sb.tile([P, Q, PACK], BF16, name="q_bf", tag="q_bf", align_bytes=64)
         query_halves = (slice(0, Q // 2), slice(Q // 2, Q))
         for rows in query_halves:
             nc.vector.tensor_copy(
@@ -96,6 +95,8 @@ def tile_attend_ownlists_positions_kernel(tc, query, keys_words, keys_scales, po
             nc.vector.quantize_mx(
                 q_codes[:, rows].bitcast(FP8X4), q_scales[:, rows], q_bf[:, rows].rearrange("p q j -> p (q j)")
             )
+        fac_rows = sb.tile([P, PASSES, PACK], F32, name="fac_rows", tag="q_bf", align_bytes=64)
+        nc.gpsimd.dma_start(fac_rows[:], fac[0].rearrange("(g p j) -> p g j", g=PASSES, j=PACK))
         qpos_wide = sb.tile([P, SLOT_HALF], F32, name="qpos_wide")
         nc.vector.tensor_copy(qpos_wide[:], qpos_col[:].to_broadcast([P, SLOT_HALF]))
 
@@ -106,10 +107,10 @@ def tile_attend_ownlists_positions_kernel(tc, query, keys_words, keys_scales, po
         banks = []
         for n, (first, last) in enumerate(SCORE_RUNS):
             bank = ps.tile([P, last - first], F32, name="score_bank%d" % n, tag=("main0", "main1", "main2", "main3", "acc2")[n])
-            plane = first // KEY_RUN
+            plane, half = first // KEY_RUN, first // KEY_HALF
             nc.tensor.matmul_mx(
                 bank[:], lhsT=q_codes[:].bitcast(FP8X4), lhsT_scale=q_scales[:],
-                rhs=k_codes[:, first:last].bitcast(FP8X4),
+                rhs=k_codes[half][:, first - half * KEY_HALF : last - half * KEY_HALF].bitcast(FP8X4),
                 rhs_scale=k_scales[4 * plane : P, first - plane * KEY_RUN : last - plane * KEY_RUN], start=True, stop=True,
             )
             banks.append(bank)

@@ -20,14 +20,14 @@ P = 128
 PACK = 4
 K_PASS = P * PACK
 PASSES = T // K_PASS
-HALF = E // 2
 KEY_RUN = T // 4
 KEY_HALF = T // 2
-STRIP = HALF // 2
+STRIP = E // 4
 SLOT_HALF = I // 2
 SCORE_RUNS = ((0, 256), (256, 512), (512, 768), (768, 896), (896, 1024))
-LAST_PLANE = ((1, slice(0, 88)), (1, slice(88, 128)))
-PLANE_PIECES = (((0, slice(0, 40)), (0, slice(40, 128))) + LAST_PLANE, ((0, slice(0, 128)),) + LAST_PLANE)
+SHORT = 40
+LAST_PLANE = ((1, slice(0, P - SHORT)), (1, slice(P - SHORT, P)))
+PLANE_PIECES = (((0, slice(0, SHORT)), (0, slice(SHORT, P))) + LAST_PLANE, ((0, slice(0, P)),) + LAST_PLANE)
 UNLISTED = -(2.0**127)
 
 
@@ -40,13 +40,13 @@ def tile_attend_ownlists_positions_kernel(tc, query, keys_words, keys_scales, po
         offsets = sb.tile([P, I // 16], U16, name="offsets")
         pos_all = sb.tile([P, T], F32, name="pos_all")
         q_raw = sb.tile([P, PACK, Q], F32, name="q_raw")
-        k_codes = [sb.tile([P, KEY_HALF], U32, name="k_codes%d" % n, align_bytes=64) for n in range(2)]
+        k_codes = [sb.tile([P, KEY_HALF], U32, name="k_codes%d" % n, tag="k_codes%d" % n, align_bytes=64) for n in range(2)]
         k_scales = sb.tile([P, KEY_RUN], U8, name="k_scales", align_bytes=64)
         qpos_col = sb.tile([P, 1], F32, name="qpos_col")
         slope_col = sb.tile([P, 1], F32, name="slope_col")
         placed = sb.tile([P, T], F32, name="placed", tag="placed", align_bytes=64)
         ident = sb.tile([P, P], F32, name="ident")
-        pos_rows = sb.tile([P, T // P], F32, name="pos_rows", tag="pos_rows", align_bytes=64)
+        pos_rows = sb.tile([P, T // P], F32, name="pos_rows", align_bytes=64)
 
         nc.vector.memset(k_scales[:].bitcast(I32), 0)
         zeros = sb.tile([P, P], F32, name="zeros", tag="zeros", align_bytes=64)
@@ -60,13 +60,18 @@ def tile_attend_ownlists_positions_kernel(tc, query, keys_words, keys_scales, po
         nc.sync.dma_start(pos_rows[:], pos[0].rearrange("(n c) -> n c", c=T // P))
         nc.sync.dma_start(qpos_col[:], qpos)
         nc.sync.dma_start(q_raw[:], query.rearrange("(p j) q -> p j q", j=PACK))
-        for quad in range(4):
+        nc.sync.dma_start(offsets[:], offs)
+
+        def load_scales(quad):
             nc.sync.dma_start(
                 k_scales[32 * quad : 32 * quad + 16, :].bitcast(I32),
                 keys_scales[0, 4 * quad : 4 * quad + 4, :].bitcast(I32).rearrange("r (k n) -> k r n", k=4),
             )
+
+        for quad in range(3):
+            load_scales(quad)
         nc.sync.dma_start(k_codes[0][:].bitcast(I32), key_words[:, 0:KEY_HALF])
-        nc.sync.dma_start(offsets[:], offs)
+        load_scales(3)
         nc.sync.dma_start(k_codes[1][:].bitcast(I32), key_words[:, KEY_HALF:T])
         nc.sync.dma_start(slope_col[:], slope)
 
@@ -76,12 +81,15 @@ def tile_attend_ownlists_positions_kernel(tc, query, keys_words, keys_scales, po
             nc.sync.dma_start(raw[:], vals[g * K_PASS : (g + 1) * K_PASS, :].rearrange("(p j) e -> p j e", j=PACK))
             v_raw.append(raw)
 
-        pos_by_row = pos_all[:].rearrange("p (n c) -> p n c", c=T // P)
+        pos_banks = []
         for h in range(2):
             spread = ps.tile([P, 4, P], F32, name="pos_bank%d" % h, tag="side%d" % h)
             for c in range(4):
                 nc.tensor.transpose(spread[:, c, :], pos_rows[:, 4 * h + c : 4 * h + c + 1].to_broadcast([P, P]), ident[:])
-            nc.scalar.activation(pos_by_row[:, :, 4 * h : 4 * h + 4], spread[:].rearrange("p c n -> p n c"), ACT.Copy)
+            pos_banks.append(spread[:].rearrange("p c n -> p n c"))
+        pos_by_row = pos_all[:].rearrange("p (n c) -> p n c", c=T // P)
+        for h in range(2):
+            nc.scalar.activation(pos_by_row[:, :, 4 * h : 4 * h + 4], pos_banks[h], ACT.Copy)
 
         q_bf = sb.tile([P, Q, PACK], BF16, name="q_bf", tag="q_bf", align_bytes=64)
         query_halves = (slice(0, Q // 2), slice(Q // 2, Q))
@@ -100,35 +108,27 @@ def tile_attend_ownlists_positions_kernel(tc, query, keys_words, keys_scales, po
         qpos_wide = sb.tile([P, SLOT_HALF], F32, name="qpos_wide")
         nc.vector.tensor_copy(qpos_wide[:], qpos_col[:].to_broadcast([P, SLOT_HALF]))
 
-        first_slots, second_slots = slice(0, SLOT_HALF), slice(SLOT_HALF, I)
-        first_offsets, second_offsets = offsets[:, 0 : SLOT_HALF // 16], offsets[:, SLOT_HALF // 16 : I // 16]
+        def listed(window, first, last):
+            return window[:].indirect(offsets[:, first // 16 : last // 16])
 
-        scores = sb.tile([P, T], F32, name="scores")
-        banks = []
+        scores = sb.tile([P, T], F32, name="scores", tag="scores", align_bytes=64)
         for n, (first, last) in enumerate(SCORE_RUNS):
             bank = ps.tile([P, last - first], F32, name="score_bank%d" % n, tag=("main0", "main1", "main2", "main3", "acc2")[n])
-            plane, half = first // KEY_RUN, first // KEY_HALF
+            run, half = first // KEY_RUN, first // KEY_HALF
             nc.tensor.matmul_mx(
                 bank[:], lhsT=q_codes[:].bitcast(FP8X4), lhsT_scale=q_scales[:],
                 rhs=k_codes[half][:, first - half * KEY_HALF : last - half * KEY_HALF].bitcast(FP8X4),
-                rhs_scale=k_scales[4 * plane : P, first - plane * KEY_RUN : last - plane * KEY_RUN], start=True, stop=True,
+                rhs_scale=k_scales[4 * run : P, first - run * KEY_RUN : last - run * KEY_RUN], start=True, stop=True,
             )
-            banks.append(bank)
+            nc.scalar.copy(scores[:, first:last], bank[:])
 
-        def empty_bank(copy, n):
-            copy(scores[:, SCORE_RUNS[n][0] : SCORE_RUNS[n][1]], banks[n][:])
-
+        halves = ((0, SLOT_HALF), (SLOT_HALF, I))
         dist = sb.tile([P, I], F32, name="dist")
-        penalty = sb.tile([P, SLOT_HALF], F32, name="penalty", tag="penalty", align_bytes=64)
-        penalty_second = sb.tile([P, SLOT_HALF], F32, name="penalty_second", tag="penalty_second", align_bytes=64)
-        nc.vector.tensor_tensor(dist[:, first_slots], pos_all[:].indirect(first_offsets), qpos_wide[:], ALU.subtract)
-        nc.vector.tensor_tensor(dist[:, second_slots], pos_all[:].indirect(second_offsets), qpos_wide[:], ALU.subtract)
-        nc.vector.scalar_tensor_tensor(penalty[:], dist[:, first_slots], slope_col[:], dist[:, first_slots], ALU.mult, ALU.mult)
-        nc.vector.scalar_tensor_tensor(
-            penalty_second[:], dist[:, second_slots], slope_col[:], dist[:, second_slots], ALU.mult, ALU.mult
-        )
-        for n in range(len(SCORE_RUNS)):
-            empty_bank(nc.scalar.copy, n)
+        penalty = [sb.tile([P, SLOT_HALF], F32, name="penalty%d" % n, tag="penalty%d" % n, align_bytes=64) for n in range(2)]
+        for first, last in halves:
+            nc.vector.tensor_tensor(dist[:, first:last], listed(pos_all, first, last), qpos_wide[:], ALU.subtract)
+        for n, (first, last) in enumerate(halves):
+            nc.vector.scalar_tensor_tensor(penalty[n][:], dist[:, first:last], slope_col[:], dist[:, first:last], ALU.mult, ALU.mult)
 
         fac_bank = []
         for g in range(PASSES):
@@ -137,12 +137,16 @@ def tile_attend_ownlists_positions_kernel(tc, query, keys_words, keys_scales, po
                 nc.tensor.transpose(spread[:, j, :], fac_rows[:, g, j : j + 1].to_broadcast([P, P]), ident[:])
             fac_bank.append(spread)
 
-        logits = sb.tile([P, I], F32, name="logits", tag="late", align_bytes=64)
-        nc.vector.tensor_tensor(logits[:, first_slots], scores[:].indirect(first_offsets), penalty[:], ALU.subtract)
-
+        logits = sb.tile([P, I], F32, name="logits", align_bytes=64)
+        nc.vector.tensor_tensor(logits[:, 0:SLOT_HALF], listed(scores, 0, SLOT_HALF), penalty[0][:], ALU.subtract)
         scores_second = sb.tile([P, SLOT_HALF], F32, name="scores_second", tag="scores_second", align_bytes=64)
-        nc.scalar.activation(scores_second[:], scores[:].indirect(second_offsets), ACT.Copy)
-        nc.gpsimd.tensor_tensor(logits[:, second_slots], scores_second[:], penalty_second[:], ALU.subtract)
+        nc.scalar.activation(scores_second[:], listed(scores, SLOT_HALF, I), ACT.Copy)
+        nc.gpsimd.tensor_tensor(logits[:, SLOT_HALF:I], scores_second[:], penalty[1][:], ALU.subtract)
+
+        neg_max = sb.tile([P, 1], F32, name="neg_max")
+        nc.vector.tensor_copy(listed(placed, 0, SLOT_HALF), logits[:, 0:SLOT_HALF])
+        nc.vector.tensor_reduce(neg_max[:], logits[:], AXIS.X, ALU.max, negate=True)
+        nc.vector.tensor_copy(listed(placed, SLOT_HALF, I), logits[:, SLOT_HALF:I])
 
         v_codes, v_scales = {}, {}
 
@@ -155,35 +159,32 @@ def tile_attend_ownlists_positions_kernel(tc, query, keys_words, keys_scales, po
                 v_codes[key] = codes[:, n * STRIP : (n + 1) * STRIP]
                 v_scales[key] = scales[:, n * STRIP : (n + 1) * STRIP]
 
+        def raw_strips(g, first, last):
+            return v_raw[g][:, :, first * STRIP : last * STRIP]
+
         def cast_on_scalar(staged, raw):
             nc.scalar.copy(staged.rearrange("p (c i) j -> p c j i", i=4), raw.rearrange("p j (c i) -> p c j i", i=4))
 
         def cast_on_gpsimd(staged, raw):
             nc.gpsimd.tensor_scalar(staged, raw.rearrange("p j e -> p e j"), 1.0, 0.0, ALU.mult, ALU.add)
 
-        neg_max = sb.tile([P, 1], F32, name="neg_max")
-        nc.vector.tensor_copy(placed[:].indirect(first_offsets), logits[:, first_slots])
-        nc.vector.tensor_reduce(neg_max[:], logits[:], AXIS.X, ALU.max, negate=True)
-        nc.vector.tensor_copy(placed[:].indirect(second_offsets), logits[:, second_slots])
-
-        v_first = sb.tile([P, HALF, PACK], BF16, name="v_first", tag="penalty", align_bytes=64)
-        cast_on_scalar(v_first[:], v_raw[0][:, :, 0:HALF])
+        v_first = sb.tile([P, 2 * STRIP, PACK], BF16, name="v_first", tag="penalty0", align_bytes=64)
+        cast_on_scalar(v_first[:], raw_strips(0, 0, 2))
         v_mid = sb.tile([P, E, PACK], BF16, name="v_mid", tag="scores_second", align_bytes=64)
-        cast_on_scalar(v_mid[:, 0:STRIP], v_raw[0][:, :, HALF : HALF + STRIP])
-        cast_on_gpsimd(v_mid[:, STRIP:HALF], v_raw[0][:, :, HALF + STRIP : E])
-        cast_on_gpsimd(v_mid[:, HALF:E], v_raw[1][:, :, 0:HALF])
-        v_third = sb.tile([P, STRIP, PACK], BF16, name="v_third", tag="penalty_second", align_bytes=64)
-        cast_on_scalar(v_third[:], v_raw[1][:, :, HALF : HALF + STRIP])
+        cast_on_scalar(v_mid[:, 0:STRIP], raw_strips(0, 2, 3))
+        cast_on_gpsimd(v_mid[:, STRIP : 2 * STRIP], raw_strips(0, 3, 4))
+        cast_on_gpsimd(v_mid[:, 2 * STRIP : E], raw_strips(1, 0, 2))
+        v_third = sb.tile([P, STRIP, PACK], BF16, name="v_third", tag="penalty1", align_bytes=64)
+        cast_on_scalar(v_third[:], raw_strips(1, 2, 3))
 
         total = sb.tile([P, 1], F32, name="total")
         probs_listed = sb.tile([P, I], F32, name="probs_listed", tag="v_raw0", align_bytes=64)
         nc.scalar.activation(probs_listed[:], logits[:], ACT.Exp, bias=neg_max[:], scale=1.0, accum_out=total[:])
         inv_total = sb.tile([P, 1], F32, name="inv_total")
-
         nc.vector.reciprocal(inv_total[:], total[:])
         quantise_values(v_first[:], ((0, 0), (0, 1)), "v_raw0")
-        v_last = sb.tile([P, STRIP, PACK], BF16, name="v_last", tag="penalty", align_bytes=64)
-        cast_on_gpsimd(v_last[:], v_raw[1][:, :, HALF + STRIP : E])
+        v_last = sb.tile([P, STRIP, PACK], BF16, name="v_last", tag="penalty0", align_bytes=64)
+        cast_on_gpsimd(v_last[:], raw_strips(1, 3, 4))
 
         probs = sb.tile([P, PASSES, 2, P, 2], F32, name="probs", align_bytes=64)
         w_bf = sb.tile([P, PASSES, 2, P, 2], BF16, name="w_bf", tag="w_bf", align_bytes=64)
@@ -201,7 +202,7 @@ def tile_attend_ownlists_positions_kernel(tc, query, keys_words, keys_scales, po
                 )
             for u in range(2):
                 nc.tensor.transpose(turned[:, u, :], w_bf[:, g, u].rearrange("q p e -> q (p e)").bitcast(F32), ident[:])
-            grouped = sb.tile([P, Q * PACK], BF16, name="w_grouped%d" % g, align_bytes=64)
+            grouped = sb.tile([P, Q * PACK], BF16, name="w_grouped%d" % g, tag="w_grouped%d" % g, align_bytes=64)
             nc.scalar.copy(grouped[:].bitcast(F32).rearrange("p (q u) -> p q u", u=2), turned[:].rearrange("p u q -> p q u"))
             w_grouped.append(grouped)
 

from contextlib import ExitStack

import concourse.mybir as mybir

D, T, Q, I, E = 512, 1024, 128, 512, 512
FLOPS = 2 * Q * D * T + 2 * Q * T * E

F32 = mybir.dt.float32
BF16 = mybir.dt.bfloat16
I32 = mybir.dt.int32
U32 = mybir.dt.uint32
U16 = mybir.dt.uint16
U8 = mybir.dt.uint8
FP8X4 = mybir.dt.float8_e4m3fn_x4
ALU = mybir.AluOpType
ACT = mybir.ActivationFunctionType
AXIS = mybir.AxisListType

P = 128
PACK = 4
K_PASS = P * PACK
PASSES = T // K_PASS
KEY_RUN = T // 4
KEY_HALF = T // 2
STRIP = E // 4
SLOT_HALF = I // 2
SCORE_RUNS = ((0, 256), (256, 512), (512, 768), (768, 896), (896, 1024))
SHORT = 40
LAST_PLANE = ((1, slice(0, P - SHORT)), (1, slice(P - SHORT, P)))
PLANE_PIECES = (((0, slice(0, SHORT)), (0, slice(SHORT, P))) + LAST_PLANE, ((0, slice(0, P)),) + LAST_PLANE)
UNLISTED = -(2.0**127)


def tile_attend_ownlists_positions_kernel(tc, query, keys_words, keys_scales, pos, qpos, slope, fac, vals, offs, out):
    nc = tc.nc
    with ExitStack() as ctx:
        sb = ctx.enter_context(tc.tile_pool(name="sb", bufs=1))
        ps = ctx.enter_context(tc.psum_pool(name="ps", bufs=1))

        offsets = sb.tile([P, I // 16], U16, name="offsets")
        pos_all = sb.tile([P, T], F32, name="pos_all")
        q_raw = sb.tile([P, PACK, Q], F32, name="q_raw")
        k_codes = [sb.tile([P, KEY_HALF], U32, name="k_codes%d" % n, tag="k_codes%d" % n, align_bytes=64) for n in range(2)]
        k_scales = sb.tile([P, KEY_RUN], U8, name="k_scales", align_bytes=64)
        qpos_col = sb.tile([P, 1], F32, name="qpos_col")
        slope_col = sb.tile([P, 1], F32, name="slope_col")
        placed = sb.tile([P, T], F32, name="placed", tag="placed", align_bytes=64)
        ident = sb.tile([P, P], F32, name="ident")
        pos_rows = sb.tile([P, T // P], F32, name="pos_rows", align_bytes=64)

        nc.vector.memset(k_scales[:].bitcast(I32), 0)
        zeros = sb.tile([P, P], F32, name="zeros", tag="zeros", align_bytes=64)
        nc.gpsimd.memset(zeros[:], 0.0)
        nc.gpsimd.affine_select(
            out=ident[:], in_=zeros[:], compare_op=ALU.not_equal, fill=1.0, base=0, pattern=[[-1, P]], channel_multiplier=1
        )
        nc.vector.memset(placed[:], UNLISTED)

        key_words = keys_words[0].rearrange("p n t -> p (n t)").bitcast(I32)
        nc.sync.dma_start(pos_rows[:], pos[0].rearrange("(n c) -> n c", c=T // P))
        nc.sync.dma_start(qpos_col[:], qpos)
        nc.sync.dma_start(q_raw[:], query.rearrange("(p j) q -> p j q", j=PACK))
        nc.sync.dma_start(offsets[:], offs)

        def load_scales(quad):
            nc.sync.dma_start(
                k_scales[32 * quad : 32 * quad + 16, :].bitcast(I32),
                keys_scales[0, 4 * quad : 4 * quad + 4, :].bitcast(I32).rearrange("r (k n) -> k r n", k=4),
            )

        for quad in range(3):
            load_scales(quad)
        nc.sync.dma_start(k_codes[0][:].bitcast(I32), key_words[:, 0:KEY_HALF])
        load_scales(3)
        nc.sync.dma_start(k_codes[1][:].bitcast(I32), key_words[:, KEY_HALF:T])
        nc.sync.dma_start(slope_col[:], slope)

        v_raw = []
        for g in range(PASSES):
            raw = sb.tile([P, PACK, E], F32, name="v_raw%d" % g, tag="v_raw%d" % g, align_bytes=64)
            nc.sync.dma_start(raw[:], vals[g * K_PASS : (g + 1) * K_PASS, :].rearrange("(p j) e -> p j e", j=PACK))
            v_raw.append(raw)

        pos_banks = []
        for h in range(2):
            spread = ps.tile([P, 4, P], F32, name="pos_bank%d" % h, tag="side%d" % h)
            for c in range(4):
                nc.tensor.transpose(spread[:, c, :], pos_rows[:, 4 * h + c : 4 * h + c + 1].to_broadcast([P, P]), ident[:])
            pos_banks.append(spread[:].rearrange("p c n -> p n c"))
        pos_by_row = pos_all[:].rearrange("p (n c) -> p n c", c=T // P)
        for h in range(2):
            nc.scalar.activation(pos_by_row[:, :, 4 * h : 4 * h + 4], pos_banks[h], ACT.Copy)

        q_bf = sb.tile([P, Q, PACK], BF16, name="q_bf", tag="q_bf", align_bytes=64)
        query_halves = (slice(0, Q // 2), slice(Q // 2, Q))
        for rows in query_halves:
            nc.vector.tensor_copy(
                q_bf[:, rows].rearrange("p (c i) j -> p c j i", i=4), q_raw[:, :, rows].rearrange("p j (c i) -> p c j i", i=4)
            )
        q_codes = sb.tile([P, Q], U32, name="q_codes", align_bytes=64)
        q_scales = sb.tile([P, Q], U8, name="q_scales", tag="zeros", align_bytes=64)
        for rows in query_halves:
            nc.vector.quantize_mx(
                q_codes[:, rows].bitcast(FP8X4), q_scales[:, rows], q_bf[:, rows].rearrange("p q j -> p (q j)")
            )
        fac_rows = sb.tile([P, PASSES, PACK], F32, name="fac_rows", tag="q_bf", align_bytes=64)
        nc.gpsimd.dma_start(fac_rows[:], fac[0].rearrange("(g p j) -> p g j", g=PASSES, j=PACK))
        qpos_wide = sb.tile([P, SLOT_HALF], F32, name="qpos_wide")
        nc.vector.tensor_copy(qpos_wide[:], qpos_col[:].to_broadcast([P, SLOT_HALF]))

        def listed(window, first, last):
            return window[:].indirect(offsets[:, first // 16 : last // 16])

        scores = sb.tile([P, T], F32, name="scores", tag="scores", align_bytes=64)
        for n, (first, last) in enumerate(SCORE_RUNS):
            bank = ps.tile([P, last - first], F32, name="score_bank%d" % n, tag=("main0", "main1", "main2", "main3", "acc2")[n])
            run, half = first // KEY_RUN, first // KEY_HALF
            nc.tensor.matmul_mx(
                bank[:], lhsT=q_codes[:].bitcast(FP8X4), lhsT_scale=q_scales[:],
                rhs=k_codes[half][:, first - half * KEY_HALF : last - half * KEY_HALF].bitcast(FP8X4),
                rhs_scale=k_scales[4 * run : P, first - run * KEY_RUN : last - run * KEY_RUN], start=True, stop=True,
            )
            nc.scalar.copy(scores[:, first:last], bank[:])

        halves = ((0, SLOT_HALF), (SLOT_HALF, I))
        dist = sb.tile([P, I], F32, name="dist")
        penalty = [sb.tile([P, SLOT_HALF], F32, name="penalty%d" % n, tag="penalty%d" % n, align_bytes=64) for n in range(2)]
        for first, last in halves:
            nc.vector.tensor_tensor(dist[:, first:last], listed(pos_all, first, last), qpos_wide[:], ALU.subtract)
        for n, (first, last) in enumerate(halves):
            nc.vector.scalar_tensor_tensor(penalty[n][:], dist[:, first:last], slope_col[:], dist[:, first:last], ALU.mult, ALU.mult)

        fac_bank = []
        for g in range(PASSES):
            spread = ps.tile([P, PACK, P], F32, name="fac_bank%d" % g, tag="main%d" % (2 + g))
            for j in range(PACK):
                nc.tensor.transpose(spread[:, j, :], fac_rows[:, g, j : j + 1].to_broadcast([P, P]), ident[:])
            fac_bank.append(spread)

        logits = sb.tile([P, I], F32, name="logits", align_bytes=64)
        nc.vector.tensor_tensor(logits[:, 0:SLOT_HALF], listed(scores, 0, SLOT_HALF), penalty[0][:], ALU.subtract)
        scores_second = sb.tile([P, SLOT_HALF], F32, name="scores_second", tag="scores_second", align_bytes=64)
        nc.scalar.activation(scores_second[:], listed(scores, SLOT_HALF, I), ACT.Copy)
        nc.gpsimd.tensor_tensor(logits[:, SLOT_HALF:I], scores_second[:], penalty[1][:], ALU.subtract)

        neg_max = sb.tile([P, 1], F32, name="neg_max")
        nc.vector.tensor_copy(listed(placed, 0, SLOT_HALF), logits[:, 0:SLOT_HALF])
        nc.vector.tensor_reduce(neg_max[:], logits[:], AXIS.X, ALU.max, negate=True)
        nc.vector.tensor_copy(listed(placed, SLOT_HALF, I), logits[:, SLOT_HALF:I])

        v_codes, v_scales = {}, {}

        def quantise_values(staged, strips, tag):
            width = len(strips) * STRIP
            codes = sb.tile([P, width], U32, name="v_codes%d_%d" % strips[0], tag=tag, align_bytes=64)
            scales = sb.tile([P, width], U8, name="v_scales%d_%d" % strips[0], align_bytes=64)
            nc.vector.quantize_mx(codes[:].bitcast(FP8X4), scales[:], staged.rearrange("p e j -> p (e j)"))
            for n, key in enumerate(strips):
                v_codes[key] = codes[:, n * STRIP : (n + 1) * STRIP]
                v_scales[key] = scales[:, n * STRIP : (n + 1) * STRIP]

        def raw_strips(g, first, last):
            return v_raw[g][:, :, first * STRIP : last * STRIP]

        def cast_on_scalar(staged, raw):
            nc.scalar.copy(staged.rearrange("p (c i) j -> p c j i", i=4), raw.rearrange("p j (c i) -> p c j i", i=4))

        def cast_on_gpsimd(staged, raw):
            nc.gpsimd.tensor_scalar(staged, raw.rearrange("p j e -> p e j"), 1.0, 0.0, ALU.mult, ALU.add)

        v_first = sb.tile([P, 2 * STRIP, PACK], BF16, name="v_first", tag="penalty0", align_bytes=64)
        cast_on_scalar(v_first[:], raw_strips(0, 0, 2))
        v_mid = sb.tile([P, E, PACK], BF16, name="v_mid", tag="scores_second", align_bytes=64)
        cast_on_scalar(v_mid[:, 0:STRIP], raw_strips(0, 2, 3))
        cast_on_gpsimd(v_mid[:, STRIP : 2 * STRIP], raw_strips(0, 3, 4))
        cast_on_gpsimd(v_mid[:, 2 * STRIP : E], raw_strips(1, 0, 2))
        v_third = sb.tile([P, STRIP, PACK], BF16, name="v_third", tag="penalty1", align_bytes=64)
        cast_on_scalar(v_third[:], raw_strips(1, 2, 3))

        total = sb.tile([P, 1], F32, name="total")
        probs_listed = sb.tile([P, I], F32, name="probs_listed", tag="v_raw0", align_bytes=64)
        nc.scalar.activation(probs_listed[:], logits[:], ACT.Exp, bias=neg_max[:], scale=1.0, accum_out=total[:])
        inv_total = sb.tile([P, 1], F32, name="inv_total")
        nc.vector.reciprocal(inv_total[:], total[:])
        quantise_values(v_first[:], ((0, 0), (0, 1)), "v_raw0")
        v_last = sb.tile([P, STRIP, PACK], BF16, name="v_last", tag="penalty0", align_bytes=64)
        cast_on_gpsimd(v_last[:], raw_strips(1, 3, 4))

        probs = sb.tile([P, PASSES, 2, P, 2], F32, name="probs", align_bytes=64)
        w_bf = sb.tile([P, PASSES, 2, P, 2], BF16, name="w_bf", tag="w_bf", align_bytes=64)
        for g in range(PASSES):
            placed_pairs = placed[:, g * K_PASS : (g + 1) * K_PASS].rearrange("q (p u e) -> q u p e", u=2, e=2)
            for u, rows in PLANE_PIECES[g]:
                nc.scalar.activation(probs[:, g, u, rows], placed_pairs[:, u, rows], ACT.Exp, bias=neg_max[:], scale=1.0)
        w_grouped = []
        for g in range(PASSES):
            turned = ps.tile([P, 2, Q], F32, name="turned%d" % g, tag="side%d" % g)
            fac_pairs = fac_bank[g][:].rearrange("q (u e) p -> q u p e", e=2)
            for u, rows in PLANE_PIECES[g]:
                nc.vector.scalar_tensor_tensor(
                    w_bf[:, g, u, rows], probs[:, g, u, rows], inv_total[:], fac_pairs[:, u, rows], ALU.mult, ALU.mult
                )
            for u in range(2):
                nc.tensor.transpose(turned[:, u, :], w_bf[:, g, u].rearrange("q p e -> q (p e)").bitcast(F32), ident[:])
            grouped = sb.tile([P, Q * PACK], BF16, name="w_grouped%d" % g, tag="w_grouped%d" % g, align_bytes=64)
            nc.scalar.copy(grouped[:].bitcast(F32).rearrange("p (q u) -> p q u", u=2), turned[:].rearrange("p u q -> p q u"))
            w_grouped.append(grouped)

        acc = [ps.tile([Q, STRIP], F32, name="acc%d" % s, tag=("main0", "main1", "acc2", "acc3")[s]) for s in range(4)]
        for g in range(PASSES):
            if g == 0:
                quantise_values(v_mid[:], ((0, 2), (0, 3), (1, 0), (1, 1)), "placed")
            else:
                quantise_values(v_third[:], ((1, 2),), "w_bf")
                quantise_values(v_last[:], ((1, 3),), "w_grouped0")
            w_codes = sb.tile([P, Q], U32, name="w_codes%d" % g, align_bytes=64)
            w_scales = sb.tile([P, Q], U8, name="w_scales%d" % g, align_bytes=64)
            nc.vector.quantize_mx(w_codes[:].bitcast(FP8X4), w_scales[:], w_grouped[g][:])
            for s in range(4):
                nc.tensor.matmul_mx(
                    acc[s][:], lhsT=w_codes[:].bitcast(FP8X4), lhsT_scale=w_scales[:],
                    rhs=v_codes[g, s].bitcast(FP8X4), rhs_scale=v_scales[g, s],
                    start=(g == 0), stop=(g == PASSES - 1),
                )

        results = []
        for s in range(4):
            result = sb.tile([Q, STRIP], F32, name="result%d" % s)
            (nc.scalar.copy if s < 2 else nc.vector.tensor_copy)(result[:], acc[s][:])
            results.append(result)
        for s in range(4):
            (nc.scalar if s in (1, 2) else nc.sync).dma_start(out[:, s * STRIP : (s + 1) * STRIP], results[s][:])
